import numpy as np, ml_dtypes
CORES = [5,29,101,125,133,157,229,253]
N = 8
import mx_ref
BF = ml_dtypes.bfloat16
def gentries(a):
    return np.ascontiguousarray(a.reshape(8, 16, -1).transpose(0, 2, 1)).reshape(8, -1)
def gtable(e):
    e = np.asarray(e); return np.ascontiguousarray(e.reshape(8, -1, 16).transpose(0, 2, 1)).reshape(128, -1).astype(np.int32)
def gcols(t, e):
    v = np.concatenate([t.reshape(8, 16, -1, 4), np.zeros((8, 16, 1, 4), BF)], axis=2)
    return np.ascontiguousarray(np.stack([v[g][:, e[g]] for g in range(8)])).reshape(128, -1)
def tile(rs):
    return np.stack(rs, axis=2).reshape(128, -1).astype(BF)
def pick(q, e):
    c = np.concatenate([q[0].reshape(128, -1, 4), np.zeros((128, 1, 4), np.uint8)], axis=1); s = np.concatenate([q[1], np.ones((16, 1), np.uint8)], axis=1)
    return (np.ascontiguousarray(c[:, e].reshape(128, -1)), np.ascontiguousarray(s[:, e]))
def join(*qs):
    return (np.concatenate([q[0] for q in qs], axis=1), np.concatenate([q[1] for q in qs], axis=1))
def put(q, e, v):
    c, s = q[0].reshape(128, -1, 4).copy(), q[1].copy(); c[:, e] = v[0].reshape(128, -1, 4); s[:, e] = v[1]
    return (c.reshape(128, -1), s)
def pk(c, s):
    return (np.ascontiguousarray(c), mx_ref.live(s))
def emit(q):
    return q[0], q[1]
def packed(v, rng):
    q = [mx_ref.quantize(np.ascontiguousarray(v[r])) for r in range(N)]
    return np.stack([a for a, b in q]), np.stack([mx_ref.plane(b, rng) for a, b in q])
def values_of_codes():
    e, c = np.zeros((128, 128, 4), np.float32), np.zeros((128, 2, 4), np.uint8)
    e[np.arange(128), np.arange(128), 0] = 1
    c[:127, :, 0] = np.arange(256).reshape(2, 128).T[:127]
    return mx_ref.matmul(mx_ref.quantize(e.reshape(128, 512).astype(BF)), (c.reshape(128, 8), np.full((16, 2), 127, np.uint8))).T.reshape(-1).astype(np.float64)
CODE_VALUE, SCALE_VALUE = values_of_codes(), 2.0 ** (np.arange(256) - 127.0)
def decode(q):
    return (CODE_VALUE[q[0]].reshape(16, 8, -1, 4) * SCALE_VALUE[q[1]][:, None, :, None] + 0.0).reshape(128, -1).astype(np.float32)
def f(rng, *shape):
    return mx_ref.flush((rng.standard_normal(shape, dtype=np.float32) * np.exp2(rng.integers(-2, 3, shape[:-1] + (1,)))).astype(BF))
def wide(rng, *shape, cols=0):
    v = rng.standard_normal(shape, dtype=np.float32) * np.exp2(rng.integers(-12, 13, shape)).astype(np.float32)
    if cols: v *= np.repeat(np.exp2(rng.integers(-cols, cols + 1, shape[:-2] + (1, shape[-1] // 4))) * (rng.random(shape[:-2] + (1, shape[-1] // 4)) > 0.0625), 4, axis=-1).astype(np.float32)
    return mx_ref.flush(v.astype(BF))
C, M, R = 320, 160, 3
SH = (N, 8, 2, C, 4)
def numbers_of(rng):
    return {"x": np.array(f(rng, N, 128, 4 * C)), "u": np.array(f(rng, N, 128, 512)), "v": np.array(f(rng, N, 128, 512))}
def lists_of(e, c, a):
    return {"al": np.stack([gtable(e[r]) for r in range(N)]), "nx": np.stack([gtable((512 * c + a)[r].reshape(8, 8 * C)) for r in range(N)])}
def lists(rng):
    return lists_of(rng.integers(0, C, (N, 8, C)), rng.integers(0, 5, SH), rng.integers(0, C, SH))
def layers(rng, still=0):
    w = np.array(f(rng, N, 128, 2048)).reshape(N, 8, 16, 4, 8, 16, 4)
    w[:, :, :still] = 0
    w[:, :, :, :, :, :still] = 0
    return w
def weights(rng, w):
    c, s = packed(np.ascontiguousarray(w).reshape(N, 128, 2048), rng)
    return {"wc": c, "ws": s}
def setup_inputs(rng):
    return {**numbers_of(rng), **lists(rng), **weights(rng, layers(rng))}
def setup_inputs_near(rng):
    d = numbers_of(rng)
    x = d["x"].reshape(N, 8, 16, C, 4)
    u = d["u"].reshape(N, 128, 128, 4)
    o = rng.permutation(N) % 2
    x[:, :, :8] = 0
    u[:, :, ::16] = 0
    u[:, :, 1::16] = 0
    for r in range(N):
        k = 2.0 ** -30 if o[r] == 0 else 1.0
        s = rng.integers(-1, 2, (8, 2, C)) * k
        for g in rng.permutation(8)[:4]: s[g, :, rng.integers(C)] = 2.0 ** 14 * rng.choice([-1.0, 1.0], 2)
        x[r, :, :2, :, 0] = s.astype(np.float32).astype(BF)
        t = np.where(s[:, 0] == 0, rng.integers(-1, 2, (8, C)), 0) * k
        x[r, :, 2, :, 0] = (1.125 * t).astype(np.float32).astype(BF)
        x[r, :, 3, :, 0] = (-t).astype(np.float32).astype(BF)
        for h in [0, 16, 32, 48, 64, 80, 96, 112, 1, 17]:
            u[r, h, h, 0] = k
            u[r, h - h % 16 + 2, h, 0] = 1.125 * k
            u[r, h - h % 16 + 3, h, 0] = 1.25 * k
    return {"x": x.reshape(N, 128, 4 * C), "u": u.reshape(N, 128, 512), "v": d["v"], **lists(rng), **weights(rng, layers(rng, 8))}
def setup_inputs_chain(rng):
    d = numbers_of(rng)
    e = rng.permutation(N)
    c = rng.integers(0, 5, SH)
    i = np.arange(4)
    c[e[0]] = rng.integers(1, 5, SH[1:])
    c[e[1]] = 0
    c[e[2]] = np.where(np.arange(8)[:, None] <= 2 * i, i + 1, 0)[:, None, None, :]
    c[e[3]][:, 0] = 0
    c[e[3]][:, 1] = rng.integers(1, 5, (8, C, 4))
    return {**d, **lists_of(rng.integers(0, C, (N, 8, C)), c, rng.integers(0, C, SH)), **weights(rng, layers(rng))}
def setup_inputs_twice(rng):
    d = numbers_of(rng)
    s = 2.0 ** -rng.integers(8, 15, (N, 16, C, 32)) * (1.125 + 0.25 * rng.integers(0, 4, (N, 16, C, 32)))
    s[:, :, :, 4] = 2.0 ** -rng.integers(8, 12, (N, 16, C)) * (1.125 + 0.25 * rng.integers(0, 4, (N, 16, C)))
    np.put_along_axis(s, rng.integers(8, 32, (N, 16, C, 1)), 1.96875, axis=3)
    s = s * rng.choice([-1.0, 1.0], s.shape)
    s[:, :, :, 0] = 0.125 * s[:, :, :, 4]
    s = s * np.exp2(rng.integers(10, 13, (N, 16, C, 1)))
    x = np.ascontiguousarray(s.reshape(N, 16, C, 8, 4).transpose(0, 1, 3, 2, 4)).reshape(N, 128, 4 * C)
    u = d["u"].reshape(N, 128, 128, 4)
    u[:, :, ::16] = 0
    for h in range(0, 128, 16):
        u[:, h, h, 0] = 1.0
        u[:, h + 1, h, 0] = -0.125
    w = np.array(mx_ref.flush((layers(rng).astype(np.float32) * np.float32(2.0 ** -12)).astype(BF))).reshape(N, 128, 4, 128, 4)
    i = np.arange(128)
    for b in range(4): w[:, i, b, i, b] = -1.0
    return {"x": x.astype(np.float32).astype(BF), "u": u.reshape(N, 128, 512), "v": d["v"], **lists(rng), **weights(rng, w)}
def setup_inputs_ends(rng):
    d = numbers_of(rng)
    e = rng.permutation(N)
    x = d["x"].reshape(N, 8, 16, C, 4)
    u = d["u"].reshape(N, 128, 128, 4)
    v = d["v"].reshape(N, 128, 128, 4)
    t = np.clip(rng.integers(-C, 2 * C, (N, 8, C)), 0, C - 1)
    c = 4 * rng.integers(0, 2, SH)
    a = np.clip(rng.integers(-C, 2 * C, SH), 0, C - 1)
    t[e[0]], c[e[0]], a[e[0]] = C - 1, 4, C - 1
    t[e[1]], c[e[1]], a[e[1]] = 0, 0, 0
    u[:, :, ::16] = 0
    u[:, :, 1::16] = 0
    for i in range(N):
        r = e[i]
        s = rng.integers(-1, 2, (8, C)) * 1.0
        s[rng.permutation(8)[:2]] = rng.choice([-1.0, 1.0], (2, 1))
        s = s * (2.0 ** -30 if i % 2 else 2.0 ** 14)
        x[r, :, :8] = s[:, None, :, None].astype(np.float32).astype(BF)
        for h in [0, 16, 32, 48, 64, 80, 96, 112, 1, 17]: u[r, h - h % 16:h - h % 16 + 8, h] = 2.0 ** -30 if i % 2 else 2.0 ** 30
    x[e[0]] = (2.0 ** 14 * rng.choice([-1.0, 1.0], (C, 1))).astype(np.float32).astype(BF)
    u[e[0]] = (2.0 ** 30 * rng.choice([-1.0, 1.0], (128, 1))).astype(np.float32).astype(BF)
    v[e[0]] = (2.0 ** 30 * rng.choice([-1.0, 1.0], (128, 1))).astype(np.float32).astype(BF)
    w = layers(rng, 8)
    w[e[0]][:, 8:, :, :, 8:] = 8
    w[e[1]] = 0
    v = (np.where(v < 0, -1.0, 1.0) * np.where(rng.permutation(N) % 2, 2.0 ** -30, 2.0 ** 30)[:, None, None, None]).astype(np.float32).astype(BF)
    return {"x": x.reshape(N, 128, 4 * C), "u": u.reshape(N, 128, 512), "v": v.reshape(N, 128, 512), **lists_of(t, c, a), **weights(rng, w)}
def setup_inputs_spread(rng):
    d = setup_inputs(rng)
    d["x"] = mx_ref.flush((wide(rng, N, 128, 4 * C, cols=6).astype(np.float32) * np.float32(2.0 ** -7)).astype(BF))
    return d
def check_inputs(d):
    b = []
    for k, most in (("x", 2.0 ** 14), ("u", 2.0 ** 30), ("v", 2.0 ** 30)):
        a = np.abs(d[k].astype(np.float32))
        if not (np.isfinite(a).all() and ((a == 0) | (a >= 2.0 ** -30) & (a <= most)).all()): b.append("a value of " + k)
    if not ((d["al"] >= 0) & (d["al"] < C)).all(): b.append("an entry of al")
    if not ((d["nx"] >= 0) & (d["nx"] < 2560) & (d["nx"] % 512 < C)).all(): b.append("an entry of nx")
    none, least, most = [emit(mx_ref.quantize(np.full((128, 16), k, np.float32).astype(BF)))[1][0, 0] for k in (0.0, 2.0 ** -30, 2.0 ** 30)]
    for r in range(N):
        if ((d["wc"][r] == 0x7F) | (d["wc"][r] == 0xFF)).any(): b.append("wc: a code that is no number")
        s = mx_ref.live(d["ws"][r])
        if ((s != none) & ((s < least) | (s > most))).any(): b.append("ws: a scale out of range")
        w = np.abs(decode(pk(d["wc"][r], d["ws"][r])).astype(np.float64)).reshape(128, 512, 4)
        if not (np.sum(w, axis=(0, 2)) <= 2048).all(): b.append("a column of W adds up to more than 2048")
    return b
def reference(x, u, v, al, nx, wc, ws):
    qu = [mx_ref.quantize(u[r]) for r in range(N)]
    lay = [pk(wc[r], ws[r]) for r in range(N)]
    now = [x[r] for r in range(N)]
    ad = np.stack([gentries(al[r]) for r in range(N)])
    follow = [gentries(nx[r]) for r in range(N)]
    for t in range(R):
        made = []
        for r in range(N):
            q = mx_ref.quantize(now[r])
            s = mx_ref.matmul(qu[r], q)
            edge = 2 * (s[1] > 0) + (s[17] > 0)
            on = np.ones(C, bool)
            for g in range(8):
                bit = s[16 * g][ad[r, g]] > 0
                n = follow[r][g][4 * C * bit + 4 * ad[r, g] + edge]
                ad[r, g] = np.where(on, n % 512, ad[r, g])
                on = on & (n >= 512)
                edge = np.where(on, n // 512 - 1, 0)
            made.append(mx_ref.quantize(gcols(decode(q).astype(BF), ad[r])))
        ad[:, :, C - M:] = np.roll(ad[:, :, C - M:], 1, axis=0)
        for r in range(N):
            q = join(pick(made[r], np.arange(C - M)), pick(made[r - 1], np.arange(C - M, C)))
            own = decode(q)
            now[r] = tile([mx_ref.matmul(pick(lay[r], np.arange(128 * b, 128 * b + 128)), q) * np.float32(0.015625) + own[:, b::4] for b in range(4)])
    y, oa = np.zeros((N, 128, C), np.float32), np.zeros((N, 8, C), np.float32)
    oc, osc = np.zeros((N, 128, 4 * C), np.uint8), np.zeros((N, 16, C), np.uint8)
    for r in range(N):
        q = mx_ref.quantize(now[r])
        y[r] = mx_ref.matmul(mx_ref.quantize(v[r]), q)
        oa[r] = ad[r]
        oc[r], osc[r] = emit(q)
    return {"y": y, "oa": oa, "oc": oc, "osc": osc}

@@ -1,0 +1,462 @@
+import math
+from concourse.bass import DstId, RemoteDMATransfer
+from concourse.mybir import dt, AluOpType as A, AxisListType, ActivationFunctionType as AF
+
+N, C, H, R = 8, 320, 160, 3
+BF, F32, I32, U16, U8, MX = "bfloat16", "float32", "int32", "uint16", "uint8", "float8_e4m3fn_x4"
+MAGIC = 12582912.0
+BIG = 1.5 * 2.0 ** 32
+
+
+def _scratch():
+    s = {}
+
+    def sb(name, n, t):
+        s[name] = ("sbuf", [128, n], t)
+    for k in range(8):
+        s["pk%d" % k] = ("psum", [128, 512], F32)
+    sb("ub", 512, BF); sb("uq", 128, MX); sb("up", 128, U8); sb("uq2", 128, MX); sb("up2", 128, U8)
+    sb("vb", 512, BF); sb("vq", 128, MX); sb("vp", 128, U8)
+    sb("wq", 512, MX); sb("wp", 512, U8)
+    sb("one", 516, BF); sb("eb", 516, BF); sb("eb64", 516, BF)
+    sb("ec", 512, MX); sb("es", 512, U8); sb("e64c", 512, MX); sb("e64s", 512, U8)
+    sb("ci", 64, I32); sb("cf", 64, F32); sb("uls", 8, U16); sb("sg", 100, F32); sb("idl", 20, U16)
+    sb("ali", 20, I32); sb("l0", 20, U16)
+    sb("nt", 640, I32); sb("ni", 640, I32); sb("nf", 3840, F32); sb("tw", 640, F32)
+    sb("iw", 320, F32); sb("orow", 320, F32); sb("yb", 320, F32); sb("kx", 120 * R, F32); sb("hb", 100 * R, I32)
+    for r in range(R + 1):
+        sb("x%d" % r, 1280, BF); sb("qx%d" % r, 320, MX); sb("sx%d" % r, 320, U8)
+    for r in range(R):
+        sb("f%d" % r, 1280, BF); sb("fp%d" % r, 1280, BF); sb("z%d" % r, 1280, BF)
+        sb("qz%d" % r, 320, MX); sb("sz%d" % r, 320, U8)
+        sb("qp%d" % r, 320, MX); sb("sp%d" % r, 320, U8)
+        sb("rq%d" % r, 320, MX); sb("rs%d" % r, 320, U8)
+        sb("ll%d" % r, 10, U16); sb("rl%d" % r, 10, U16)
+        sb("bw%d" % r, 320, BF); sb("br%d" % r, 640, BF); sb("bt%d" % r, 640, BF)
+        sb("er%d" % r, 640, BF); sb("et%d" % r, 640, BF)
+        sb("tr%d" % r, 640, F32); sb("gt%d" % r, 640, F32)
+        sb("fs%d" % r, 1000, F32); sb("is%d" % r, 320, I32)
+        sb("us%d" % r, 100, U16)
+    return s
+
+
+SCRATCH = _scratch()
+SEMAPHORES = (["vq", "sq", "tq", "gq", "loc"]
+              + ["ld_x0", "ld_x1", "ld_u", "ld_v", "ld_w", "ld_al", "ld_nx", "outs"]
+              + ["kx%d" % r for r in range(R)]
+              + ["%s%d%d" % (k, r, h) for k in ("rc", "rp", "qa") for r in range(R) for h in range(2)]
+              + ["%s%d" % (k, r) for k in ("rl", "la") for r in range(R)])
+
+
+def _relays(core, nxt, topo):
+    w = [c for c in topo.cores_of(core) if c != core and topo.may_write(c, nxt)]
+    near = [c for c in w if topo.die(c) == topo.die(core)]
+    far = [c for c in w if topo.die(c) != topo.die(core)]
+    return near[0], near[1], far[0]
+
+
+def _mask(es):
+    m = 0
+    for e in es:
+        m |= 1 << e
+    return m
+
+
+def _hand_on(g, core, T, topo):
+    mine = [c for c in topo.cores_of(core) if T.rank_of(c) is not None]
+    if not mine:
+        return
+    nxt = T.cores[(T.rank_of(mine[0]) + 1) % N]
+    rel = _relays(mine[0], nxt, topo)
+    if core not in rel:
+        return
+    k = rel.index(core)
+    rid, pid = topo.addr(nxt, core)
+    m = topo.mask(core, nxt)
+    ne = len(topo.engines(core, nxt))
+    near = len(topo.engines(mine[0], core))
+    n = 0
+    for r in range(R):
+        for h in range(2):
+            if k == 0:
+                g.wait_ge(T.sem["rp%d%d" % (r, h)], near)
+                g.remote_dma(T["sp%d" % r][:, H * h:H * h + H], T["rs%d" % r][:, H * h:H * h + H],
+                             T.sem["qa%d%d" % (r, h)], T.sem.loc, pid, rid, m)
+            else:
+                a = H * h + 80 * (k - 1)
+                g.wait_ge(T.sem["rc%d%d" % (r, h)], near // 2)
+                g.remote_dma(T["qp%d" % r][:, a:a + 80].bitcast(dt.uint8), T["rq%d" % r][:, a:a + 80].bitcast(dt.uint8),
+                             T.sem["qa%d%d" % (r, h)], T.sem.loc, pid, rid, m)
+            n += ne
+        if k == 0:
+            g.wait_ge(T.sem["rl%d" % r], near)
+            g.remote_dma(T["ll%d" % r][:], T["rl%d" % r][:], T.sem["la%d" % r], T.sem.loc, pid, rid, m)
+            n += ne
+    g.wait_ge(T.sem.loc, n)
+
+
+def rank_program(g, core, T, topo):
+    rank = T.rank_of(core)
+    if rank is None:
+        return _hand_on(g, core, T, topo)
+    nxt = T.cores[(rank + 1) % N]
+    rel = _relays(core, nxt, topo)
+    before = T.cores[(rank - 1) % N]
+    far_engines = len(topo.engines(_relays(before, core, topo)[0], core))
+    Q = {"v": g.vector, "s": g.scalar, "t": g.tensor, "g": g, "y": g.sync}
+    cnt = {"v": 0, "s": 0, "t": 0, "g": 0}
+    seen = {k: {} for k in Q}
+    dma_n = {}
+    loc = [0]
+
+    def need(e, toks):
+        for t in toks:
+            if isinstance(t, list):
+                need(e, t)
+            elif seen[e].get(t[0], 0) < t[1]:
+                Q[e].wait_ge(T.sem[t[0]], t[1])
+                seen[e][t[0]] = t[1]
+
+    def op(e, toks, name, *a, **k):
+        need(e, toks)
+        q = Q[e]
+        f = {"cp": lambda: q.tensor_copy(*a), "tt": lambda: q.tensor_tensor(*a), "ts": lambda: q.tensor_scalar(*a),
+             "ms": lambda: q.memset(*a), "tp": lambda: q.transpose(*a), "qz": lambda: q.quantize_mx(*a),
+             "scan": lambda: q.tensor_tensor_scan(*a), "act": lambda: q.activation(*a, **k), "mm": lambda: q.matmul_mx(*a),
+             "iota": lambda: q.iota(*a, **k), "sel": lambda: q.affine_select(*a)}[name]
+        f().then_inc(T.sem[e + "q"], 1)
+        cnt[e] += 1
+        return (e + "q", cnt[e])
+
+    def dma(e, toks, out, in_, sem):
+        need(e, toks)
+        Q[e].dma_start(out, in_).then_inc(T.sem[sem], 16)
+        dma_n[sem] = dma_n.get(sem, 0) + 16
+
+    def done(sem):
+        return (sem, dma_n[sem])
+
+    banks = [T["pk%d" % k] for k in range(8)]
+    readers = [[] for k in range(8)]
+    turn = [0]
+
+    def bank():
+        k = turn[0] % 8
+        turn[0] += 1
+        return k
+
+    def mm(toks, k, n, lc, ls, b, rc, rs, a, start=True, stop=True):
+        w = [toks, readers[k]] if start else [toks]
+        if start:
+            readers[k] = []
+        return op("t", w, "mm", banks[k][:, 0:n], lc[:, 128 * b:128 * b + 128], ls[:, 128 * b:128 * b + 128],
+                  rc[:, a:a + n], rs[:, a:a + n], start, stop)
+
+    ci, cf = T.ci, T.cf
+
+    def icol(k):
+        return ci[:, k:k + 1]
+
+    def col(k):
+        return cf[:, k:k + 1]
+
+    gi = op("g", [], "iota", ci[:, 0:1], [[0, 1]], 0, 1)
+    gn = op("g", [], "iota", T.nt[:, 320:640], [[1, 4], [4, 80]], 0, 0)
+    gi3 = op("g", [], "iota", ci[:, 32:40], [[16, 8]], 0, 0)
+    g_id = op("g", [], "iota", T.ni[:, 0:20], [[16, 10], [0, 2]], 0, 0)
+    lanes = {"y": [], "s": []}
+    for i in range(16):
+        lanes["s" if i % 2 else "y"].append(i)
+
+    def table_loads(q, t):
+        for l in lanes[q]:
+            if l // 8 == t:
+                e = (l // 2) % 4
+                dma(q, [], T.nt[l:128:16, 0:320], T.nx[e:128:4, 80 * t:80 * t + 80], "ld_nx")
+                if t:
+                    dma(q, [gn], T.nt[l:128:16, 320:640], T.nx[e:128:4, 0:80], "ld_nx")
+    table_loads("y", 0)
+    table_loads("s", 0)
+    dma("s", [], T.ub[:], T.u[:], "ld_u")
+    dma("y", [], T.x0[:, 0:640], T.x[:, 0:640], "ld_x0")
+    table_loads("s", 1)
+    table_loads("y", 1)
+    dma("y", [], T.x0[:, 640:1280], T.x[:, 640:1280], "ld_x1")
+    dma("s", [], T.ali[:], T.al[:], "ld_al")
+    dma("y", [], T.wq[:].bitcast(dt.uint8), T.wc[:], "ld_w")
+    dma("y", [], T.wp[:], T.ws[:], "ld_w")
+    dma("y", [], T.vb[:], T.v[:], "ld_v")
+
+    o1 = op("v", [gi], "ts", icol(1), icol(0), 15, None, A.bitwise_and)
+    op("v", [], "ts", icol(2), icol(0), 4, 1, A.arith_shift_right, A.bitwise_and)
+    op("v", [], "ts", icol(3), icol(0), 1, 3, A.arith_shift_right, A.bitwise_and)
+    o4 = op("v", [], "ts", icol(4), icol(0), 1, None, A.bitwise_and)
+    o5 = op("v", [o4], "cp", cf[:, 1:5], ci[:, 1:5])
+    LF, GF, EF, YF = 1, 2, 3, 4
+    ln2, ln16 = math.log(2.0), math.log(16.0)
+    b2 = -ln2 + math.log(0.95)
+    v_one = op("v", [], "ms", T.one[:], 1.0)
+    op("v", [o5], "tt", col(5), col(GF), col(YF), A.max)
+    op("v", [], "ts", col(6), col(EF), -1.0, 3.0, A.mult, A.add)
+    k1 = op("v", [], "ts", col(14), col(YF), -1.0, 1.0, A.mult, A.add)
+    k2 = op("v", [k1], "ts", col(7), col(5), 3.0, 1.0, A.mult, A.add)
+    k3 = op("v", [k2], "tt", col(8), col(6), col(7), A.mult)
+    q1 = op("s", [k3], "act", col(9), col(8), AF.Exp, scale=ln2)
+    q2 = op("s", [q1], "act", col(10), col(9), AF.Identity, bias=MAGIC)
+    op("v", [], "ts", col(12), col(GF), (ln2 - ln16) / 512.0, ln16 / 512.0, A.mult, A.add)
+    c5 = op("v", [], "ts", col(13), col(GF), b2 + ln16, -ln16, A.mult, A.add)
+    op("v", [], "ts", col(15), col(LF), 14.0, None, A.not_equal)
+    op("v", [], "ts", col(16), col(LF), 10.0, None, A.not_equal)
+    op("v", [], "ts", col(17), col(LF), 14.0, None, A.is_equal)
+    k4 = op("v", [], "ts", col(18), col(LF), 10.0, 17.0, A.is_equal, A.mult)
+    op("v", [k4], "tt", col(19), col(15), col(16), A.mult)
+    k5 = op("v", [], "tt", col(20), col(17), col(18), A.add)
+    k6 = op("v", [k5, gi3], "ts", cf[:, 32:40], ci[:, 32:40], col(19), col(20), A.mult, A.add)
+    k7 = op("v", [], "tt", col(21), col(GF), col(14), A.mult)
+    v_ul = op("v", [k6], "cp", T.uls[:], cf[:, 32:40])
+    k8 = op("v", [k7], "ts", col(22), col(21), 1.0 - 2.0 ** -15, 2.0 ** -15, A.mult, A.add)
+    g_eb = op("g", [v_one], "sel", T.eb[:], T.one[:], [[-1, 516]], A.is_equal, 0.0, 3, 4)
+    g_iw = op("g", [], "iota", T.iw[:], [[1, 320]], 0, 0, allow_small_or_imprecise_dtypes=True)
+    v64 = op("s", [g_eb], "act", T.eb64[:], T.eb[:], AF.Copy, scale=64.0)
+    op("v", [], "ms", T.kx[:, 0:120 * R:2], 4680.0 * 2.0 ** -15)
+    op("v", [], "ms", T.kx[:, 1:120 * R:2], 4680.0)
+    op("v", [], "ms", T.hb[:], 1)
+    g1 = op("v", [], "ms", T.sg[:], 1.0)
+    seg = op("v", [g1], "ms", T.sg[:, 0:100:5], 0.0)
+    k9 = op("v", [q2, k8], "ts", col(23), col(10), MAGIC, col(22), A.subtract, A.mult)
+    nt, ni, nf, tw = T.nt, T.ni, T.nf, T.tw
+    w1 = op("v", [done("ld_nx"), gn], "ts", nf[:, 0:640], nt[:], -159.5, BIG, A.add, A.add)
+    w2 = op("s", [w1], "act", nf[:, 640:1280], nf[:, 0:640], AF.Identity, bias=-BIG)
+    w3 = op("s", [w2, c5], "act", nf[:, 1280:1920], nf[:, 640:1280], AF.Exp, bias=col(13), scale=col(12))
+    w4 = op("s", [w3], "act", nf[:, 1920:2560], nf[:, 1280:1920], AF.Identity, bias=MAGIC)
+    op("v", [k9], "tt", col(24), col(23), col(YF), A.mult)
+    c8 = op("v", [], "tt", col(25), col(23), col(14), A.mult)
+    qu = op("v", [("ld_u", 16)], "qz", T.uq[:], T.up[:], T.ub[:])
+    op("v", [qu, v_ul], "cp", T.uq2[:].bitcast(dt.uint32), T.uq[:].bitcast(dt.uint32).indirect(T.uls[:]))
+    v_u = op("v", [], "cp", T.up2[:], T.up[:].indirect(T.uls[:]))
+    qx = [op("v", [("ld_x%d" % h, 16)], "qz", T.qx0[:, H * h:H * h + H], T.sx0[:, H * h:H * h + H], T.x0[:, 640 * h:640 * h + 640])
+          for h in range(2)]
+
+    def send_codes(r, h, tok):
+        need("g", [tok])
+        es = topo.engines(core, rel[1])
+        n = len(es) // 2
+        tr = []
+        for k in (1, 2):
+            a = H * h + 80 * (k - 1)
+            rid, pid = topo.addr(rel[k], core)
+            tr.append(RemoteDMATransfer(dst_ids=[DstId(rid=rid, pnc=pid)], dma_engine_mask=_mask(es[n * k - n:n * k]),
+                                        remote_sem=T.sem["rc%d%d" % (r, h)], src=T["qx%d" % r][:, a:a + 80].bitcast(dt.uint8),
+                                        dst=T["rq%d" % r][:, a:a + 80].bitcast(dt.uint8)))
+        g.remote_dma_fused(tr, local_sem=T.sem.loc)
+        rid, pid = topo.addr(rel[0], core)
+        g.remote_dma(T["rs%d" % r][:, H * h:H * h + H], T["sx%d" % r][:, H * h:H * h + H], T.sem["rp%d%d" % (r, h)],
+                     T.sem.loc, pid, rid, topo.mask(core, rel[0]))
+        loc[0] += 4 * n
+
+    def scores(r, h, tok):
+        k = bank()
+        return k, mm([tok, v_u], k, H, T.uq2, T.up2, 0, T["qx%d" % r], T["sx%d" % r], H * h)
+
+    def bits(r, h, kt):
+        k, t = kt
+        o = op("v", [t], "ts", T["bw%d" % r][:, H * h:H * h + H], banks[k][:, 0:H], 0.0, None, A.is_gt)
+        readers[k].append(o)
+        return o
+
+    def unpack(r, h, tok, own=True):
+        ps = []
+        for b in range(4):
+            k = bank()
+            qc, qs = (T["qx%d" % r], T["sx%d" % r]) if own else (T["qp%d" % r], T["sp%d" % r])
+            ps.append((k, mm([tok, vE], k, H, T.ec, T.es, b, qc, qs, H * h)))
+        return ps
+
+    def unpack_copy(r, h, ps, own=True):
+        d = T["f%d" % r] if own else T["fp%d" % r]
+        for b in range(4):
+            k, t = ps[b]
+            o = op("s", [t], "act", d[:, 320 * b + H * h:320 * b + H * h + H], banks[k][:, 0:H], AF.Copy)
+            readers[k].append(o)
+        return o
+
+    def edge_rows(r, h, tok):
+        return op("s", [tok, v_id], "act", T["er%d" % r][:, 320 * h:320 * h + 320],
+                  T["bw%d" % r][:, H * h:H * h + H].indirect(T.idl[:]), AF.Copy)
+
+    sc = [scores(0, 0, qx[0]), scores(0, 1, qx[1])]
+    send_codes(0, 0, qx[0])
+    send_codes(0, 1, qx[1])
+    i1 = op("v", [g_id], "ts", ci[:, 40:60], ni[:, 0:20], col(LF), None, A.add)
+    n1 = op("v", [i1], "ts", ni[:], nt[:], 511, None, A.bitwise_and)
+    v_id = op("v", [i1], "cp", T.idl[:], ci[:, 40:60])
+    n2 = op("v", [n1], "tt", nf[:, 2560:2880], ni[:, 0:320], ni[:, 320:640], A.subtract)
+    w5 = op("v", [w4], "tt", nf[:, 3200:3520], nf[:, 1920:2240], nf[:, 2240:2560], A.subtract)
+    bt_ = [bits(0, 0, sc[0]), bits(0, 1, sc[1])]
+    n3 = op("s", [n2, c8], "act", nf[:, 2880:3200], nf[:, 2560:2880], AF.Copy, scale=col(24))
+    w6 = op("s", [w5, c8], "act", nf[:, 3520:3840], nf[:, 3200:3520], AF.Copy, scale=col(25))
+    l0 = T.l0
+    op("v", [], "ts", col(26), col(GF), -320.0, 320.0, A.mult, A.add)
+    c2 = op("v", [], "ts", col(27), col(GF), 320.0, None, A.mult)
+    v_l0 = op("v", [("ld_al", 16)], "cp", l0[:], T.ali[:])
+
+    def dup(dst, src, toks, h):
+        a = 20 * h
+        op("v", [toks, c2], "cp", dst[:, 20 + a:40 + a:2], src)
+        op("v", [], "cp", dst[:, 21 + a:40 + a:2], src)
+        op("v", [], "ts", dst[:, 60 + a:80 + a:2], src, col(27), None, A.add)
+        return op("v", [], "ts", dst[:, 61 + a:80 + a:2], src, col(26), None, A.add)
+    lists = [dup(T.us0, l0[:, 10 * h:10 * h + 10], [v_l0], h) for h in range(2)]
+    c3 = op("v", [], "ts", col(11), col(GF), -4680.0 * 2.0 ** -15, 4680.0 * 2.0 ** -15, A.mult, A.add)
+    for q in range(4):
+        wl = op("v", [w6, n3], "tt", tw[:, q:320:4], nf[:, 2880 + 80 * q:2960 + 80 * q], nf[:, 3520 + 80 * q:3600 + 80 * q], A.add)
+    v_tw = op("s", [wl, k1], "act", tw[:, 320:640], tw[:, 0:320], AF.Copy, scale=col(14))
+    for b in range(4):
+        vE = op("v", [g_eb], "qz", T.ec[:, 128 * b:128 * b + 128], T.es[:, 128 * b:128 * b + 128], T.eb[:, 3 - b:515 - b])
+    pF = unpack(0, 0, qx[0])
+    tF = [None, None]
+
+    def table_lookup(r, h, e, tok):
+        out, win = T["tr%d" % r][:, 320 * h:320 * h + 320], tw[:].indirect(T["us%d" % r][:, 60 + 20 * h:80 + 20 * h])
+        return op("v", [tok, v_tw], "cp", out, win) if e == "v" else op("s", [tok, v_tw], "act", out, win, AF.Copy)
+
+    def table_turn(r, h, tok):
+        a, gt, fs = 320 * h, T["gt%d" % r], T["fs%d" % r]
+        t = op("v", [tok], "tp", gt[:, a:a + 320], T["tr%d" % r][:, a:a + 320])
+        x1, x2 = fs[:, 80 + 40 * h:120 + 40 * h], fs[:, 920 + 40 * h:960 + 40 * h]
+        op("v", [t], "tt", x1, gt[:, a:a + 320:8], gt[:, a + 2:a + 320:8], A.add)
+        p = op("v", [], "tt", x2, gt[:, a + 4:a + 320:8], gt[:, a + 6:a + 320:8], A.add)
+        return op("v", [p], "tt", fs[:, 40 * h:40 * h + 40], x1, x2, A.add)
+
+    trow = [table_lookup(0, 0, "s", lists[0]), table_lookup(0, 1, "v", lists[1])]
+    for r in range(R):
+        rn = r + 1
+        us, fs, ints, bw = T["us%d" % r], T["fs%d" % r], T["is%d" % r], T["bw%d" % r]
+        br, btb, gt = T["br%d" % r], T["bt%d" % r], T["gt%d" % r]
+        kb, hh = 120 * r, 100 * r
+        cur = (l0[:, 0:10], l0[:, 10:20]) if r == 0 else (T["us%d" % (r - 1)][:, 0:10], T["ll%d" % (r - 1)][:])
+        p1 = op("v", [bt_, lists], "cp", br[:, 0:320], bw[:].indirect(us[:, 20:40]))
+        p2 = op("s", [bt_, lists], "act", br[:, 320:640], bw[:].indirect(us[:, 40:60]), AF.Copy)
+        if r == 0:
+            er = [edge_rows(0, 0, bt_[0]), None]
+            tab = [table_turn(0, h, trow[h]) for h in range(2)]
+        er[1] = edge_rows(r, 1, bt_[1])
+        v_bt = op("v", [p1, p2], "tp", btb[:], br[:])
+        km = op("v", [v_bt, tab], "tt", fs[:, 160:200], fs[:, 1:80:2], btb[:, 0:640:16], A.mult)
+        ks = op("v", [km], "tt", fs[:, 200:240], fs[:, 160:200], fs[:, 0:80:2], A.add)
+        for d in (1, 2, 3):
+            dma("y", [ks], T.kx[32 * d:128, kb + 40 * (3 - d):kb + 40 * (4 - d)], fs[0:128 - 32 * d, 200:240], "kx%d" % r)
+        if r == 0:
+            tF[0] = unpack_copy(0, 0, pF)
+        tF[1] = unpack_copy(r, 1, unpack(r, 1, qx[1]))
+        nm = [op("v", [v_bt], "tt", fs[:, 240 + 40 * e:280 + 40 * e], gt[:, 9 + 2 * e:640:16], btb[:, 0:640:16], A.mult) for e in range(4)]
+        ko = op("v", [ks, c3], "ts", fs[:, 860:880], fs[:, 200:240:2], col(GF), col(11), A.mult, A.add)
+        ns = [op("v", [nm[e]], "tt", fs[:, 400 + 40 * e:440 + 40 * e], fs[:, 240 + 40 * e:280 + 40 * e], gt[:, 1 + 2 * e:640:16], A.add)
+              for e in range(4)]
+        op("v", [], "cp", fs[:, 560:610:5], cur[0])
+        op("v", [], "cp", fs[:, 610:660:5], cur[1])
+        et = T["et%d" % r]
+        e1 = op("v", [er], "tp", et[:], T["er%d" % r][:])
+        de = [op("v", [ns[e]], "tt", fs[:, 561 + e:660:5], fs[:, 400 + 40 * e:440 + 40 * e:2], fs[:, 401 + 40 * e:440 + 40 * e:2], A.add)
+              for e in range(4)]
+        op("v", [e1], "ts", fs[:, 880:900], et[:, 14:640:32], 3.0, 1.0, A.mult, A.add)
+        e3 = op("v", [], "ts", fs[:, 900:920], et[:, 10:640:32], 32768.0, 32768.0, A.mult, A.add)
+        st = op("v", [e3], "tt", ints[:, 0:20], fs[:, 880:900], fs[:, 900:920], A.mult)
+        sv, at = ints[:, 0:20], 20
+        for j in range(6):
+            tv = ints[:, at:at + 20]
+            a = kb + 40 * (j // 2) + j % 2
+            st = op("v", [st, done("kx%d" % r)], "tt", tv, T.kx[:, a:kb + 40 * (j // 2) + 40:2], sv, A.mult)
+            sv = ints[:, at + 20:at + 40]
+            st = op("v", [st], "ts", sv, tv, 0x78000 if j % 2 else 0x8888, None, A.bitwise_and)
+            at += 40
+        tv = ints[:, at:at + 20]
+        st = op("v", [st, ko], "tt", tv, fs[:, 860:880], sv, A.mult)
+        hs = [op("v", [st], "ts", T.hb[:, hh + 1 + e:hh + 100:5], tv, 1 << (4 * e + 3), None, A.bitwise_and) for e in range(4)]
+        st = op("v", [hs, de], "tt", fs[:, 660:760], T.hb[:, hh:hh + 100], fs[:, 560:660], A.mult)
+        st = op("v", [st, seg], "scan", fs[:, 760:860], T.sg[:], fs[:, 660:760], 0.0, A.mult, A.add)
+        lm = op("v", [st], "cp", us[:, 10:20], fs[:, 814:860:5])
+        need("g", [lm])
+        rid, pid = topo.addr(rel[0], core)
+        g.remote_dma(T["rl%d" % r][:], us[:, 10:20], T.sem["rl%d" % r], T.sem.loc, pid, rid, topo.mask(core, rel[0]))
+        loc[0] += len(topo.engines(core, rel[0]))
+        ls = op("v", [], "cp", us[:, 0:10], fs[:, 764:810:5])
+        qa = [("qa%d%d" % (r, h), 3 * far_engines) for h in range(2)]
+        tP = [unpack_copy(r, 0, unpack(r, 0, qa[0], own=False), own=False), None]
+        if r == 0:
+            for b in range(4):
+                v64q = op("v", [v64], "qz", T.e64c[:, 128 * b:128 * b + 128], T.e64s[:, 128 * b:128 * b + 128], T.eb64[:, 3 - b:515 - b])
+
+        def make(h, toks, off, F):
+            z, q, s, o = T["z%d" % r], T["qz%d" % r], T["sz%d" % r], []
+            for b in range(4):
+                win, out = F[:, 320 * b:320 * b + 320].indirect(off), z[:, 640 * h + b:640 * h + 640:4]
+                o.append(op("v", [toks], "cp", out, win) if b < 2 else op("s", [toks], "act", out, win, AF.Copy))
+            zq = op("v", [o], "qz", q[:, H * h:H * h + H], s[:, H * h:H * h + H], z[:, 640 * h:640 * h + 640])
+            ps = []
+            for b in range(4):
+                k = bank()
+                mm([zq, ("ld_w", 32)], k, H, T.wq, T.wp, b, q, s, H * h, True, False)
+                ps.append((k, mm([zq, v64q], k, H, T.e64c, T.e64s, b, q, s, H * h, False, True)))
+            return ps
+
+        def renew(h, b, ps, e):
+            k, t = ps[b]
+            out = T["x%d" % rn][:, 640 * h + b:640 * h + 640:4]
+            o = op("v", [t], "ts", out, banks[k][:, 0:H], 0.015625, None, A.mult) if e == "v" else \
+                op("s", [t], "act", out, banks[k][:, 0:H], AF.Copy, scale=0.015625)
+            readers[k].append(o)
+            return o
+
+        def requant(h, toks):
+            return op("v", [toks], "qz", T["qx%d" % rn][:, H * h:H * h + H], T["sx%d" % rn][:, H * h:H * h + H],
+                      T["x%d" % rn][:, 640 * h:640 * h + 640])
+
+        def outputs(h, tok, ea, eb):
+            k = bank()
+            t = mm([tok, vv], k, H, T.vq, T.vp, 0, T["qx%d" % rn], T["sx%d" % rn], H * h)
+            dma(ea, [tok], T.oc[:, 640 * h:640 * h + 640], T["qx%d" % rn][:, H * h:H * h + H].bitcast(dt.uint8), "outs")
+            for i in range(4):
+                dma(eb if i % 2 else ea, [tok], T.osc[4 * i:4 * i + 4, H * h:H * h + H], T["sx%d" % rn][32 * i:32 * i + 4, H * h:H * h + H], "outs")
+            o = op("v", [t], "cp", T.yb[:, H * h:H * h + H], banks[k][:, 0:H])
+            readers[k].append(o)
+            dma(ea, [o], T.y[:, H * h:H * h + H], T.yb[:, H * h:H * h + H], "outs")
+
+        ps = make(0, [ls, tF], us[:, 0:10], T["f%d" % r])
+        if rn < R:
+            lists = [dup(T["us%d" % rn], us[:, 0:10], [ls], 0), None]
+        else:
+            vv = op("v", [("ld_v", 16)], "qz", T.vq[:], T.vp[:], T.vb[:])
+        o = [renew(0, b, ps, "v" if b % 2 else "s") for b in range(4)]
+        tP[1] = unpack_copy(r, 1, unpack(r, 1, qa[1], own=False), own=False)
+        qx = [requant(0, o), None]
+        land, la = T["ll%d" % r], ("la%d" % r, far_engines)
+        if rn < R:
+            s0 = scores(rn, 0, qx[0])
+            p0 = unpack(rn, 0, qx[0])
+            send_codes(rn, 0, qx[0])
+            t0 = table_lookup(rn, 0, "s", lists[0])
+            tF = [unpack_copy(rn, 0, p0), None]
+            bt_ = [bits(rn, 0, s0), None]
+            tab = [table_turn(rn, 0, t0), None]
+            er = [edge_rows(rn, 0, bt_[0]), None]
+        else:
+            oa1 = op("s", [ls, g_iw], "act", T.orow[:, 0:H], T.iw[:].indirect(us[:, 0:10]), AF.Copy)
+            outputs(0, qx[0], "y", "y")
+        ps = make(1, [la, tP], land[:], T["fp%d" % r])
+        if rn < R:
+            lists[1] = dup(T["us%d" % rn], land[:], [la], 1)
+            tab[1] = table_turn(rn, 1, table_lookup(rn, 1, "v", lists[1]))
+        else:
+            oa2 = op("v", [la, g_iw], "cp", T.orow[:, H:C], T.iw[:].indirect(land[:]))
+            dma("y", [oa1, oa2], T.oa[:], T.orow[0:128:16, :], "outs")
+        o = [renew(1, b, ps, "s") for b in range(4)]
+        qx[1] = requant(1, o)
+        if rn < R:
+            send_codes(rn, 1, qx[1])
+            bt_[1] = bits(rn, 1, scores(rn, 1, qx[1]))
+        else:
+            outputs(1, qx[1], "y", "s")
+    need("g", [("loc", loc[0]), done("outs")])
+    for e in ("v", "s", "t", "g"):
+        need("g", [(e + "q", cnt[e])])

@@ -1,11 +1,10 @@
-import math
 from concourse.bass import DstId, RemoteDMATransfer
-from concourse.mybir import dt, AluOpType as A, AxisListType, ActivationFunctionType as AF
+from concourse.mybir import dt, AluOpType as A, ActivationFunctionType as AF
 
 N, C, H, R = 8, 320, 160, 3
 BF, F32, I32, U16, U8, MX = "bfloat16", "float32", "int32", "uint16", "uint8", "float8_e4m3fn_x4"
-MAGIC = 12582912.0
-BIG = 1.5 * 2.0 ** 32
+SAME = 4680.0
+INV = 0.015625
 
 
 def _scratch():
@@ -18,12 +17,12 @@ def _scratch():
     sb("ub", 512, BF); sb("uq", 128, MX); sb("up", 128, U8); sb("uq2", 128, MX); sb("up2", 128, U8)
     sb("vb", 512, BF); sb("vq", 128, MX); sb("vp", 128, U8)
     sb("wq", 512, MX); sb("wp", 512, U8)
-    sb("one", 516, BF); sb("eb", 516, BF); sb("eb64", 516, BF)
-    sb("ec", 512, MX); sb("es", 512, U8); sb("e64c", 512, MX); sb("e64s", 512, U8)
-    sb("ci", 64, I32); sb("cf", 64, F32); sb("uls", 8, U16); sb("sg", 100, F32); sb("idl", 20, U16)
+    sb("c64", 516, BF); sb("eb", 516, BF); sb("ec", 512, MX); sb("es", 512, U8)
+    sb("ci", 64, I32); sb("cf", 64, F32); sb("uls", 8, U16); sb("sg", 100, F32); sb("idl", 20, U16); sb("rt", 24, U16)
     sb("ali", 20, I32); sb("l0", 20, U16)
-    sb("nt", 640, I32); sb("ni", 640, I32); sb("nf", 3840, F32); sb("tw", 640, F32)
-    sb("iw", 320, F32); sb("orow", 320, F32); sb("yb", 320, F32); sb("kx", 120 * R, F32); sb("hb", 100 * R, I32)
+    sb("nt", 160, I32); sb("ni", 480, I32); sb("ia", 320, F32); sb("un", 176, F32); sb("nf", 176, F32); sb("hn", 384, BF)
+    sb("ru", 576, F32); sb("rw", 672, F32); sb("gg", 384, F32); sb("g2", 384, F32); sb("tw", 640, F32)
+    sb("iw", 320, F32); sb("orow", 320, F32); sb("yb", 320, F32); sb("kx", 240, F32); sb("hb", 100, I32)
     for r in range(R + 1):
         sb("x%d" % r, 1280, BF); sb("qx%d" % r, 320, MX); sb("sx%d" % r, 320, U8)
     for r in range(R):
@@ -35,15 +34,14 @@ def _scratch():
         sb("bw%d" % r, 320, BF); sb("br%d" % r, 640, BF); sb("bt%d" % r, 640, BF)
         sb("er%d" % r, 640, BF); sb("et%d" % r, 640, BF)
         sb("tr%d" % r, 640, F32); sb("gt%d" % r, 640, F32)
-        sb("fs%d" % r, 1000, F32); sb("is%d" % r, 320, I32)
+        sb("fs%d" % r, 740, F32); sb("is%d" % r, 260, I32)
         sb("us%d" % r, 100, U16)
     return s
 
 
 SCRATCH = _scratch()
 SEMAPHORES = (["vq", "sq", "tq", "gq", "loc"]
-              + ["ld_x0", "ld_x1", "ld_u", "ld_v", "ld_w", "ld_al", "ld_nx", "outs"]
-              + ["kx%d" % r for r in range(R)]
+              + ["ld_x0", "ld_x1", "ld_u", "ld_v", "ld_w", "ld_al", "ld_nx", "outs", "kx0", "kx1", "kx2"]
               + ["%s%d%d" % (k, r, h) for k in ("rc", "rp", "qa") for r in range(R) for h in range(2)]
               + ["%s%d" % (k, r) for k in ("rl", "la") for r in range(R)])
 
@@ -132,8 +130,6 @@ def rank_program(g, core, T, topo):
         need(e, toks)
         Q[e].dma_start(out, in_).then_inc(T.sem[sem], 16)
         dma_n[sem] = dma_n.get(sem, 0) + 16
-
-    def done(sem):
         return (sem, dma_n[sem])
 
     banks = [T["pk%d" % k] for k in range(8)]
@@ -160,81 +156,73 @@ def rank_program(g, core, T, topo):
     def col(k):
         return cf[:, k:k + 1]
 
-    gi = op("g", [], "iota", ci[:, 0:1], [[0, 1]], 0, 1)
-    gn = op("g", [], "iota", T.nt[:, 320:640], [[1, 4], [4, 80]], 0, 0)
-    gi3 = op("g", [], "iota", ci[:, 32:40], [[16, 8]], 0, 0)
-    g_id = op("g", [], "iota", T.ni[:, 0:20], [[16, 10], [0, 2]], 0, 0)
-    lanes = {"y": [], "s": []}
-    for i in range(16):
-        lanes["s" if i % 2 else "y"].append(i)
+    ld_nx = dma("y", [], T.nt[:], T.nx[:], "ld_nx")
+    ld_u = dma("s", [], T.ub[:], T.u[:], "ld_u")
+    ld_x = [dma("y", [], T.x0[:, 640 * h:640 * h + 640], T.x[:, 640 * h:640 * h + 640], "ld_x%d" % h) for h in range(2)]
+    ld_al = dma("s", [], T.ali[:], T.al[:], "ld_al")
 
-    def table_loads(q, t):
-        for l in lanes[q]:
-            if l // 8 == t:
-                e = (l // 2) % 4
-                dma(q, [], T.nt[l:128:16, 0:320], T.nx[e:128:4, 80 * t:80 * t + 80], "ld_nx")
-                if t:
-                    dma(q, [gn], T.nt[l:128:16, 320:640], T.nx[e:128:4, 0:80], "ld_nx")
-    table_loads("y", 0)
-    table_loads("s", 0)
-    dma("s", [], T.ub[:], T.u[:], "ld_u")
-    dma("y", [], T.x0[:, 0:640], T.x[:, 0:640], "ld_x0")
-    table_loads("s", 1)
-    table_loads("y", 1)
-    dma("y", [], T.x0[:, 640:1280], T.x[:, 640:1280], "ld_x1")
-    dma("s", [], T.ali[:], T.al[:], "ld_al")
-    dma("y", [], T.wq[:].bitcast(dt.uint8), T.wc[:], "ld_w")
-    dma("y", [], T.wp[:], T.ws[:], "ld_w")
-    dma("y", [], T.vb[:], T.v[:], "ld_v")
+    fl = {"allow_small_or_imprecise_dtypes": True}
+    v_c64 = op("v", [], "ms", T.c64[:], 64.0)
+    g_p = op("g", [], "iota", icol(0), [[0, 1]], 0, 1)
+    g_ia = op("g", [], "iota", T.ia[:, 0:160], [[0, 2], [4, 80]], 0, 0, **fl)
+    op("g", [], "iota", ci[:, 8:16], [[16, 8]], 0, 0)
+    g_rt = op("g", [], "iota", ci[:, 16:28], [[4, 4], [32, 3]], 0, 0)
+    g_id = op("g", [], "iota", ci[:, 28:48], [[16, 10], [0, 2]], 0, 0)
+    g_eb = op("g", [v_c64], "sel", T.eb[:], T.c64[:], [[-1, 516]], A.is_equal, 0.0, 3, 4)
+    LANE, ODD, M4, R8, T8 = 1, 2, 3, 4, 5
+    op("v", [], "ms", T.un[:, 160:176], 8.0)
+    op("v", [], "ms", T.nf[:, 160:176], 0.0)
+    for k, (sh, m) in enumerate([(0, 15), (4, 1), (2, 3), (0, 7), (3, 1)]):
+        o = op("v", [g_p], "ts", icol(1 + k), icol(0), sh, m, A.arith_shift_right, A.bitwise_and)
+    cols = op("v", [o], "cp", cf[:, 1:6], ci[:, 1:6])
+    op("v", [], "ms", T.hn[:, 0:192], 16.0)
+    o = op("v", [], "ms", T.hn[:, 192:384], 2.0)
+    KL, UP0, UP1, ES, KO, TH = 6, 7, 8, 9, 10, 11
 
-    o1 = op("v", [gi], "ts", icol(1), icol(0), 15, None, A.bitwise_and)
-    op("v", [], "ts", icol(2), icol(0), 4, 1, A.arith_shift_right, A.bitwise_and)
-    op("v", [], "ts", icol(3), icol(0), 1, 3, A.arith_shift_right, A.bitwise_and)
-    o4 = op("v", [], "ts", icol(4), icol(0), 1, None, A.bitwise_and)
-    o5 = op("v", [o4], "cp", cf[:, 1:5], ci[:, 1:5])
-    LF, GF, EF, YF = 1, 2, 3, 4
-    ln2, ln16 = math.log(2.0), math.log(16.0)
-    b2 = -ln2 + math.log(0.95)
-    v_one = op("v", [], "ms", T.one[:], 1.0)
-    op("v", [o5], "tt", col(5), col(GF), col(YF), A.max)
-    op("v", [], "ts", col(6), col(EF), -1.0, 3.0, A.mult, A.add)
-    k1 = op("v", [], "ts", col(14), col(YF), -1.0, 1.0, A.mult, A.add)
-    k2 = op("v", [k1], "ts", col(7), col(5), 3.0, 1.0, A.mult, A.add)
-    k3 = op("v", [k2], "tt", col(8), col(6), col(7), A.mult)
-    q1 = op("s", [k3], "act", col(9), col(8), AF.Exp, scale=ln2)
-    q2 = op("s", [q1], "act", col(10), col(9), AF.Identity, bias=MAGIC)
-    op("v", [], "ts", col(12), col(GF), (ln2 - ln16) / 512.0, ln16 / 512.0, A.mult, A.add)
-    c5 = op("v", [], "ts", col(13), col(GF), b2 + ln16, -ln16, A.mult, A.add)
-    op("v", [], "ts", col(15), col(LF), 14.0, None, A.not_equal)
-    op("v", [], "ts", col(16), col(LF), 10.0, None, A.not_equal)
-    op("v", [], "ts", col(17), col(LF), 14.0, None, A.is_equal)
-    k4 = op("v", [], "ts", col(18), col(LF), 10.0, 17.0, A.is_equal, A.mult)
-    op("v", [k4], "tt", col(19), col(15), col(16), A.mult)
-    k5 = op("v", [], "tt", col(20), col(17), col(18), A.add)
-    k6 = op("v", [k5, gi3], "ts", cf[:, 32:40], ci[:, 32:40], col(19), col(20), A.mult, A.add)
-    k7 = op("v", [], "tt", col(21), col(GF), col(14), A.mult)
-    v_ul = op("v", [k6], "cp", T.uls[:], cf[:, 32:40])
-    k8 = op("v", [k7], "ts", col(22), col(21), 1.0 - 2.0 ** -15, 2.0 ** -15, A.mult, A.add)
-    g_eb = op("g", [v_one], "sel", T.eb[:], T.one[:], [[-1, 516]], A.is_equal, 0.0, 3, 4)
-    g_iw = op("g", [], "iota", T.iw[:], [[1, 320]], 0, 0, allow_small_or_imprecise_dtypes=True)
-    v64 = op("s", [g_eb], "act", T.eb64[:], T.eb[:], AF.Copy, scale=64.0)
-    op("v", [], "ms", T.kx[:, 0:120 * R:2], 4680.0 * 2.0 ** -15)
-    op("v", [], "ms", T.kx[:, 1:120 * R:2], 4680.0)
-    op("v", [], "ms", T.hb[:], 1)
-    g1 = op("v", [], "ms", T.sg[:], 1.0)
-    seg = op("v", [g1], "ms", T.sg[:, 0:100:5], 0.0)
-    k9 = op("v", [q2, k8], "ts", col(23), col(10), MAGIC, col(22), A.subtract, A.mult)
-    nt, ni, nf, tw = T.nt, T.ni, T.nf, T.tw
-    w1 = op("v", [done("ld_nx"), gn], "ts", nf[:, 0:640], nt[:], -159.5, BIG, A.add, A.add)
-    w2 = op("s", [w1], "act", nf[:, 640:1280], nf[:, 0:640], AF.Identity, bias=-BIG)
-    w3 = op("s", [w2, c5], "act", nf[:, 1280:1920], nf[:, 640:1280], AF.Exp, bias=col(13), scale=col(12))
-    w4 = op("s", [w3], "act", nf[:, 1920:2560], nf[:, 1280:1920], AF.Identity, bias=MAGIC)
-    op("v", [k9], "tt", col(24), col(23), col(YF), A.mult)
-    c8 = op("v", [], "tt", col(25), col(23), col(14), A.mult)
-    qu = op("v", [("ld_u", 16)], "qz", T.uq[:], T.up[:], T.ub[:])
-    op("v", [qu, v_ul], "cp", T.uq2[:].bitcast(dt.uint32), T.uq[:].bitcast(dt.uint32).indirect(T.uls[:]))
-    v_u = op("v", [], "cp", T.up2[:], T.up[:].indirect(T.uls[:]))
-    qx = [op("v", [("ld_x%d" % h, 16)], "qz", T.qx0[:, H * h:H * h + H], T.sx0[:, H * h:H * h + H], T.x0[:, 640 * h:640 * h + 640])
+    def line(k, src, a, b):
+        return op("s", [cols], "act", col(k), col(src), AF.Identity, scale=a, bias=b)
+    s_an = op("s", [cols, g_ia], "act", T.ia[:, 160:320], T.ia[:, 0:160], AF.Identity, bias=col(M4))
+    line(12, T8, -192.0, 575.0)
+    line(13, T8, 193.0, -381.0)
+    s1 = line(14, LANE, 16.0, -223.0)
+    line(UP0, ODD, 320.0, 0.0)
+    line(UP1, ODD, -320.0, 320.0)
+    line(ES, LANE, -2.0, 31.0)
+    s2 = line(KO, ODD, -SAME, SAME)
+    op("v", [cols], "ts", col(KL), col(R8), 0.0, None, A.is_equal)
+    op("v", [], "ts", col(15), col(LANE), 14.0, None, A.is_lt)
+    v_hn = op("v", [o], "ms", T.hn[:, 0:384:4], 0.0)
+    op("v", [], "ts", col(TH), col(LANE), 0.0, 1e29, A.is_equal, A.mult)
+    o = op("v", [s1], "ts", col(16), col(R8), 4.0, col(12), A.min, A.add)
+    v_ul = op("v", [g_rt, v_hn], "ts", T.uls[:], ci[:, 8:16], col(15), col(14), A.mult, A.max)
+    o = op("v", [o], "ts", col(17), col(13), col(KL), col(16), A.mult, A.add)
+    o = op("v", [o], "ts", col(18), col(KL), -194.0, col(17), A.mult, A.add)
+    op("v", [], "ts", T.rt[:, 0:24:2], ci[:, 16:28], col(17), None, A.add)
+    v_rt = op("v", [o], "ts", T.rt[:, 1:24:2], ci[:, 16:28], col(18), 16.0, A.add, A.add)
+
+    nt, ni, un, nf, ru, rw, tw = T.nt, T.ni, T.un, T.nf, T.ru, T.rw, T.tw
+    op("v", [ld_nx], "ts", ni[:, 0:160], nt[:], 1.0 / 512, 8.0 - 159.5 / 512, A.mult, A.add)
+    o = op("v", [], "ts", ni[:, 160:320], nt[:], 7, 28, A.arith_shift_right, A.bitwise_and)
+    n1 = op("v", [], "ts", ni[:, 320:480], nt[:], 511, None, A.bitwise_and)
+    o = op("v", [o], "tt", un[:, 0:160], ni[:, 0:160], ni[:, 160:320], A.max)
+    qu = op("v", [ld_u], "qz", T.uq[:], T.up[:], T.ub[:])
+    op("v", [o], "tp", ru[:, 0:96], un[:, 0:96])
+    t1 = op("v", [], "tp", ru[:, 96:192], un[:, 80:176])
+    o = op("s", [t1], "act", ru[:, 192:384], ru[:, 0:192], AF.Square, bias=-8.0)
+    u4 = op("s", [o], "act", ru[:, 384:576], ru[:, 192:384], AF.Square)
+    s_u = op("s", [qu, v_ul], "act", T.up2[:], T.up[:].indirect(T.uls[:]), AF.Copy)
+    n2 = op("v", [n1, s_an], "tt", nf[:, 0:160], ni[:, 320:480], T.ia[:, 160:320], A.subtract)
+    k1 = op("v", [t1, v_hn], "scan", rw[:, 0:192], T.hn[:, 0:192], ru[:, 0:192], 0.0, A.mult, A.add)
+    op("v", [n2], "tp", rw[:, 384:480], nf[:, 0:96])
+    n3 = op("v", [], "tp", rw[:, 480:576], nf[:, 80:176])
+    k2 = op("v", [u4], "scan", rw[:, 192:384], T.hn[:, 192:384], ru[:, 384:576], 0.0, A.mult, A.add)
+    op("v", [k1], "tt", rw[:, 0:96:4], rw[:, 99:192:4], rw[:, 3:96:4], A.subtract)
+    op("v", [], "ts", rw[:, 1:96:4], rw[:, 3:96:4], -8.0 * 4369, None, A.add)
+    op("v", [n3], "tt", rw[:, 576:672], rw[:, 480:576], rw[:, 384:480], A.subtract)
+    k3 = op("v", [k2], "tt", rw[:, 194:288:4], rw[:, 291:384:4], rw[:, 195:288:4], A.subtract)
+    k4 = op("s", [k3, v_rt], "act", T.gg[:], rw[:].indirect(T.rt[:]), AF.Copy)
+    v_u = [s_u, op("v", [qu, v_ul], "cp", T.uq2[:].bitcast(dt.uint32), T.uq[:].bitcast(dt.uint32).indirect(T.uls[:]))]
+    qx = [op("v", [ld_x[h]], "qz", T.qx0[:, H * h:H * h + H], T.sx0[:, H * h:H * h + H], T.x0[:, 640 * h:640 * h + 640])
           for h in range(2)]
 
     def send_codes(r, h, tok):
@@ -260,132 +248,121 @@ def rank_program(g, core, T, topo):
 
     def bits(r, h, kt):
         k, t = kt
-        o = op("v", [t], "ts", T["bw%d" % r][:, H * h:H * h + H], banks[k][:, 0:H], 0.0, None, A.is_gt)
+        o = op("v", [t], "ts", T["bw%d" % r][:, H * h:H * h + H], banks[k][:, 0:H], col(TH), None, A.is_gt)
         readers[k].append(o)
         return o
 
-    def unpack(r, h, tok, own=True):
-        ps = []
-        for b in range(4):
-            k = bank()
-            qc, qs = (T["qx%d" % r], T["sx%d" % r]) if own else (T["qp%d" % r], T["sp%d" % r])
-            ps.append((k, mm([tok, vE], k, H, T.ec, T.es, b, qc, qs, H * h)))
-        return ps
+    def unpack(qc, qs, toks):
+        ks = [bank() for b in range(4)]
+        return [(ks[b], mm([toks], ks[b], C, T.ec, T.es, b, qc, qs, 0)) for b in range(4)]
 
-    def unpack_copy(r, h, ps, own=True):
-        d = T["f%d" % r] if own else T["fp%d" % r]
+    def unpack_copy(d, ps):
         for b in range(4):
             k, t = ps[b]
-            o = op("s", [t], "act", d[:, 320 * b + H * h:320 * b + H * h + H], banks[k][:, 0:H], AF.Copy)
+            o = op("s", [t], "act", d[:, C * b:C * b + C], banks[k][:, 0:C], AF.Copy, scale=INV)
             readers[k].append(o)
         return o
 
     def edge_rows(r, h, tok):
-        return op("s", [tok, v_id], "act", T["er%d" % r][:, 320 * h:320 * h + 320],
-                  T["bw%d" % r][:, H * h:H * h + H].indirect(T.idl[:]), AF.Copy)
+        return op("s", [tok, v_id, s2], "act", T["er%d" % r][:, C * h:C * h + C],
+                  T["bw%d" % r][:, H * h:H * h + H].indirect(T.idl[:]), AF.Identity, scale=col(ES), bias=1.0)
+
+    def turn_half(dst, src, r, h, tok):
+        return op("v", [tok], "tp", T[dst + str(r)][:, C * h:C * h + C], T[src + str(r)][:, C * h:C * h + C])
+
+    def dup(dst, src, toks, h):
+        a = 20 * h
+        op("v", [toks, s2], "ts", dst[:, 60 + a:80 + a:2], src, col(UP0), None, A.add)
+        t = op("v", [], "ts", dst[:, 61 + a:80 + a:2], src, col(UP1), None, A.add)
+        op("v", [], "cp", dst[:, 20 + a:40 + a:2], src)
+        return t, op("v", [], "cp", dst[:, 21 + a:40 + a:2], src)
+
+    def table_lookup(r, h, e, tok):
+        out, win = T["tr%d" % r][:, C * h:C * h + C], tw[:].indirect(T["us%d" % r][:, 60 + 20 * h:80 + 20 * h])
+        return op("v", [tok, v_tw], "cp", out, win) if e == "v" else op("s", [tok, v_tw], "act", out, win, AF.Copy)
 
     sc = [scores(0, 0, qx[0]), scores(0, 1, qx[1])]
     send_codes(0, 0, qx[0])
     send_codes(0, 1, qx[1])
-    i1 = op("v", [g_id], "ts", ci[:, 40:60], ni[:, 0:20], col(LF), None, A.add)
-    n1 = op("v", [i1], "ts", ni[:], nt[:], 511, None, A.bitwise_and)
-    v_id = op("v", [i1], "cp", T.idl[:], ci[:, 40:60])
-    n2 = op("v", [n1], "tt", nf[:, 2560:2880], ni[:, 0:320], ni[:, 320:640], A.subtract)
-    w5 = op("v", [w4], "tt", nf[:, 3200:3520], nf[:, 1920:2240], nf[:, 2240:2560], A.subtract)
-    bt_ = [bits(0, 0, sc[0]), bits(0, 1, sc[1])]
-    n3 = op("s", [n2, c8], "act", nf[:, 2880:3200], nf[:, 2560:2880], AF.Copy, scale=col(24))
-    w6 = op("s", [w5, c8], "act", nf[:, 3520:3840], nf[:, 3200:3520], AF.Copy, scale=col(25))
+    g_iw = op("g", [], "iota", T.iw[:], [[1, 320]], 0, 0, **fl)
     l0 = T.l0
-    op("v", [], "ts", col(26), col(GF), -320.0, 320.0, A.mult, A.add)
-    c2 = op("v", [], "ts", col(27), col(GF), 320.0, None, A.mult)
-    v_l0 = op("v", [("ld_al", 16)], "cp", l0[:], T.ali[:])
-
-    def dup(dst, src, toks, h):
-        a = 20 * h
-        op("v", [toks, c2], "cp", dst[:, 20 + a:40 + a:2], src)
-        op("v", [], "cp", dst[:, 21 + a:40 + a:2], src)
-        op("v", [], "ts", dst[:, 60 + a:80 + a:2], src, col(27), None, A.add)
-        return op("v", [], "ts", dst[:, 61 + a:80 + a:2], src, col(26), None, A.add)
+    v_l0 = op("v", [ld_al], "cp", l0[:], T.ali[:])
+    k5 = op("v", [k4], "tp", T.g2[:], T.gg[:])
     lists = [dup(T.us0, l0[:, 10 * h:10 * h + 10], [v_l0], h) for h in range(2)]
-    c3 = op("v", [], "ts", col(11), col(GF), -4680.0 * 2.0 ** -15, 4680.0 * 2.0 ** -15, A.mult, A.add)
-    for q in range(4):
-        wl = op("v", [w6, n3], "tt", tw[:, q:320:4], nf[:, 2880 + 80 * q:2960 + 80 * q], nf[:, 3520 + 80 * q:3600 + 80 * q], A.add)
-    v_tw = op("s", [wl, k1], "act", tw[:, 320:640], tw[:, 0:320], AF.Copy, scale=col(14))
-    for b in range(4):
-        vE = op("v", [g_eb], "qz", T.ec[:, 128 * b:128 * b + 128], T.es[:, 128 * b:128 * b + 128], T.eb[:, 3 - b:515 - b])
-    pF = unpack(0, 0, qx[0])
-    tF = [None, None]
+    v_tw = []
+    for m in range(4):
+        v_tw.append(op("v", [k5], "cp", tw[:, m:320:4], T.g2[:, 96 * m:96 * m + 80]))
+        v_tw.append(op("s", [k5], "act", tw[:, 320 + m:640:4], T.g2[:, 96 * m:96 * m + 80], AF.Copy, scale=col(KL)))
+    v_id = op("v", [g_id], "ts", T.idl[:], ci[:, 28:48], col(LANE), None, A.add)
+    bt_ = [bits(0, 0, sc[0]), bits(0, 1, sc[1])]
+    trow = [table_lookup(0, 0, "s", lists[0][0]), table_lookup(0, 1, "v", lists[1][0])]
+    vE = []
 
-    def table_lookup(r, h, e, tok):
-        out, win = T["tr%d" % r][:, 320 * h:320 * h + 320], tw[:].indirect(T["us%d" % r][:, 60 + 20 * h:80 + 20 * h])
-        return op("v", [tok, v_tw], "cp", out, win) if e == "v" else op("s", [tok, v_tw], "act", out, win, AF.Copy)
+    def const_tile(b):
+        vE.append(op("v", [g_eb], "qz", T.ec[:, 128 * b:128 * b + 128], T.es[:, 128 * b:128 * b + 128], T.eb[:, 3 - b:515 - b]))
 
-    def table_turn(r, h, tok):
-        a, gt, fs = 320 * h, T["gt%d" % r], T["fs%d" % r]
-        t = op("v", [tok], "tp", gt[:, a:a + 320], T["tr%d" % r][:, a:a + 320])
-        x1, x2 = fs[:, 80 + 40 * h:120 + 40 * h], fs[:, 920 + 40 * h:960 + 40 * h]
-        op("v", [t], "tt", x1, gt[:, a:a + 320:8], gt[:, a + 2:a + 320:8], A.add)
-        p = op("v", [], "tt", x2, gt[:, a + 4:a + 320:8], gt[:, a + 6:a + 320:8], A.add)
-        return op("v", [p], "tt", fs[:, 40 * h:40 * h + 40], x1, x2, A.add)
-
-    trow = [table_lookup(0, 0, "s", lists[0]), table_lookup(0, 1, "v", lists[1])]
     for r in range(R):
         rn = r + 1
         us, fs, ints, bw = T["us%d" % r], T["fs%d" % r], T["is%d" % r], T["bw%d" % r]
-        br, btb, gt = T["br%d" % r], T["bt%d" % r], T["gt%d" % r]
-        kb, hh = 120 * r, 100 * r
+        br, btb, gt, et = T["br%d" % r], T["bt%d" % r], T["gt%d" % r], T["et%d" % r]
         cur = (l0[:, 0:10], l0[:, 10:20]) if r == 0 else (T["us%d" % (r - 1)][:, 0:10], T["ll%d" % (r - 1)][:])
-        p1 = op("v", [bt_, lists], "cp", br[:, 0:320], bw[:].indirect(us[:, 20:40]))
-        p2 = op("s", [bt_, lists], "act", br[:, 320:640], bw[:].indirect(us[:, 40:60]), AF.Copy)
+        p1 = op("v", [bt_, lists[0][1]], "cp", br[:, 0:320], bw[:].indirect(us[:, 20:40]))
+        p2 = op("s", [bt_, lists[1][1]], "act", br[:, 320:640], bw[:].indirect(us[:, 40:60]), AF.Copy)
         if r == 0:
+            tab = [turn_half("gt", "tr", 0, h, trow[h]) for h in (1, 0)]
             er = [edge_rows(0, 0, bt_[0]), None]
-            tab = [table_turn(0, h, trow[h]) for h in range(2)]
+            op("v", [], "ms", T.kx[:, 1:240:2], SAME)
         er[1] = edge_rows(r, 1, bt_[1])
         v_bt = op("v", [p1, p2], "tp", btb[:], br[:])
-        km = op("v", [v_bt, tab], "tt", fs[:, 160:200], fs[:, 1:80:2], btb[:, 0:640:16], A.mult)
-        ks = op("v", [km], "tt", fs[:, 200:240], fs[:, 160:200], fs[:, 0:80:2], A.add)
-        for d in (1, 2, 3):
-            dma("y", [ks], T.kx[32 * d:128, kb + 40 * (3 - d):kb + 40 * (4 - d)], fs[0:128 - 32 * d, 200:240], "kx%d" % r)
+        signs = btb[:, 0:640:8]
+        ks = op("v", [v_bt, tab], "scan", fs[:, 0:80], signs, gt[:, 0:640:8], 0.0, A.mult, A.add)
+        kd = [dma("y", [ks], T.kx[32 * d:128, 80 * (3 - d):80 * (4 - d)], fs[0:128 - 32 * d, 0:80], "kx%d" % (3 - d)) for d in (3, 2, 1)]
         if r == 0:
-            tF[0] = unpack_copy(0, 0, pF)
-        tF[1] = unpack_copy(r, 1, unpack(r, 1, qx[1]))
-        nm = [op("v", [v_bt], "tt", fs[:, 240 + 40 * e:280 + 40 * e], gt[:, 9 + 2 * e:640:16], btb[:, 0:640:16], A.mult) for e in range(4)]
-        ko = op("v", [ks, c3], "ts", fs[:, 860:880], fs[:, 200:240:2], col(GF), col(11), A.mult, A.add)
-        ns = [op("v", [nm[e]], "tt", fs[:, 400 + 40 * e:440 + 40 * e], fs[:, 240 + 40 * e:280 + 40 * e], gt[:, 1 + 2 * e:640:16], A.add)
-              for e in range(4)]
-        op("v", [], "cp", fs[:, 560:610:5], cur[0])
-        op("v", [], "cp", fs[:, 610:660:5], cur[1])
-        et = T["et%d" % r]
-        e1 = op("v", [er], "tp", et[:], T["er%d" % r][:])
-        de = [op("v", [ns[e]], "tt", fs[:, 561 + e:660:5], fs[:, 400 + 40 * e:440 + 40 * e:2], fs[:, 401 + 40 * e:440 + 40 * e:2], A.add)
-              for e in range(4)]
-        op("v", [e1], "ts", fs[:, 880:900], et[:, 14:640:32], 3.0, 1.0, A.mult, A.add)
-        e3 = op("v", [], "ts", fs[:, 900:920], et[:, 10:640:32], 32768.0, 32768.0, A.mult, A.add)
-        st = op("v", [e3], "tt", ints[:, 0:20], fs[:, 880:900], fs[:, 900:920], A.mult)
-        sv, at = ints[:, 0:20], 20
+            dma("y", [], T.wq[:].bitcast(dt.uint8), T.wc[:], "ld_w")
+            ld_w = dma("y", [], T.wp[:], T.ws[:], "ld_w")
+        if r == 1:
+            ld_v = dma("y", [], T.vb[:], T.v[:], "ld_v")
+        ns = [op("v", [], "scan", fs[:, 100 + 80 * e:180 + 80 * e], signs, gt[:, 1 + e:640:8], 0.0, A.mult, A.add) for e in range(4)]
+        if r == 0:
+            e0 = turn_half("et", "er", 0, 0, er[0])
+            g1 = op("v", [], "ms", T.sg[:], 1.0)
+            op("v", [], "ms", T.hb[:, 0:100:5], 1)
+        e1 = turn_half("et", "er", r, 1, er[1])
+        ko = op("v", [ks, s2], "ts", fs[:, 80:100], fs[:, 1:80:4], col(ODD), col(KO), A.mult, A.add)
+        if r == 0:
+            seg = op("v", [g1], "ms", T.sg[:, 0:100:5], 0.0)
+        st = op("v", [e0, e1], "tt", fs[:, 720:740], et[:, 14:640:32], et[:, 15:640:32], A.mult)
+        fill = [lambda e=e: op("v", [ns[e]], "tt", fs[:, 421 + e:520:5], fs[:, 101 + 80 * e:180 + 80 * e:4],
+                               fs[:, 103 + 80 * e:180 + 80 * e:4], A.add) for e in range(4)]
+        fill += [lambda: op("v", [], "cp", fs[:, 420:470:5], cur[0]), lambda: op("v", [], "cp", fs[:, 470:520:5], cur[1])]
+        if r == 0:
+            for b in range(4):
+                const_tile(b)
+        qa = [("qa%d%d" % (r, h), 3 * far_engines) for h in range(2)]
+        tF = unpack_copy(T["f%d" % r], unpack(T["qx%d" % r], T["sx%d" % r], [qx, vE]))
+        if r > 0:
+            tP = unpack_copy(T["fp%d" % r], unpack(T["qp%d" % r], T["sp%d" % r], [qa]))
+        sv, at, de = fs[:, 720:740], 0, []
         for j in range(6):
             tv = ints[:, at:at + 20]
-            a = kb + 40 * (j // 2) + j % 2
-            st = op("v", [st, done("kx%d" % r)], "tt", tv, T.kx[:, a:kb + 40 * (j // 2) + 40:2], sv, A.mult)
+            a = 80 * (j // 2) + 1 + 2 * (j % 2)
+            st = op("v", [st, kd[j // 2]], "tt", tv, T.kx[:, a:80 * (j // 2) + 80:4], sv, A.mult)
+            de.append(fill[j]())
             sv = ints[:, at + 20:at + 40]
-            st = op("v", [st], "ts", sv, tv, 0x78000 if j % 2 else 0x8888, None, A.bitwise_and)
+            st = op("v", [st], "ts", sv, tv, 15, 15, A.arith_shift_right, A.bitwise_and) if j % 2 else \
+                op("v", [st], "ts", sv, tv, 0x8888, None, A.bitwise_and)
             at += 40
         tv = ints[:, at:at + 20]
-        st = op("v", [st, ko], "tt", tv, fs[:, 860:880], sv, A.mult)
-        hs = [op("v", [st], "ts", T.hb[:, hh + 1 + e:hh + 100:5], tv, 1 << (4 * e + 3), None, A.bitwise_and) for e in range(4)]
-        st = op("v", [hs, de], "tt", fs[:, 660:760], T.hb[:, hh:hh + 100], fs[:, 560:660], A.mult)
-        st = op("v", [st, seg], "scan", fs[:, 760:860], T.sg[:], fs[:, 660:760], 0.0, A.mult, A.add)
-        lm = op("v", [st], "cp", us[:, 10:20], fs[:, 814:860:5])
+        st = op("v", [st, ko], "tt", tv, fs[:, 80:100], sv, A.mult)
+        hs = [op("v", [st], "ts", T.hb[:, 1 + e:100:5], tv, 4 * e + 3, 1, A.arith_shift_right, A.bitwise_and) for e in range(4)]
+        st = op("v", [hs, de], "tt", fs[:, 520:620], T.hb[:], fs[:, 420:520], A.mult)
+        st = op("v", [st, seg], "scan", fs[:, 620:720], T.sg[:], fs[:, 520:620], 0.0, A.mult, A.add)
+        lm = op("v", [st], "cp", us[:, 10:20], fs[:, 674:720:5])
         need("g", [lm])
         rid, pid = topo.addr(rel[0], core)
         g.remote_dma(T["rl%d" % r][:], us[:, 10:20], T.sem["rl%d" % r], T.sem.loc, pid, rid, topo.mask(core, rel[0]))
         loc[0] += len(topo.engines(core, rel[0]))
-        ls = op("v", [], "cp", us[:, 0:10], fs[:, 764:810:5])
-        qa = [("qa%d%d" % (r, h), 3 * far_engines) for h in range(2)]
-        tP = [unpack_copy(r, 0, unpack(r, 0, qa[0], own=False), own=False), None]
-        if r == 0:
-            for b in range(4):
-                v64q = op("v", [v64], "qz", T.e64c[:, 128 * b:128 * b + 128], T.e64s[:, 128 * b:128 * b + 128], T.eb64[:, 3 - b:515 - b])
+        ls = op("v", [], "cp", us[:, 0:10], fs[:, 624:670:5])
 
         def make(h, toks, off, F):
             z, q, s, o = T["z%d" % r], T["qz%d" % r], T["sz%d" % r], []
@@ -396,15 +373,15 @@ def rank_program(g, core, T, topo):
             ps = []
             for b in range(4):
                 k = bank()
-                mm([zq, ("ld_w", 32)], k, H, T.wq, T.wp, b, q, s, H * h, True, False)
-                ps.append((k, mm([zq, v64q], k, H, T.e64c, T.e64s, b, q, s, H * h, False, True)))
+                mm([zq, ld_w], k, H, T.wq, T.wp, b, q, s, H * h, True, False)
+                ps.append((k, mm([zq], k, H, T.ec, T.es, b, q, s, H * h, False, True)))
             return ps
 
         def renew(h, b, ps, e):
             k, t = ps[b]
             out = T["x%d" % rn][:, 640 * h + b:640 * h + 640:4]
-            o = op("v", [t], "ts", out, banks[k][:, 0:H], 0.015625, None, A.mult) if e == "v" else \
-                op("s", [t], "act", out, banks[k][:, 0:H], AF.Copy, scale=0.015625)
+            o = op("v", [t], "ts", out, banks[k][:, 0:H], INV, None, A.mult) if e == "v" else \
+                op("s", [t], "act", out, banks[k][:, 0:H], AF.Copy, scale=INV)
             readers[k].append(o)
             return o
 
@@ -422,41 +399,45 @@ def rank_program(g, core, T, topo):
             readers[k].append(o)
             dma(ea, [o], T.y[:, H * h:H * h + H], T.yb[:, H * h:H * h + H], "outs")
 
+        land, la = T["ll%d" % r], ("la%d" % r, far_engines)
         ps = make(0, [ls, tF], us[:, 0:10], T["f%d" % r])
         if rn < R:
             lists = [dup(T["us%d" % rn], us[:, 0:10], [ls], 0), None]
+            t0 = table_lookup(rn, 0, "s", lists[0][0])
         else:
-            vv = op("v", [("ld_v", 16)], "qz", T.vq[:], T.vp[:], T.vb[:])
-        o = [renew(0, b, ps, "v" if b % 2 else "s") for b in range(4)]
-        tP[1] = unpack_copy(r, 1, unpack(r, 1, qa[1], own=False), own=False)
+            vv = op("v", [ld_v], "qz", T.vq[:], T.vp[:], T.vb[:])
+            oa1 = op("s", [ls, g_iw], "act", T.orow[:, 0:H], T.iw[:].indirect(us[:, 0:10]), AF.Copy)
+        if r == 0:
+            pP = unpack(T.qp0, T.sp0, [qa])
+        o = [renew(0, b, ps, "s" if b == 3 else "v") for b in range(4)]
+        if r == 0:
+            tP = unpack_copy(T.fp0, pP)
         qx = [requant(0, o), None]
-        land, la = T["ll%d" % r], ("la%d" % r, far_engines)
         if rn < R:
             s0 = scores(rn, 0, qx[0])
-            p0 = unpack(rn, 0, qx[0])
             send_codes(rn, 0, qx[0])
-            t0 = table_lookup(rn, 0, "s", lists[0])
-            tF = [unpack_copy(rn, 0, p0), None]
+            tab = [turn_half("gt", "tr", rn, 0, t0), None]
             bt_ = [bits(rn, 0, s0), None]
-            tab = [table_turn(rn, 0, t0), None]
             er = [edge_rows(rn, 0, bt_[0]), None]
         else:
-            oa1 = op("s", [ls, g_iw], "act", T.orow[:, 0:H], T.iw[:].indirect(us[:, 0:10]), AF.Copy)
             outputs(0, qx[0], "y", "y")
         ps = make(1, [la, tP], land[:], T["fp%d" % r])
         if rn < R:
             lists[1] = dup(T["us%d" % rn], land[:], [la], 1)
-            tab[1] = table_turn(rn, 1, table_lookup(rn, 1, "v", lists[1]))
+            tab[1] = turn_half("gt", "tr", rn, 1, table_lookup(rn, 1, "v", lists[1][0]))
+            o = [renew(1, b, ps, "s") for b in range(4)]
         else:
             oa2 = op("v", [la, g_iw], "cp", T.orow[:, H:C], T.iw[:].indirect(land[:]))
             dma("y", [oa1, oa2], T.oa[:], T.orow[0:128:16, :], "outs")
-        o = [renew(1, b, ps, "s") for b in range(4)]
+            o = [renew(1, b, ps, "v" if b % 2 else "s") for b in range(4)]
         qx[1] = requant(1, o)
         if rn < R:
             send_codes(rn, 1, qx[1])
-            bt_[1] = bits(rn, 1, scores(rn, 1, qx[1]))
+            s1 = scores(rn, 1, qx[1])
+            e0 = turn_half("et", "er", rn, 0, er[0])
+            bt_[1] = bits(rn, 1, s1)
         else:
             outputs(1, qx[1], "y", "s")
-    need("g", [("loc", loc[0]), done("outs")])
+    need("g", [("loc", loc[0]), ("outs", dma_n["outs"])])
     for e in ("v", "s", "t", "g"):
         need("g", [(e + "q", cnt[e])])

@@ -17,12 +17,12 @@ def _scratch():
     sb("ub", 512, BF); sb("uq", 128, MX); sb("up", 128, U8); sb("uq2", 128, MX); sb("up2", 128, U8)
     sb("vb", 512, BF); sb("vq", 128, MX); sb("vp", 128, U8)
     sb("wq", 512, MX); sb("wp", 512, U8)
-    sb("c64", 516, BF); sb("eb", 516, BF); sb("ec", 512, MX); sb("es", 512, U8)
-    sb("ci", 64, I32); sb("cf", 64, F32); sb("uls", 8, U16); sb("sg", 100, F32); sb("idl", 20, U16); sb("rt", 24, U16)
-    sb("ali", 20, I32); sb("l0", 20, U16)
-    sb("nt", 160, I32); sb("ni", 480, I32); sb("ia", 320, F32); sb("un", 176, F32); sb("nf", 176, F32); sb("hn", 384, BF)
-    sb("ru", 576, F32); sb("rw", 672, F32); sb("gg", 384, F32); sb("g2", 384, F32); sb("tw", 640, F32)
-    sb("iw", 320, F32); sb("orow", 320, F32); sb("yb", 320, F32); sb("kx", 240, F32); sb("hb", 100, I32)
+    sb("c64", 192, BF); sb("eb", 516, BF); sb("ec", 512, MX); sb("es", 512, U8)
+    sb("ci", 64, I32); sb("cf", 64, F32); sb("uls", 8, U16); sb("sg", 500, F32); sb("idl", 20, U16); sb("rt", 24, U16)
+    sb("ali", 20, I32)
+    sb("nt", 160, I32); sb("ni", 480, I32); sb("un", 176, F32); sb("nf", 176, F32); sb("hn", 384, BF)
+    sb("ru", 576, F32); sb("rw", 672, F32); sb("gg", 384, F32); sb("tw", 704, F32)
+    sb("iw", 320, F32); sb("orow", 320, F32); sb("yb", 320, F32); sb("kx", 240, F32)
     for r in range(R + 1):
         sb("x%d" % r, 1280, BF); sb("qx%d" % r, 320, MX); sb("sx%d" % r, 320, U8)
     for r in range(R):
@@ -34,7 +34,7 @@ def _scratch():
         sb("bw%d" % r, 320, BF); sb("br%d" % r, 640, BF); sb("bt%d" % r, 640, BF)
         sb("er%d" % r, 640, BF); sb("et%d" % r, 640, BF)
         sb("tr%d" % r, 640, F32); sb("gt%d" % r, 640, F32)
-        sb("fs%d" % r, 740, F32); sb("is%d" % r, 260, I32)
+        sb("fs%d" % r, 1240, F32); sb("is%d" % r, 340, I32)
         sb("us%d" % r, 100, U16)
     return s
 
@@ -157,61 +157,82 @@ def rank_program(g, core, T, topo):
         return cf[:, k:k + 1]
 
     ld_nx = dma("y", [], T.nt[:], T.nx[:], "ld_nx")
-    ld_u = dma("s", [], T.ub[:], T.u[:], "ld_u")
-    ld_x = [dma("y", [], T.x0[:, 640 * h:640 * h + 640], T.x[:, 640 * h:640 * h + 640], "ld_x%d" % h) for h in range(2)]
     ld_al = dma("s", [], T.ali[:], T.al[:], "ld_al")
+    ld_u = dma("y", [], T.ub[:], T.u[:], "ld_u")
+    ld_x = [dma("y", [], T.x0[:, 640 * h:640 * h + 640], T.x[:, 640 * h:640 * h + 640], "ld_x%d" % h) for h in range(2)]
 
     fl = {"allow_small_or_imprecise_dtypes": True}
     v_c64 = op("v", [], "ms", T.c64[:], 64.0)
+    v_eb = op("v", [], "ms", T.eb[:], 0.0)
     g_p = op("g", [], "iota", icol(0), [[0, 1]], 0, 1)
-    g_ia = op("g", [], "iota", T.ia[:, 0:160], [[0, 2], [4, 80]], 0, 0, **fl)
-    op("g", [], "iota", ci[:, 8:16], [[16, 8]], 0, 0)
+    g_eb = op("g", [v_eb], "sel", T.eb[:, 3:515:4], T.c64[:, 0:128], [[-1, 128]], A.is_equal, 0.0, 0, 1)
+    g_ul = op("g", [], "iota", ci[:, 8:16], [[16, 8]], 0, 0)
     g_rt = op("g", [], "iota", ci[:, 16:28], [[4, 4], [32, 3]], 0, 0)
     g_id = op("g", [], "iota", ci[:, 28:48], [[16, 10], [0, 2]], 0, 0)
-    g_eb = op("g", [v_c64], "sel", T.eb[:], T.c64[:], [[-1, 516]], A.is_equal, 0.0, 3, 4)
-    LANE, ODD, M4, R8, T8 = 1, 2, 3, 4, 5
-    op("v", [], "ms", T.un[:, 160:176], 8.0)
-    op("v", [], "ms", T.nf[:, 160:176], 0.0)
-    for k, (sh, m) in enumerate([(0, 15), (4, 1), (2, 3), (0, 7), (3, 1)]):
+    LANE, ODD, R8, T8 = 1, 2, 3, 4
+    for k, (sh, m) in enumerate([(0, 15), (4, 1), (0, 7), (3, 1)]):
         o = op("v", [g_p], "ts", icol(1 + k), icol(0), sh, m, A.arith_shift_right, A.bitwise_and)
-    cols = op("v", [o], "cp", cf[:, 1:6], ci[:, 1:6])
-    op("v", [], "ms", T.hn[:, 0:192], 16.0)
-    o = op("v", [], "ms", T.hn[:, 192:384], 2.0)
+    cols = op("v", [o], "cp", cf[:, 1:5], ci[:, 1:5])
     KL, UP0, UP1, ES, KO, TH = 6, 7, 8, 9, 10, 11
+
+    def fill_s(out, n, c, toks=()):
+        return op("s", [v_c64, list(toks)], "act", out, T.c64[:, 0:n], AF.Copy, scale=c / 64.0)
 
     def line(k, src, a, b):
         return op("s", [cols], "act", col(k), col(src), AF.Identity, scale=a, bias=b)
-    s_an = op("s", [cols, g_ia], "act", T.ia[:, 160:320], T.ia[:, 0:160], AF.Identity, bias=col(M4))
+    fill_s(T.hn[:, 0:192], 192, 16.0)
+    o = fill_s(T.hn[:, 192:384], 192, 2.0)
+    fill_s(T.un[:, 160:176], 16, 8.0)
     line(12, T8, -192.0, 575.0)
     line(13, T8, 193.0, -381.0)
     s1 = line(14, LANE, 16.0, -223.0)
-    line(UP0, ODD, 320.0, 0.0)
-    line(UP1, ODD, -320.0, 320.0)
+    line(UP0, ODD, 384.0, 0.0)
+    line(UP1, ODD, -384.0, 384.0)
     line(ES, LANE, -2.0, 31.0)
     s2 = line(KO, ODD, -SAME, SAME)
+    fill_s(T.nf[:, 160:176], 16, 0.0)
+    v_hn = fill_s(T.hn[:, 0:384:4], 96, 0.0, [o])
+    fill_s(T.kx[:, 1:240:2], 120, SAME)
+    seg = fill_s(T.sg[:, 0:500:5], 100, 0.0)
     op("v", [cols], "ts", col(KL), col(R8), 0.0, None, A.is_equal)
     op("v", [], "ts", col(15), col(LANE), 14.0, None, A.is_lt)
-    v_hn = op("v", [o], "ms", T.hn[:, 0:384:4], 0.0)
     op("v", [], "ts", col(TH), col(LANE), 0.0, 1e29, A.is_equal, A.mult)
+
+    def const_tile(b):
+        return op("v", [g_eb], "qz", T.ec[:, 128 * b:128 * b + 128], T.es[:, 128 * b:128 * b + 128], T.eb[:, 3 - b:515 - b])
+    const_tile(0)
     o = op("v", [s1], "ts", col(16), col(R8), 4.0, col(12), A.min, A.add)
-    v_ul = op("v", [g_rt, v_hn], "ts", T.uls[:], ci[:, 8:16], col(15), col(14), A.mult, A.max)
+    const_tile(1)
     o = op("v", [o], "ts", col(17), col(13), col(KL), col(16), A.mult, A.add)
-    o = op("v", [o], "ts", col(18), col(KL), -194.0, col(17), A.mult, A.add)
-    op("v", [], "ts", T.rt[:, 0:24:2], ci[:, 16:28], col(17), None, A.add)
-    v_rt = op("v", [o], "ts", T.rt[:, 1:24:2], ci[:, 16:28], col(18), 16.0, A.add, A.add)
+    const_tile(2)
+    c18 = op("v", [o], "ts", col(18), col(KL), -194.0, col(17), A.mult, A.add)
+
+    def dup(dst, src, toks, h, n=20):
+        a = 20 * h
+        op("v", [toks, s2], "ts", dst[:, 60 + a:60 + a + n:2], src, col(UP0), None, A.add)
+        t = op("v", [], "ts", dst[:, 61 + a:60 + a + n:2], src, col(UP1), None, A.add)
+        op("v", [], "cp", dst[:, 20 + a:20 + a + n:2], src)
+        return t, op("v", [], "cp", dst[:, 21 + a:20 + a + n:2], src)
+
+    vE = const_tile(3)
+    v_ul = op("v", [g_ul], "ts", T.uls[:], ci[:, 8:16], col(15), col(14), A.mult, A.max)
+    op("v", [g_rt, c18], "ts", T.rt[:, 0:24:2], ci[:, 16:28], col(17), None, A.add)
+    v_rt = op("v", [], "ts", T.rt[:, 1:24:2], ci[:, 16:28], col(18), 16.0, A.add, A.add)
+    v_id = op("v", [g_id], "ts", T.idl[:], ci[:, 28:48], col(LANE), None, A.add)
+    lists = [dup(T.us0, T.ali[:], [ld_al], 0, 40)] * 2
 
     nt, ni, un, nf, ru, rw, tw = T.nt, T.ni, T.un, T.nf, T.ru, T.rw, T.tw
     op("v", [ld_nx], "ts", ni[:, 0:160], nt[:], 1.0 / 512, 8.0 - 159.5 / 512, A.mult, A.add)
     o = op("v", [], "ts", ni[:, 160:320], nt[:], 7, 28, A.arith_shift_right, A.bitwise_and)
     n1 = op("v", [], "ts", ni[:, 320:480], nt[:], 511, None, A.bitwise_and)
     o = op("v", [o], "tt", un[:, 0:160], ni[:, 0:160], ni[:, 160:320], A.max)
-    qu = op("v", [ld_u], "qz", T.uq[:], T.up[:], T.ub[:])
-    op("v", [o], "tp", ru[:, 0:96], un[:, 0:96])
+    n2 = op("v", [n1], "cp", nf[:, 0:160], ni[:, 320:480])
+    op("v", [o, v_hn], "tp", ru[:, 0:96], un[:, 0:96])
     t1 = op("v", [], "tp", ru[:, 96:192], un[:, 80:176])
     o = op("s", [t1], "act", ru[:, 192:384], ru[:, 0:192], AF.Square, bias=-8.0)
     u4 = op("s", [o], "act", ru[:, 384:576], ru[:, 192:384], AF.Square)
+    qu = op("v", [ld_u], "qz", T.uq[:], T.up[:], T.ub[:])
     s_u = op("s", [qu, v_ul], "act", T.up2[:], T.up[:].indirect(T.uls[:]), AF.Copy)
-    n2 = op("v", [n1, s_an], "tt", nf[:, 0:160], ni[:, 320:480], T.ia[:, 160:320], A.subtract)
     k1 = op("v", [t1, v_hn], "scan", rw[:, 0:192], T.hn[:, 0:192], ru[:, 0:192], 0.0, A.mult, A.add)
     op("v", [n2], "tp", rw[:, 384:480], nf[:, 0:96])
     n3 = op("v", [], "tp", rw[:, 480:576], nf[:, 80:176])
@@ -252,14 +273,14 @@ def rank_program(g, core, T, topo):
         readers[k].append(o)
         return o
 
-    def unpack(qc, qs, toks):
+    def unpack(qc, qs, toks, a=0, n=C):
         ks = [bank() for b in range(4)]
-        return [(ks[b], mm([toks], ks[b], C, T.ec, T.es, b, qc, qs, 0)) for b in range(4)]
+        return [(ks[b], mm([toks], ks[b], n, T.ec, T.es, b, qc, qs, a)) for b in range(4)]
 
-    def unpack_copy(d, ps):
+    def unpack_copy(d, ps, a=0, n=C):
         for b in range(4):
             k, t = ps[b]
-            o = op("s", [t], "act", d[:, C * b:C * b + C], banks[k][:, 0:C], AF.Copy, scale=INV)
+            o = op("s", [t], "act", d[:, C * b + a:C * b + a + n], banks[k][:, 0:n], AF.Copy, scale=INV)
             readers[k].append(o)
         return o
 
@@ -270,105 +291,103 @@ def rank_program(g, core, T, topo):
     def turn_half(dst, src, r, h, tok):
         return op("v", [tok], "tp", T[dst + str(r)][:, C * h:C * h + C], T[src + str(r)][:, C * h:C * h + C])
 
-    def dup(dst, src, toks, h):
-        a = 20 * h
-        op("v", [toks, s2], "ts", dst[:, 60 + a:80 + a:2], src, col(UP0), None, A.add)
-        t = op("v", [], "ts", dst[:, 61 + a:80 + a:2], src, col(UP1), None, A.add)
-        op("v", [], "cp", dst[:, 20 + a:40 + a:2], src)
-        return t, op("v", [], "cp", dst[:, 21 + a:40 + a:2], src)
-
     def table_lookup(r, h, e, tok):
         out, win = T["tr%d" % r][:, C * h:C * h + C], tw[:].indirect(T["us%d" % r][:, 60 + 20 * h:80 + 20 * h])
         return op("v", [tok, v_tw], "cp", out, win) if e == "v" else op("s", [tok, v_tw], "act", out, win, AF.Copy)
+
+    def signs_by_list(r, h):
+        out, win = T["br%d" % r][:, C * h:C * h + C], T["bw%d" % r][:].indirect(T["us%d" % r][:, 20 + 20 * h:40 + 20 * h])
+        return op("s", [bt_, lists[1][1]], "act", out, win, AF.Copy) if h else op("v", [bt_, lists[0][1]], "cp", out, win)
 
     sc = [scores(0, 0, qx[0]), scores(0, 1, qx[1])]
     send_codes(0, 0, qx[0])
     send_codes(0, 1, qx[1])
     g_iw = op("g", [], "iota", T.iw[:], [[1, 320]], 0, 0, **fl)
-    l0 = T.l0
-    v_l0 = op("v", [ld_al], "cp", l0[:], T.ali[:])
-    k5 = op("v", [k4], "tp", T.g2[:], T.gg[:])
-    lists = [dup(T.us0, l0[:, 10 * h:10 * h + 10], [v_l0], h) for h in range(2)]
-    v_tw = []
+    bt_ = [bits(0, 0, sc[0]), None]
     for m in range(4):
-        v_tw.append(op("v", [k5], "cp", tw[:, m:320:4], T.g2[:, 96 * m:96 * m + 80]))
-        v_tw.append(op("s", [k5], "act", tw[:, 320 + m:640:4], T.g2[:, 96 * m:96 * m + 80], AF.Copy, scale=col(KL)))
-    v_id = op("v", [g_id], "ts", T.idl[:], ci[:, 28:48], col(LANE), None, A.add)
-    bt_ = [bits(0, 0, sc[0]), bits(0, 1, sc[1])]
-    trow = [table_lookup(0, 0, "s", lists[0][0]), table_lookup(0, 1, "v", lists[1][0])]
-    vE = []
-
-    def const_tile(b):
-        vE.append(op("v", [g_eb], "qz", T.ec[:, 128 * b:128 * b + 128], T.es[:, 128 * b:128 * b + 128], T.eb[:, 3 - b:515 - b]))
+        k5 = op("v", [k4], "tp", tw[:, m:384:4], T.gg[:, 96 * m:96 * m + 96])
+    bt_[1] = bits(0, 1, sc[1])
+    v_tw = op("s", [k5], "act", tw[:, 384:704], tw[:, 0:320], AF.Copy, scale=col(KL))
+    trow = [table_lookup(0, 0, "s", lists[0][0]), None]
+    p2 = signs_by_list(0, 1)
 
     for r in range(R):
         rn = r + 1
-        us, fs, ints, bw = T["us%d" % r], T["fs%d" % r], T["is%d" % r], T["bw%d" % r]
+        us, fs, ints = T["us%d" % r], T["fs%d" % r], T["is%d" % r]
         br, btb, gt, et = T["br%d" % r], T["bt%d" % r], T["gt%d" % r], T["et%d" % r]
-        cur = (l0[:, 0:10], l0[:, 10:20]) if r == 0 else (T["us%d" % (r - 1)][:, 0:10], T["ll%d" % (r - 1)][:])
-        p1 = op("v", [bt_, lists[0][1]], "cp", br[:, 0:320], bw[:].indirect(us[:, 20:40]))
-        p2 = op("s", [bt_, lists[1][1]], "act", br[:, 320:640], bw[:].indirect(us[:, 40:60]), AF.Copy)
+        cur = (T.ali[:, 0:10], T.ali[:, 10:20]) if r == 0 else (T["us%d" % (r - 1)][:, 0:10], T["ll%d" % (r - 1)][:])
+        p1 = signs_by_list(r, 0)
         if r == 0:
-            tab = [turn_half("gt", "tr", 0, h, trow[h]) for h in (1, 0)]
+            trow[1] = table_lookup(0, 1, "v", lists[1][0])
+            tab = [turn_half("gt", "tr", 0, 0, trow[0]), turn_half("gt", "tr", 0, 1, trow[1])]
             er = [edge_rows(0, 0, bt_[0]), None]
-            op("v", [], "ms", T.kx[:, 1:240:2], SAME)
-        er[1] = edge_rows(r, 1, bt_[1])
+        else:
+            p2 = signs_by_list(r, 1)
         v_bt = op("v", [p1, p2], "tp", btb[:], br[:])
+        er[1] = edge_rows(r, 1, bt_[1])
         signs = btb[:, 0:640:8]
         ks = op("v", [v_bt, tab], "scan", fs[:, 0:80], signs, gt[:, 0:640:8], 0.0, A.mult, A.add)
-        kd = [dma("y", [ks], T.kx[32 * d:128, 80 * (3 - d):80 * (4 - d)], fs[0:128 - 32 * d, 0:80], "kx%d" % (3 - d)) for d in (3, 2, 1)]
+        kd = [dma("y", [ks, seg], T.kx[32 * d:128, 80 * (3 - d):80 * (4 - d)], fs[0:128 - 32 * d, 0:80], "kx%d" % (3 - d))
+              for d in (3, 2, 1)]
         if r == 0:
             dma("y", [], T.wq[:].bitcast(dt.uint8), T.wc[:], "ld_w")
             ld_w = dma("y", [], T.wp[:], T.ws[:], "ld_w")
         if r == 1:
             ld_v = dma("y", [], T.vb[:], T.v[:], "ld_v")
+        dv, dw, sg = fs[:, 420:520], fs[:, 620:720], T.sg
         ns = [op("v", [], "scan", fs[:, 100 + 80 * e:180 + 80 * e], signs, gt[:, 1 + e:640:8], 0.0, A.mult, A.add) for e in range(4)]
+        ko = op("v", [ks, s2], "ts", ints[:, 240:260], fs[:, 1:80:4], col(ODD), col(KO), A.mult, A.add)
+        for d in (420, 620):
+            for h in range(2):
+                old = op("v", [], "cp", fs[:, d + 4 + 50 * h:d + 50 + 50 * h:5], cur[h])
         if r == 0:
             e0 = turn_half("et", "er", 0, 0, er[0])
-            g1 = op("v", [], "ms", T.sg[:], 1.0)
-            op("v", [], "ms", T.hb[:, 0:100:5], 1)
+        far = [fs[:, 520 + 20 * e:540 + 20 * e] for e in range(4)] + [fs[:, 424:520:5]]
+        de = [op("v", [ns[e]], "tt", far[e], fs[:, 101 + 80 * e:180 + 80 * e:4], fs[:, 103 + 80 * e:180 + 80 * e:4], A.add)
+              for e in range(4)]
         e1 = turn_half("et", "er", r, 1, er[1])
-        ko = op("v", [ks, s2], "ts", fs[:, 80:100], fs[:, 1:80:4], col(ODD), col(KO), A.mult, A.add)
-        if r == 0:
-            seg = op("v", [g1], "ms", T.sg[:, 0:100:5], 0.0)
+        m4 = [op("v", [ko], "ts", ints[:, 260 + 20 * e:280 + 20 * e], ints[:, 240:260], 3 - e, 0x1111, A.arith_shift_right, A.bitwise_and)
+              for e in range(4)]
         st = op("v", [e0, e1], "tt", fs[:, 720:740], et[:, 14:640:32], et[:, 15:640:32], A.mult)
-        fill = [lambda e=e: op("v", [ns[e]], "tt", fs[:, 421 + e:520:5], fs[:, 101 + 80 * e:180 + 80 * e:4],
-                               fs[:, 103 + 80 * e:180 + 80 * e:4], A.add) for e in range(4)]
-        fill += [lambda: op("v", [], "cp", fs[:, 420:470:5], cur[0]), lambda: op("v", [], "cp", fs[:, 470:520:5], cur[1])]
-        if r == 0:
-            for b in range(4):
-                const_tile(b)
+        dd = [op("v", [de, old], "tt", fs[:, 420 + e:520:5], far[e], far[e + 1], A.subtract) for e in range(4)]
+        got = [fs[:, 744 + 100 * e:840 + 100 * e:5] for e in range(4)] + [fs[:, 624:720:5]]
+        f4, pk = [], []
+        fill = [lambda e=e: f4.append(op("v", [m4], "ts", sg[:, 100 + e:500:5], ints[:, 260:340], float(16 ** e) if e < 4 else 0.0,
+                                         None, A.not_equal)) for e in range(1, 5)]
+        fill += [lambda e=e: pk.append(op("v", [f4, dd, seg], "scan", fs[:, 740 + 100 * e:840 + 100 * e],
+                                          sg[:, 100 + 100 * e:200 + 100 * e], dv, 0.0, A.mult, A.add)) for e in range(4)]
+        fill += [lambda e=e: pk.append(op("v", [pk[:e + 2]], "tt", fs[:, 620 + e:720:5], got[e], got[e + 1], A.subtract))
+                 for e in range(4)]
         qa = [("qa%d%d" % (r, h), 3 * far_engines) for h in range(2)]
         tF = unpack_copy(T["f%d" % r], unpack(T["qx%d" % r], T["sx%d" % r], [qx, vE]))
         if r > 0:
-            tP = unpack_copy(T["fp%d" % r], unpack(T["qp%d" % r], T["sp%d" % r], [qa]))
-        sv, at, de = fs[:, 720:740], 0, []
+            unpack_copy(T["fp%d" % r], unpack(T["qp%d" % r], T["sp%d" % r], [qa[0]], 0, H), 0, H)
+        sv, at = fs[:, 720:740], 0
         for j in range(6):
             tv = ints[:, at:at + 20]
             a = 80 * (j // 2) + 1 + 2 * (j % 2)
             st = op("v", [st, kd[j // 2]], "tt", tv, T.kx[:, a:80 * (j // 2) + 80:4], sv, A.mult)
-            de.append(fill[j]())
+            fill[2 * j]()
             sv = ints[:, at + 20:at + 40]
             st = op("v", [st], "ts", sv, tv, 15, 15, A.arith_shift_right, A.bitwise_and) if j % 2 else \
                 op("v", [st], "ts", sv, tv, 0x8888, None, A.bitwise_and)
+            fill[2 * j + 1]()
             at += 40
-        tv = ints[:, at:at + 20]
-        st = op("v", [st, ko], "tt", tv, fs[:, 80:100], sv, A.mult)
-        hs = [op("v", [st], "ts", T.hb[:, 1 + e:100:5], tv, 4 * e + 3, 1, A.arith_shift_right, A.bitwise_and) for e in range(4)]
-        st = op("v", [hs, de], "tt", fs[:, 520:620], T.hb[:], fs[:, 420:520], A.mult)
-        st = op("v", [st, seg], "scan", fs[:, 620:720], T.sg[:], fs[:, 520:620], 0.0, A.mult, A.add)
-        lm = op("v", [st], "cp", us[:, 10:20], fs[:, 674:720:5])
-        need("g", [lm])
+        hs = [op("v", [st], "ts", sg[:, e:100:5], sv, float(2 ** e) if e < 4 else 0.0, None, A.not_equal) for e in range(1, 5)]
+        st = op("v", [hs, pk], "scan", fs[:, 1140:1240], sg[:, 0:100], dw, 0.0, A.mult, A.add)
+        ls = op("v", [st], "cp", us[:, 0:20], fs[:, 1144:1240:5])
+        need("g", [ls])
         rid, pid = topo.addr(rel[0], core)
         g.remote_dma(T["rl%d" % r][:], us[:, 10:20], T.sem["rl%d" % r], T.sem.loc, pid, rid, topo.mask(core, rel[0]))
         loc[0] += len(topo.engines(core, rel[0]))
-        ls = op("v", [], "cp", us[:, 0:10], fs[:, 624:670:5])
 
-        def make(h, toks, off, F):
+        def make(h, toks, off, F, between=None):
             z, q, s, o = T["z%d" % r], T["qz%d" % r], T["sz%d" % r], []
             for b in range(4):
                 win, out = F[:, 320 * b:320 * b + 320].indirect(off), z[:, 640 * h + b:640 * h + 640:4]
                 o.append(op("v", [toks], "cp", out, win) if b < 2 else op("s", [toks], "act", out, win, AF.Copy))
+            if between:
+                between()
             zq = op("v", [o], "qz", q[:, H * h:H * h + H], s[:, H * h:H * h + H], z[:, 640 * h:640 * h + 640])
             ps = []
             for b in range(4):
@@ -395,9 +414,12 @@ def rank_program(g, core, T, topo):
             dma(ea, [tok], T.oc[:, 640 * h:640 * h + 640], T["qx%d" % rn][:, H * h:H * h + H].bitcast(dt.uint8), "outs")
             for i in range(4):
                 dma(eb if i % 2 else ea, [tok], T.osc[4 * i:4 * i + 4, H * h:H * h + H], T["sx%d" % rn][32 * i:32 * i + 4, H * h:H * h + H], "outs")
-            o = op("v", [t], "cp", T.yb[:, H * h:H * h + H], banks[k][:, 0:H])
-            readers[k].append(o)
-            dma(ea, [o], T.y[:, H * h:H * h + H], T.yb[:, H * h:H * h + H], "outs")
+
+            def store_y():
+                o = op("v", [t], "cp", T.yb[:, H * h:H * h + H], banks[k][:, 0:H])
+                readers[k].append(o)
+                dma(ea, [o], T.y[:, H * h:H * h + H], T.yb[:, H * h:H * h + H], "outs")
+            return store_y
 
         land, la = T["ll%d" % r], ("la%d" % r, far_engines)
         ps = make(0, [ls, tF], us[:, 0:10], T["f%d" % r])
@@ -407,21 +429,22 @@ def rank_program(g, core, T, topo):
         else:
             vv = op("v", [ld_v], "qz", T.vq[:], T.vp[:], T.vb[:])
             oa1 = op("s", [ls, g_iw], "act", T.orow[:, 0:H], T.iw[:].indirect(us[:, 0:10]), AF.Copy)
-        if r == 0:
-            pP = unpack(T.qp0, T.sp0, [qa])
+        late = (H, H) if r else (0, C)
+        pP = unpack(T["qp%d" % r], T["sp%d" % r], [qa], *late)
         o = [renew(0, b, ps, "s" if b == 3 else "v") for b in range(4)]
-        if r == 0:
-            tP = unpack_copy(T.fp0, pP)
+        tP = unpack_copy(T["fp%d" % r], pP, *late)
         qx = [requant(0, o), None]
         if rn < R:
             s0 = scores(rn, 0, qx[0])
             send_codes(rn, 0, qx[0])
             tab = [turn_half("gt", "tr", rn, 0, t0), None]
-            bt_ = [bits(rn, 0, s0), None]
-            er = [edge_rows(rn, 0, bt_[0]), None]
+
+            def behind():
+                bt_[0] = bits(rn, 0, s0)
+                er[0] = edge_rows(rn, 0, bt_[0])
         else:
-            outputs(0, qx[0], "y", "y")
-        ps = make(1, [la, tP], land[:], T["fp%d" % r])
+            behind = outputs(0, qx[0], "y", "y")
+        ps = make(1, [la, tP], land[:], T["fp%d" % r], behind)
         if rn < R:
             lists[1] = dup(T["us%d" % rn], land[:], [la], 1)
             tab[1] = turn_half("gt", "tr", rn, 1, table_lookup(rn, 1, "v", lists[1][0]))
@@ -437,7 +460,7 @@ def rank_program(g, core, T, topo):
             e0 = turn_half("et", "er", rn, 0, er[0])
             bt_[1] = bits(rn, 1, s1)
         else:
-            outputs(1, qx[1], "y", "s")
+            outputs(1, qx[1], "y", "s")()
     need("g", [("loc", loc[0]), ("outs", dma_n["outs"])])
     for e in ("v", "s", "t", "g"):
         need("g", [(e + "q", cnt[e])])

@@ -3,7 +3,8 @@ from concourse.mybir import dt, AluOpType as A, ActivationFunctionType as AF
 
 N, C, H, R = 8, 320, 160, 3
 BF, F32, I32, U16, U8, MX = "bfloat16", "float32", "int32", "uint16", "uint8", "float8_e4m3fn_x4"
-SAME = 4680.0
+EA = (0, 1, 4, 5)
+SAME = 1632.0
 INV = 0.015625
 
 
@@ -18,10 +19,10 @@ def _scratch():
     sb("vb", 512, BF); sb("vq", 128, MX); sb("vp", 128, U8)
     sb("wq", 512, MX); sb("wp", 512, U8)
     sb("c64", 192, BF); sb("eb", 516, BF); sb("ec", 512, MX); sb("es", 512, U8)
-    sb("ci", 64, I32); sb("cf", 64, F32); sb("uls", 8, U16); sb("sg", 500, F32); sb("idl", 20, U16); sb("rt", 24, U16)
+    sb("ci", 64, I32); sb("cf", 64, F32); sb("uls", 8, U16); sb("sg", 100, F32); sb("idl", 20, U16); sb("rt", 24, U16)
     sb("ali", 20, I32)
     sb("nt", 160, I32); sb("ni", 480, I32); sb("un", 176, F32); sb("nf", 176, F32); sb("hn", 384, BF)
-    sb("ru", 576, F32); sb("rw", 672, F32); sb("gg", 384, F32); sb("tw", 704, F32)
+    sb("ru", 384, F32); sb("rw", 672, F32); sb("gg", 384, F32); sb("tw", 704, F32)
     sb("iw", 320, F32); sb("orow", 320, F32); sb("yb", 320, F32); sb("kx", 240, F32)
     for r in range(R + 1):
         sb("x%d" % r, 1280, BF); sb("qx%d" % r, 320, MX); sb("sx%d" % r, 320, U8)
@@ -34,14 +35,14 @@ def _scratch():
         sb("bw%d" % r, 320, BF); sb("br%d" % r, 640, BF); sb("bt%d" % r, 640, BF)
         sb("er%d" % r, 640, BF); sb("et%d" % r, 640, BF)
         sb("tr%d" % r, 640, F32); sb("gt%d" % r, 640, F32)
-        sb("fs%d" % r, 1240, F32); sb("is%d" % r, 340, I32)
+        sb("fs%d" % r, 740, F32); sb("is%d" % r, 280, I32)
         sb("us%d" % r, 100, U16)
     return s
 
 
 SCRATCH = _scratch()
 SEMAPHORES = (["vq", "sq", "tq", "gq", "loc"]
-              + ["ld_x0", "ld_x1", "ld_u", "ld_v", "ld_w", "ld_al", "ld_nx", "outs", "kx0", "kx1", "kx2"]
+              + ["ld_x0", "ld_x1", "ld_u", "ld_v", "ld_w", "ld_al", "ld_nx", "outs"]
               + ["%s%d%d" % (k, r, h) for k in ("rc", "rp", "qa") for r in range(R) for h in range(2)]
               + ["%s%d" % (k, r) for k in ("rl", "la") for r in range(R)])
 
@@ -180,32 +181,34 @@ def rank_program(g, core, T, topo):
 
     def line(k, src, a, b):
         return op("s", [cols], "act", col(k), col(src), AF.Identity, scale=a, bias=b)
-    fill_s(T.hn[:, 0:192], 192, 16.0)
+    fill_s(T.hn[:, 0:192], 192, 4.0)
     o = fill_s(T.hn[:, 192:384], 192, 2.0)
-    fill_s(T.un[:, 160:176], 16, 8.0)
+    fill_s(T.un[:, 160:176], 16, 32.0)
     line(12, T8, -192.0, 575.0)
     line(13, T8, 193.0, -381.0)
+    line(19, T8, 193.0, -575.0)
+    line(21, T8, -192.0, 591.0)
     s1 = line(14, LANE, 16.0, -223.0)
     line(UP0, ODD, 384.0, 0.0)
     line(UP1, ODD, -384.0, 384.0)
-    line(ES, LANE, -2.0, 31.0)
+    line(ES, LANE, -14.0, 211.0)
     s2 = line(KO, ODD, -SAME, SAME)
     fill_s(T.nf[:, 160:176], 16, 0.0)
-    v_hn = fill_s(T.hn[:, 0:384:4], 96, 0.0, [o])
+    fill_s(T.hn[:, 2:192:4], 48, 64.0, [o])
+    fill_s(T.hn[:, 194:384:4], 48, 8.0)
+    v_hn = fill_s(T.hn[:, 0:384:4], 96, 0.0)
     fill_s(T.kx[:, 1:240:2], 120, SAME)
-    seg = fill_s(T.sg[:, 0:500:5], 100, 0.0)
+    seg = fill_s(T.sg[:, 0:100:5], 20, 0.0)
     op("v", [cols], "ts", col(KL), col(R8), 0.0, None, A.is_equal)
     op("v", [], "ts", col(15), col(LANE), 14.0, None, A.is_lt)
     op("v", [], "ts", col(TH), col(LANE), 0.0, 1e29, A.is_equal, A.mult)
 
     def const_tile(b):
         return op("v", [g_eb], "qz", T.ec[:, 128 * b:128 * b + 128], T.es[:, 128 * b:128 * b + 128], T.eb[:, 3 - b:515 - b])
-    const_tile(0)
-    o = op("v", [s1], "ts", col(16), col(R8), 4.0, col(12), A.min, A.add)
-    const_tile(1)
-    o = op("v", [o], "ts", col(17), col(13), col(KL), col(16), A.mult, A.add)
-    const_tile(2)
-    c18 = op("v", [o], "ts", col(18), col(KL), -194.0, col(17), A.mult, A.add)
+    for b in range(4):
+        vE = const_tile(b)
+    op("v", [s1], "ts", col(20), col(R8), 4.0, col(21), A.min, A.add)
+    c16 = op("v", [], "ts", col(16), col(R8), 4.0, col(12), A.min, A.add)
 
     def dup(dst, src, toks, h, n=20):
         a = 20 * h
@@ -214,37 +217,35 @@ def rank_program(g, core, T, topo):
         op("v", [], "cp", dst[:, 20 + a:20 + a + n:2], src)
         return t, op("v", [], "cp", dst[:, 21 + a:20 + a + n:2], src)
 
-    vE = const_tile(3)
-    v_ul = op("v", [g_ul], "ts", T.uls[:], ci[:, 8:16], col(15), col(14), A.mult, A.max)
-    op("v", [g_rt, c18], "ts", T.rt[:, 0:24:2], ci[:, 16:28], col(17), None, A.add)
-    v_rt = op("v", [], "ts", T.rt[:, 1:24:2], ci[:, 16:28], col(18), 16.0, A.add, A.add)
-    v_id = op("v", [g_id], "ts", T.idl[:], ci[:, 28:48], col(LANE), None, A.add)
-    lists = [dup(T.us0, T.ali[:], [ld_al], 0, 40)] * 2
-
     nt, ni, un, nf, ru, rw, tw = T.nt, T.ni, T.un, T.nf, T.ru, T.rw, T.tw
-    op("v", [ld_nx], "ts", ni[:, 0:160], nt[:], 1.0 / 512, 8.0 - 159.5 / 512, A.mult, A.add)
-    o = op("v", [], "ts", ni[:, 160:320], nt[:], 7, 28, A.arith_shift_right, A.bitwise_and)
+    op("v", [ld_nx], "ts", ni[:, 0:160], nt[:], 1.0 / 512, 32.0 - 159.5 / 512, A.mult, A.add)
+    o = op("v", [], "ts", ni[:, 160:320], nt[:], 5, 112, A.arith_shift_right, A.bitwise_and)
     n1 = op("v", [], "ts", ni[:, 320:480], nt[:], 511, None, A.bitwise_and)
+    op("v", [c16], "ts", col(17), col(13), col(KL), col(16), A.mult, A.add)
     o = op("v", [o], "tt", un[:, 0:160], ni[:, 0:160], ni[:, 160:320], A.max)
     n2 = op("v", [n1], "cp", nf[:, 0:160], ni[:, 320:480])
+    v_ul = op("v", [g_ul], "ts", T.uls[:], ci[:, 8:16], col(15), col(14), A.mult, A.max)
+    c18 = op("v", [], "ts", col(18), col(19), col(KL), col(20), A.mult, A.add)
     op("v", [o, v_hn], "tp", ru[:, 0:96], un[:, 0:96])
     t1 = op("v", [], "tp", ru[:, 96:192], un[:, 80:176])
-    o = op("s", [t1], "act", ru[:, 192:384], ru[:, 0:192], AF.Square, bias=-8.0)
-    u4 = op("s", [o], "act", ru[:, 384:576], ru[:, 192:384], AF.Square)
+    u4 = op("s", [t1], "act", ru[:, 192:384], ru[:, 0:192], AF.Square, bias=-32.0)
     qu = op("v", [ld_u], "qz", T.uq[:], T.up[:], T.ub[:])
     s_u = op("s", [qu, v_ul], "act", T.up2[:], T.up[:].indirect(T.uls[:]), AF.Copy)
-    k1 = op("v", [t1, v_hn], "scan", rw[:, 0:192], T.hn[:, 0:192], ru[:, 0:192], 0.0, A.mult, A.add)
+    qx = [op("v", [ld_x[0]], "qz", T.qx0[:, 0:H], T.sx0[:, 0:H], T.x0[:, 0:640])]
     op("v", [n2], "tp", rw[:, 384:480], nf[:, 0:96])
     n3 = op("v", [], "tp", rw[:, 480:576], nf[:, 80:176])
-    k2 = op("v", [u4], "scan", rw[:, 192:384], T.hn[:, 192:384], ru[:, 384:576], 0.0, A.mult, A.add)
-    op("v", [k1], "tt", rw[:, 0:96:4], rw[:, 99:192:4], rw[:, 3:96:4], A.subtract)
-    op("v", [], "ts", rw[:, 1:96:4], rw[:, 3:96:4], -8.0 * 4369, None, A.add)
+    k1 = op("v", [t1, v_hn], "scan", rw[:, 0:192], T.hn[:, 0:192], ru[:, 0:192], 0.0, A.mult, A.add)
     op("v", [n3], "tt", rw[:, 576:672], rw[:, 480:576], rw[:, 384:480], A.subtract)
+    k2 = op("v", [u4], "scan", rw[:, 192:384], T.hn[:, 192:384], ru[:, 192:384], 0.0, A.mult, A.add)
+    op("v", [k1], "tt", rw[:, 0:96:4], rw[:, 99:192:4], rw[:, 3:96:4], A.subtract)
+    op("v", [], "ts", rw[:, 1:96:4], rw[:, 3:96:4], -32.0 * 1285, None, A.add)
+    op("v", [g_rt, c18], "ts", T.rt[:, 0:24:2], ci[:, 16:28], col(17), None, A.add)
+    v_rt = op("v", [], "ts", T.rt[:, 1:24:2], ci[:, 16:28], col(18), None, A.add)
     k3 = op("v", [k2], "tt", rw[:, 194:288:4], rw[:, 291:384:4], rw[:, 195:288:4], A.subtract)
     k4 = op("s", [k3, v_rt], "act", T.gg[:], rw[:].indirect(T.rt[:]), AF.Copy)
     v_u = [s_u, op("v", [qu, v_ul], "cp", T.uq2[:].bitcast(dt.uint32), T.uq[:].bitcast(dt.uint32).indirect(T.uls[:]))]
-    qx = [op("v", [ld_x[h]], "qz", T.qx0[:, H * h:H * h + H], T.sx0[:, H * h:H * h + H], T.x0[:, 640 * h:640 * h + 640])
-          for h in range(2)]
+    qx.append(op("v", [ld_x[1]], "qz", T.qx0[:, H:C], T.sx0[:, H:C], T.x0[:, 640:1280]))
+    lists = [dup(T.us0, T.ali[:], [ld_al], 0, 40)] * 2
 
     def send_codes(r, h, tok):
         need("g", [tok])
@@ -284,9 +285,12 @@ def rank_program(g, core, T, topo):
             readers[k].append(o)
         return o
 
-    def edge_rows(r, h, tok):
-        return op("s", [tok, v_id, s2], "act", T["er%d" % r][:, C * h:C * h + C],
-                  T["bw%d" % r][:, H * h:H * h + H].indirect(T.idl[:]), AF.Identity, scale=col(ES), bias=1.0)
+    def edge_rows(r, h, tok, e="s", a=0, n=20):
+        out = T["er%d" % r][:, C * h + 16 * a:C * h + 16 * (a + n)]
+        win = T["bw%d" % r][:, H * h:H * h + H].indirect(T.idl[:, a:a + n])
+        if e == "v":
+            return op("v", [tok, v_id, s2], "ts", out, win, col(ES), 1.0, A.mult, A.add)
+        return op("s", [tok, v_id, s2], "act", out, win, AF.Identity, scale=col(ES), bias=1.0)
 
     def turn_half(dst, src, r, h, tok):
         return op("v", [tok], "tp", T[dst + str(r)][:, C * h:C * h + C], T[src + str(r)][:, C * h:C * h + C])
@@ -303,10 +307,11 @@ def rank_program(g, core, T, topo):
     send_codes(0, 0, qx[0])
     send_codes(0, 1, qx[1])
     g_iw = op("g", [], "iota", T.iw[:], [[1, 320]], 0, 0, **fl)
-    bt_ = [bits(0, 0, sc[0]), None]
+    v_id = op("v", [g_id], "ts", T.idl[:], ci[:, 28:48], col(LANE), None, A.add)
+    bt_ = [bits(0, 0, sc[0]), bits(0, 1, sc[1])]
+    er = [edge_rows(0, 0, bt_[0]), None]
     for m in range(4):
         k5 = op("v", [k4], "tp", tw[:, m:384:4], T.gg[:, 96 * m:96 * m + 96])
-    bt_[1] = bits(0, 1, sc[1])
     v_tw = op("s", [k5], "act", tw[:, 384:704], tw[:, 0:320], AF.Copy, scale=col(KL))
     trow = [table_lookup(0, 0, "s", lists[0][0]), None]
     p2 = signs_by_list(0, 1)
@@ -319,63 +324,53 @@ def rank_program(g, core, T, topo):
         p1 = signs_by_list(r, 0)
         if r == 0:
             trow[1] = table_lookup(0, 1, "v", lists[1][0])
+            er[1] = edge_rows(0, 1, bt_[1])
             tab = [turn_half("gt", "tr", 0, 0, trow[0]), turn_half("gt", "tr", 0, 1, trow[1])]
-            er = [edge_rows(0, 0, bt_[0]), None]
+            e0 = turn_half("et", "er", 0, 0, er[0])
+            dma("y", [ld_x], T.wq[:].bitcast(dt.uint8), T.wc[:], "ld_w")
+            ld_w = dma("y", [], T.wp[:], T.ws[:], "ld_w")
+            ld_v = dma("y", [ld_w], T.vb[:], T.v[:], "ld_v")
         else:
             p2 = signs_by_list(r, 1)
+            er[1] = [edge_rows(r, 1, bt_[1], "v", 0, 10), edge_rows(r, 1, bt_[1], "s", 10, 10)]
         v_bt = op("v", [p1, p2], "tp", btb[:], br[:])
-        er[1] = edge_rows(r, 1, bt_[1])
-        signs = btb[:, 0:640:8]
-        ks = op("v", [v_bt, tab], "scan", fs[:, 0:80], signs, gt[:, 0:640:8], 0.0, A.mult, A.add)
-        kd = [dma("y", [ks, seg], T.kx[32 * d:128, 80 * (3 - d):80 * (4 - d)], fs[0:128 - 32 * d, 0:80], "kx%d" % (3 - d))
-              for d in (3, 2, 1)]
-        if r == 0:
-            dma("y", [], T.wq[:].bitcast(dt.uint8), T.wc[:], "ld_w")
-            ld_w = dma("y", [], T.wp[:], T.ws[:], "ld_w")
-        if r == 1:
-            ld_v = dma("y", [], T.vb[:], T.v[:], "ld_v")
-        dv, dw, sg = fs[:, 420:520], fs[:, 620:720], T.sg
-        ns = [op("v", [], "scan", fs[:, 100 + 80 * e:180 + 80 * e], signs, gt[:, 1 + e:640:8], 0.0, A.mult, A.add) for e in range(4)]
-        ko = op("v", [ks, s2], "ts", ints[:, 240:260], fs[:, 1:80:4], col(ODD), col(KO), A.mult, A.add)
-        for d in (420, 620):
-            for h in range(2):
-                old = op("v", [], "cp", fs[:, d + 4 + 50 * h:d + 50 + 50 * h:5], cur[h])
-        if r == 0:
-            e0 = turn_half("et", "er", 0, 0, er[0])
-        far = [fs[:, 520 + 20 * e:540 + 20 * e] for e in range(4)] + [fs[:, 424:520:5]]
-        de = [op("v", [ns[e]], "tt", far[e], fs[:, 101 + 80 * e:180 + 80 * e:4], fs[:, 103 + 80 * e:180 + 80 * e:4], A.add)
-              for e in range(4)]
         e1 = turn_half("et", "er", r, 1, er[1])
-        m4 = [op("v", [ko], "ts", ints[:, 260 + 20 * e:280 + 20 * e], ints[:, 240:260], 3 - e, 0x1111, A.arith_shift_right, A.bitwise_and)
-              for e in range(4)]
+        kx, dv, sg = T.kx, fs[:, 420:520], T.sg
+        k3 = op("v", [v_bt, tab, seg], "scan", kx[96:128, 0:80], btb[0:32, 0:640:8], gt[0:32, 0:640:8], 0.0, A.mult, A.add)
+        ks = op("v", [], "scan", fs[:, 0:80], btb[:, 0:640:8], gt[:, 0:640:8], 0.0, A.mult, A.add)
         st = op("v", [e0, e1], "tt", fs[:, 720:740], et[:, 14:640:32], et[:, 15:640:32], A.mult)
-        dd = [op("v", [de, old], "tt", fs[:, 420 + e:520:5], far[e], far[e + 1], A.subtract) for e in range(4)]
-        got = [fs[:, 744 + 100 * e:840 + 100 * e:5] for e in range(4)] + [fs[:, 624:720:5]]
-        f4, pk = [], []
-        fill = [lambda e=e: f4.append(op("v", [m4], "ts", sg[:, 100 + e:500:5], ints[:, 260:340], float(16 ** e) if e < 4 else 0.0,
-                                         None, A.not_equal)) for e in range(1, 5)]
-        fill += [lambda e=e: pk.append(op("v", [f4, dd, seg], "scan", fs[:, 740 + 100 * e:840 + 100 * e],
-                                          sg[:, 100 + 100 * e:200 + 100 * e], dv, 0.0, A.mult, A.add)) for e in range(4)]
-        fill += [lambda e=e: pk.append(op("v", [pk[:e + 2]], "tt", fs[:, 620 + e:720:5], got[e], got[e + 1], A.subtract))
-                 for e in range(4)]
+        k2 = op("s", [ks], "act", kx[64:128, 81:160:2], fs[0:64, 1:80:2], AF.Copy)
+        k1 = [op("s", [], "act", kx[32 * q + 32:32 * q + 64, 161:240:2], fs[32 * q:32 * q + 32, 1:80:2], AF.Copy) for q in range(3)]
+        kd = [k3, k2, k1]
+        far = [fs[:, 520 + 20 * e:540 + 20 * e] for e in range(4)] + [fs[:, 424:520:5]]
+        ns, de, dd, ko = [], [], [], []
+        fill = [lambda e=e: ns.append(op("v", [], "scan", fs[:, 100 + 80 * e:180 + 80 * e], btb[:, 0:640:8], gt[:, 1 + e:640:8],
+                                         0.0, A.mult, A.add)) for e in range(4)]
+        fill += [lambda h=h: de.append(op("v", [], "cp", fs[:, 424 + 50 * h:470 + 50 * h:5], cur[h])) for h in range(2)]
+        fill += [lambda e=e: de.append(op("v", [ns[e]], "tt", far[e], fs[:, 101 + 80 * e:180 + 80 * e:4],
+                                          fs[:, 103 + 80 * e:180 + 80 * e:4], A.add)) for e in range(4)]
+        fill += [lambda: ko.append(op("v", [ks, s2], "ts", fs[:, 80:100], fs[:, 1:80:4], col(ODD), col(KO), A.mult, A.add))]
+        fill += [lambda e=e: dd.append(op("v", [de], "tt", fs[:, 420 + e:520:5], far[e], far[e + 1], A.subtract)) for e in range(4)]
         qa = [("qa%d%d" % (r, h), 3 * far_engines) for h in range(2)]
         tF = unpack_copy(T["f%d" % r], unpack(T["qx%d" % r], T["sx%d" % r], [qx, vE]))
         if r > 0:
             unpack_copy(T["fp%d" % r], unpack(T["qp%d" % r], T["sp%d" % r], [qa[0]], 0, H), 0, H)
         sv, at = fs[:, 720:740], 0
-        for j in range(6):
+        for j in range(7):
             tv = ints[:, at:at + 20]
             a = 80 * (j // 2) + 1 + 2 * (j % 2)
-            st = op("v", [st, kd[j // 2]], "tt", tv, T.kx[:, a:80 * (j // 2) + 80:4], sv, A.mult)
-            fill[2 * j]()
+            st = op("v", [st, kd[j // 2]], "tt", tv, kx[:, a:80 * (j // 2) + 80:4], sv, A.mult) if j < 6 else \
+                op("v", [st, ko], "tt", tv, fs[:, 80:100], sv, A.mult)
+            fill.pop(0)()
             sv = ints[:, at + 20:at + 40]
-            st = op("v", [st], "ts", sv, tv, 15, 15, A.arith_shift_right, A.bitwise_and) if j % 2 else \
-                op("v", [st], "ts", sv, tv, 0x8888, None, A.bitwise_and)
-            fill[2 * j + 1]()
+            st = op("v", [st], "ts", sv, tv, 15, 0x33, A.arith_shift_right, A.bitwise_and) if j % 2 else \
+                op("v", [st], "ts", sv, tv, 0xA0A0, None, A.bitwise_and)
+            fill.pop(0)()
             at += 40
-        hs = [op("v", [st], "ts", sg[:, e:100:5], sv, float(2 ** e) if e < 4 else 0.0, None, A.not_equal) for e in range(1, 5)]
-        st = op("v", [hs, pk], "scan", fs[:, 1140:1240], sg[:, 0:100], dw, 0.0, A.mult, A.add)
-        ls = op("v", [st], "cp", us[:, 0:20], fs[:, 1144:1240:5])
+        fill.pop(0)()
+        hs = [op("v", [st], "ts", sg[:, e:100:5], sv, float(32 * 4 ** EA[e]) if e < 4 else 0.0, None, A.not_equal) for e in range(1, 5)]
+        st = op("v", [hs, dd], "scan", fs[:, 620:720], sg[:], dv, 0.0, A.mult, A.add)
+        ls = op("v", [st], "cp", us[:, 0:20], fs[:, 624:720:5])
         need("g", [ls])
         rid, pid = topo.addr(rel[0], core)
         g.remote_dma(T["rl%d" % r][:], us[:, 10:20], T.sem["rl%d" % r], T.sem.loc, pid, rid, topo.mask(core, rel[0]))

@@ -6,6 +6,7 @@ BF, F32, I32, U16, U8, MX = "bfloat16", "float32", "int32", "uint16", "uint8", "
 EA = (0, 1, 4, 5)
 SAME = 1632.0
 INV = 0.015625
+WAITS = ["n", "nnk", "nm", "dm", "mm", "cc", "ccf", "fff", "p", "pp", "p", "qq", "qq"]
 
 
 def _scratch():
@@ -19,10 +20,10 @@ def _scratch():
     sb("vb", 512, BF); sb("vq", 128, MX); sb("vp", 128, U8)
     sb("wq", 512, MX); sb("wp", 512, U8)
     sb("c64", 192, BF); sb("eb", 516, BF); sb("ec", 512, MX); sb("es", 512, U8)
-    sb("ci", 64, I32); sb("cf", 64, F32); sb("uls", 8, U16); sb("sg", 100, F32); sb("idl", 20, U16); sb("rt", 24, U16)
-    sb("ali", 20, I32)
+    sb("ci", 64, I32); sb("cf", 64, F32); sb("uls", 8, U16); sb("sg", 500, F32); sb("rt", 24, U16)
+    sb("ali", 20, I32); sb("l0", 20, U16)
     sb("nt", 160, I32); sb("ni", 480, I32); sb("un", 176, F32); sb("nf", 176, F32); sb("hn", 384, BF)
-    sb("ru", 384, F32); sb("rw", 672, F32); sb("gg", 384, F32); sb("tw", 704, F32)
+    sb("ru", 384, F32); sb("rw", 672, F32); sb("gg", 384, F32); sb("tw", 384, F32); sb("tq", 320, F32)
     sb("iw", 320, F32); sb("orow", 320, F32); sb("yb", 320, F32); sb("kx", 240, F32)
     for r in range(R + 1):
         sb("x%d" % r, 1280, BF); sb("qx%d" % r, 320, MX); sb("sx%d" % r, 320, U8)
@@ -33,10 +34,10 @@ def _scratch():
         sb("rq%d" % r, 320, MX); sb("rs%d" % r, 320, U8)
         sb("ll%d" % r, 10, U16); sb("rl%d" % r, 10, U16)
         sb("bw%d" % r, 320, BF); sb("br%d" % r, 640, BF); sb("bt%d" % r, 640, BF)
-        sb("er%d" % r, 640, BF); sb("et%d" % r, 640, BF)
-        sb("tr%d" % r, 640, F32); sb("gt%d" % r, 640, F32)
-        sb("fs%d" % r, 740, F32); sb("is%d" % r, 280, I32)
-        sb("us%d" % r, 100, U16)
+        s["er%d" % r] = ("sbuf", [128, 20, 32], BF); sb("et%d" % r, 640, BF)
+        s["tr%d" % r] = ("sbuf", [128, 20, 32], F32); sb("gt%d" % r, 640, F32)
+        sb("fs%d" % r, 1140, F32); sb("is%d" % r, 340, I32)
+        sb("us%d" % r, 60, U16)
     return s
 
 
@@ -51,7 +52,7 @@ def _relays(core, nxt, topo):
     w = [c for c in topo.cores_of(core) if c != core and topo.may_write(c, nxt)]
     near = [c for c in w if topo.die(c) == topo.die(core)]
     far = [c for c in w if topo.die(c) != topo.die(core)]
-    return near[0], near[1], far[0]
+    return near[0], near[1], far[0], far[1]
 
 
 def _mask(es):
@@ -77,7 +78,9 @@ def _hand_on(g, core, T, topo):
     n = 0
     for r in range(R):
         for h in range(2):
-            if k == 0:
+            if k % 3 == 0 and k != 3 * h:
+                continue
+            if k % 3 == 0:
                 g.wait_ge(T.sem["rp%d%d" % (r, h)], near)
                 g.remote_dma(T["sp%d" % r][:, H * h:H * h + H], T["rs%d" % r][:, H * h:H * h + H],
                              T.sem["qa%d%d" % (r, h)], T.sem.loc, pid, rid, m)
@@ -159,8 +162,9 @@ def rank_program(g, core, T, topo):
 
     ld_nx = dma("y", [], T.nt[:], T.nx[:], "ld_nx")
     ld_al = dma("s", [], T.ali[:], T.al[:], "ld_al")
+    ld_x = [dma("y", [], T.x0[:, 0:640], T.x[:, 0:640], "ld_x0")]
     ld_u = dma("y", [], T.ub[:], T.u[:], "ld_u")
-    ld_x = [dma("y", [], T.x0[:, 640 * h:640 * h + 640], T.x[:, 640 * h:640 * h + 640], "ld_x%d" % h) for h in range(2)]
+    ld_x.append(dma("y", [], T.x0[:, 640:1280], T.x[:, 640:1280], "ld_x1"))
 
     fl = {"allow_small_or_imprecise_dtypes": True}
     v_c64 = op("v", [], "ms", T.c64[:], 64.0)
@@ -169,7 +173,6 @@ def rank_program(g, core, T, topo):
     g_eb = op("g", [v_eb], "sel", T.eb[:, 3:515:4], T.c64[:, 0:128], [[-1, 128]], A.is_equal, 0.0, 0, 1)
     g_ul = op("g", [], "iota", ci[:, 8:16], [[16, 8]], 0, 0)
     g_rt = op("g", [], "iota", ci[:, 16:28], [[4, 4], [32, 3]], 0, 0)
-    g_id = op("g", [], "iota", ci[:, 28:48], [[16, 10], [0, 2]], 0, 0)
     LANE, ODD, R8, T8 = 1, 2, 3, 4
     for k, (sh, m) in enumerate([(0, 15), (4, 1), (0, 7), (3, 1)]):
         o = op("v", [g_p], "ts", icol(1 + k), icol(0), sh, m, A.arith_shift_right, A.bitwise_and)
@@ -189,8 +192,7 @@ def rank_program(g, core, T, topo):
     line(19, T8, 193.0, -575.0)
     line(21, T8, -192.0, 591.0)
     s1 = line(14, LANE, 16.0, -223.0)
-    line(UP0, ODD, 384.0, 0.0)
-    line(UP1, ODD, -384.0, 384.0)
+    line(22, ODD, -1.0, 1.0)
     line(ES, LANE, -14.0, 211.0)
     s2 = line(KO, ODD, -SAME, SAME)
     fill_s(T.nf[:, 160:176], 16, 0.0)
@@ -198,44 +200,40 @@ def rank_program(g, core, T, topo):
     fill_s(T.hn[:, 194:384:4], 48, 8.0)
     v_hn = fill_s(T.hn[:, 0:384:4], 96, 0.0)
     fill_s(T.kx[:, 1:240:2], 120, SAME)
-    seg = fill_s(T.sg[:, 0:100:5], 20, 0.0)
+    seg = fill_s(T.sg[:, 0:500:5], 100, 0.0)
     op("v", [cols], "ts", col(KL), col(R8), 0.0, None, A.is_equal)
     op("v", [], "ts", col(15), col(LANE), 14.0, None, A.is_lt)
     op("v", [], "ts", col(TH), col(LANE), 0.0, 1e29, A.is_equal, A.mult)
 
     def const_tile(b):
         return op("v", [g_eb], "qz", T.ec[:, 128 * b:128 * b + 128], T.es[:, 128 * b:128 * b + 128], T.eb[:, 3 - b:515 - b])
-    for b in range(4):
-        vE = const_tile(b)
-    op("v", [s1], "ts", col(20), col(R8), 4.0, col(21), A.min, A.add)
-    c16 = op("v", [], "ts", col(16), col(R8), 4.0, col(12), A.min, A.add)
+    vE = [const_tile(0)]
 
     def dup(dst, src, toks, h, n=20):
-        a = 20 * h
-        op("v", [toks, s2], "ts", dst[:, 60 + a:60 + a + n:2], src, col(UP0), None, A.add)
-        t = op("v", [], "ts", dst[:, 61 + a:60 + a + n:2], src, col(UP1), None, A.add)
-        op("v", [], "cp", dst[:, 20 + a:20 + a + n:2], src)
-        return t, op("v", [], "cp", dst[:, 21 + a:20 + a + n:2], src)
+        op("v", [toks], "cp", dst[:, 20 + 20 * h:20 + 20 * h + n:2], src)
+        return op("v", [], "cp", dst[:, 21 + 20 * h:20 + 20 * h + n:2], src)
 
     nt, ni, un, nf, ru, rw, tw = T.nt, T.ni, T.un, T.nf, T.ru, T.rw, T.tw
     op("v", [ld_nx], "ts", ni[:, 0:160], nt[:], 1.0 / 512, 32.0 - 159.5 / 512, A.mult, A.add)
     o = op("v", [], "ts", ni[:, 160:320], nt[:], 5, 112, A.arith_shift_right, A.bitwise_and)
     n1 = op("v", [], "ts", ni[:, 320:480], nt[:], 511, None, A.bitwise_and)
-    op("v", [c16], "ts", col(17), col(13), col(KL), col(16), A.mult, A.add)
+    op("v", [s1], "ts", col(20), col(R8), 4.0, col(21), A.min, A.add)
     o = op("v", [o], "tt", un[:, 0:160], ni[:, 0:160], ni[:, 160:320], A.max)
     n2 = op("v", [n1], "cp", nf[:, 0:160], ni[:, 320:480])
-    v_ul = op("v", [g_ul], "ts", T.uls[:], ci[:, 8:16], col(15), col(14), A.mult, A.max)
-    c18 = op("v", [], "ts", col(18), col(19), col(KL), col(20), A.mult, A.add)
+    c16 = op("v", [], "ts", col(16), col(R8), 4.0, col(12), A.min, A.add)
     op("v", [o, v_hn], "tp", ru[:, 0:96], un[:, 0:96])
     t1 = op("v", [], "tp", ru[:, 96:192], un[:, 80:176])
     u4 = op("s", [t1], "act", ru[:, 192:384], ru[:, 0:192], AF.Square, bias=-32.0)
-    qu = op("v", [ld_u], "qz", T.uq[:], T.up[:], T.ub[:])
-    s_u = op("s", [qu, v_ul], "act", T.up2[:], T.up[:].indirect(T.uls[:]), AF.Copy)
     qx = [op("v", [ld_x[0]], "qz", T.qx0[:, 0:H], T.sx0[:, 0:H], T.x0[:, 0:640])]
     op("v", [n2], "tp", rw[:, 384:480], nf[:, 0:96])
     n3 = op("v", [], "tp", rw[:, 480:576], nf[:, 80:176])
+    op("v", [c16], "ts", col(17), col(13), col(KL), col(16), A.mult, A.add)
+    v_ul = op("v", [g_ul], "ts", T.uls[:], ci[:, 8:16], col(15), col(14), A.mult, A.max)
+    qu = op("v", [ld_u], "qz", T.uq[:], T.up[:], T.ub[:])
+    v_u = [op("s", [qu, v_ul], "act", T.up2[:], T.up[:].indirect(T.uls[:]), AF.Copy)]
     k1 = op("v", [t1, v_hn], "scan", rw[:, 0:192], T.hn[:, 0:192], ru[:, 0:192], 0.0, A.mult, A.add)
     op("v", [n3], "tt", rw[:, 576:672], rw[:, 480:576], rw[:, 384:480], A.subtract)
+    c18 = op("v", [], "ts", col(18), col(19), col(KL), col(20), A.mult, A.add)
     k2 = op("v", [u4], "scan", rw[:, 192:384], T.hn[:, 192:384], ru[:, 192:384], 0.0, A.mult, A.add)
     op("v", [k1], "tt", rw[:, 0:96:4], rw[:, 99:192:4], rw[:, 3:96:4], A.subtract)
     op("v", [], "ts", rw[:, 1:96:4], rw[:, 3:96:4], -32.0 * 1285, None, A.add)
@@ -243,9 +241,8 @@ def rank_program(g, core, T, topo):
     v_rt = op("v", [], "ts", T.rt[:, 1:24:2], ci[:, 16:28], col(18), None, A.add)
     k3 = op("v", [k2], "tt", rw[:, 194:288:4], rw[:, 291:384:4], rw[:, 195:288:4], A.subtract)
     k4 = op("s", [k3, v_rt], "act", T.gg[:], rw[:].indirect(T.rt[:]), AF.Copy)
-    v_u = [s_u, op("v", [qu, v_ul], "cp", T.uq2[:].bitcast(dt.uint32), T.uq[:].bitcast(dt.uint32).indirect(T.uls[:]))]
+    v_u.append(op("v", [qu, v_ul], "cp", T.uq2[:].bitcast(dt.uint32), T.uq[:].bitcast(dt.uint32).indirect(T.uls[:])))
     qx.append(op("v", [ld_x[1]], "qz", T.qx0[:, H:C], T.sx0[:, H:C], T.x0[:, 640:1280]))
-    lists = [dup(T.us0, T.ali[:], [ld_al], 0, 40)] * 2
 
     def send_codes(r, h, tok):
         need("g", [tok])
@@ -259,9 +256,9 @@ def rank_program(g, core, T, topo):
                                         remote_sem=T.sem["rc%d%d" % (r, h)], src=T["qx%d" % r][:, a:a + 80].bitcast(dt.uint8),
                                         dst=T["rq%d" % r][:, a:a + 80].bitcast(dt.uint8)))
         g.remote_dma_fused(tr, local_sem=T.sem.loc)
-        rid, pid = topo.addr(rel[0], core)
+        rid, pid = topo.addr(rel[3 * h], core)
         g.remote_dma(T["rs%d" % r][:, H * h:H * h + H], T["sx%d" % r][:, H * h:H * h + H], T.sem["rp%d%d" % (r, h)],
-                     T.sem.loc, pid, rid, topo.mask(core, rel[0]))
+                     T.sem.loc, pid, rid, topo.mask(core, rel[3 * h]))
         loc[0] += 4 * n
 
     def scores(r, h, tok):
@@ -276,7 +273,7 @@ def rank_program(g, core, T, topo):
 
     def unpack(qc, qs, toks, a=0, n=C):
         ks = [bank() for b in range(4)]
-        return [(ks[b], mm([toks], ks[b], n, T.ec, T.es, b, qc, qs, a)) for b in range(4)]
+        return [(ks[b], mm([toks, vE[b]], ks[b], n, T.ec, T.es, b, qc, qs, a)) for b in range(4)]
 
     def unpack_copy(d, ps, a=0, n=C):
         for b in range(4):
@@ -285,91 +282,128 @@ def rank_program(g, core, T, topo):
             readers[k].append(o)
         return o
 
-    def edge_rows(r, h, tok, e="s", a=0, n=20):
-        out = T["er%d" % r][:, C * h + 16 * a:C * h + 16 * (a + n)]
-        win = T["bw%d" % r][:, H * h:H * h + H].indirect(T.idl[:, a:a + n])
-        if e == "v":
-            return op("v", [tok, v_id, s2], "ts", out, win, col(ES), 1.0, A.mult, A.add)
-        return op("s", [tok, v_id, s2], "act", out, win, AF.Identity, scale=col(ES), bias=1.0)
+    def edge_rows(r, h, tok):
+        for a in (0, 16):
+            o = op("v", [tok, s2], "ts", T["er%d" % r][:, 10 * h:10 * h + 10, a:a + 16], T["bw%d" % r][:, H * h:H * h + H],
+                   col(ES), 1.0, A.mult, A.add)
+        return o
 
-    def turn_half(dst, src, r, h, tok):
-        return op("v", [tok], "tp", T[dst + str(r)][:, C * h:C * h + C], T[src + str(r)][:, C * h:C * h + C])
+    def turn_edges(r, h, tok):
+        return op("v", [tok], "tp", T["et%d" % r][:, C * h:C * h + C], T["er%d" % r][:, 10 * h:10 * h + 10, :])
 
-    def table_lookup(r, h, e, tok):
-        out, win = T["tr%d" % r][:, C * h:C * h + C], tw[:].indirect(T["us%d" % r][:, 60 + 20 * h:80 + 20 * h])
-        return op("v", [tok, v_tw], "cp", out, win) if e == "v" else op("s", [tok, v_tw], "act", out, win, AF.Copy)
+    def turn_tables(r, h, tok):
+        return op("v", [tok], "tp", T["gt%d" % r][:, C * h:C * h + C], T["tr%d" % r][:, 10 * h:10 * h + 10, :])
 
-    def signs_by_list(r, h):
-        out, win = T["br%d" % r][:, C * h:C * h + C], T["bw%d" % r][:].indirect(T["us%d" % r][:, 20 + 20 * h:40 + 20 * h])
-        return op("s", [bt_, lists[1][1]], "act", out, win, AF.Copy) if h else op("v", [bt_, lists[0][1]], "cp", out, win)
+    def table_lookup(r, h, e, off, tok):
+        out, win = T.tq[:, H * h:H * h + H], tw[:].indirect(off)
+        return op("v", [tok, k5], "cp", out, win) if e == "v" else op("s", [tok, k5], "act", out, win, AF.Copy)
+
+    def table_twice(r, h, e, tok):
+        for s in range(2):
+            out, src = T["tr%d" % r][:, 10 * h:10 * h + 10, 16 * s:16 * s + 16], T.tq[:, H * h:H * h + H]
+            o = op("v", [tok], "ts", out, src, col(UP0 + s), None, A.mult) if e == "v" else \
+                op("s", [tok], "act", out, src, AF.Copy, scale=col(UP0 + s))
+        return o
+
+    def signs_by_list(r, h, e=None):
+        a, b = (18, 40) if h else (0, 18)
+        out, win = T["br%d" % r][:, 16 * a:16 * b], T["bw%d" % r][:].indirect(T["us%d" % r][:, 20 + a:20 + b])
+        return op("s", [bt_, lists[1]], "act", out, win, AF.Copy) if h or e else op("v", [bt_, lists[0]], "cp", out, win)
+
+    def keep_old(r, a, n, src):
+        return op("v", [], "cp", T["fs%d" % r][:, 424 + 5 * a:420 + 5 * (a + n):5], src)
 
     sc = [scores(0, 0, qx[0]), scores(0, 1, qx[1])]
     send_codes(0, 0, qx[0])
     send_codes(0, 1, qx[1])
     g_iw = op("g", [], "iota", T.iw[:], [[1, 320]], 0, 0, **fl)
-    v_id = op("v", [g_id], "ts", T.idl[:], ci[:, 28:48], col(LANE), None, A.add)
+    lists = [dup(T.us0, T.ali[:], [ld_al], 0, 40)] * 2
+    op("v", [s2], "ts", col(UP0), col(22), col(KL), None, A.max)
+    op("v", [], "ts", col(UP1), col(ODD), col(KL), None, A.max)
+    l0 = op("v", [], "cp", T.l0[:], T.ali[:])
+    old = keep_old(0, 0, 20, T.ali[:])
     bt_ = [bits(0, 0, sc[0]), bits(0, 1, sc[1])]
-    er = [edge_rows(0, 0, bt_[0]), None]
+    p1 = signs_by_list(0, 0, "s")
+    p2 = signs_by_list(0, 1)
     for m in range(4):
         k5 = op("v", [k4], "tp", tw[:, m:384:4], T.gg[:, 96 * m:96 * m + 96])
-    v_tw = op("s", [k5], "act", tw[:, 384:704], tw[:, 0:320], AF.Copy, scale=col(KL))
-    trow = [table_lookup(0, 0, "s", lists[0][0]), None]
-    p2 = signs_by_list(0, 1)
 
     for r in range(R):
         rn = r + 1
         us, fs, ints = T["us%d" % r], T["fs%d" % r], T["is%d" % r]
         br, btb, gt, et = T["br%d" % r], T["bt%d" % r], T["gt%d" % r], T["et%d" % r]
-        cur = (T.ali[:, 0:10], T.ali[:, 10:20]) if r == 0 else (T["us%d" % (r - 1)][:, 0:10], T["ll%d" % (r - 1)][:])
-        p1 = signs_by_list(r, 0)
         if r == 0:
-            trow[1] = table_lookup(0, 1, "v", lists[1][0])
-            er[1] = edge_rows(0, 1, bt_[1])
-            tab = [turn_half("gt", "tr", 0, 0, trow[0]), turn_half("gt", "tr", 0, 1, trow[1])]
-            e0 = turn_half("et", "er", 0, 0, er[0])
+            er = [edge_rows(0, h, bt_[h]) for h in range(2)]
+            trow = {h: table_twice(0, h, "s", table_lookup(0, h, "v", T.l0[:, 10 * h:10 * h + 10], l0)) for h in (1, 0)}
+            e0 = turn_edges(0, 0, er[0])
+            e1 = turn_edges(0, 1, er[1])
+            v_bt = op("v", [p1, p2], "tp", btb[:], br[:])
+            tab = [turn_tables(0, h, trow[h]) for h in (1, 0)]
             dma("y", [ld_x], T.wq[:].bitcast(dt.uint8), T.wc[:], "ld_w")
             ld_w = dma("y", [], T.wp[:], T.ws[:], "ld_w")
             ld_v = dma("y", [ld_w], T.vb[:], T.v[:], "ld_v")
         else:
+            er[1] = edge_rows(r, 1, bt_[1])
+            p1 = signs_by_list(r, 0)
             p2 = signs_by_list(r, 1)
-            er[1] = [edge_rows(r, 1, bt_[1], "v", 0, 10), edge_rows(r, 1, bt_[1], "s", 10, 10)]
-        v_bt = op("v", [p1, p2], "tp", btb[:], br[:])
-        e1 = turn_half("et", "er", r, 1, er[1])
-        kx, dv, sg = T.kx, fs[:, 420:520], T.sg
+            e1 = turn_edges(r, 1, er[1])
+            v_bt = op("v", [p1, p2], "tp", btb[:], br[:])
+        kx, sg, dv = T.kx, T.sg, fs[:, 420:520]
+        far = [fs[:, 520 + 20 * e:540 + 20 * e] for e in range(4)] + [fs[:, 424:520:5]]
+        got = [fs[:, 744 + 100 * e:840 + 100 * e:5] for e in range(4)] + [fs[:, 424:520:5]]
+        st = op("v", [e0, e1], "tt", fs[:, 80:100], et[:, 14:640:32], et[:, 15:640:32], A.mult)
         k3 = op("v", [v_bt, tab, seg], "scan", kx[96:128, 0:80], btb[0:32, 0:640:8], gt[0:32, 0:640:8], 0.0, A.mult, A.add)
         ks = op("v", [], "scan", fs[:, 0:80], btb[:, 0:640:8], gt[:, 0:640:8], 0.0, A.mult, A.add)
-        st = op("v", [e0, e1], "tt", fs[:, 720:740], et[:, 14:640:32], et[:, 15:640:32], A.mult)
         k2 = op("s", [ks], "act", kx[64:128, 81:160:2], fs[0:64, 1:80:2], AF.Copy)
         k1 = [op("s", [], "act", kx[32 * q + 32:32 * q + 64, 161:240:2], fs[32 * q:32 * q + 32, 1:80:2], AF.Copy) for q in range(3)]
         kd = [k3, k2, k1]
-        far = [fs[:, 520 + 20 * e:540 + 20 * e] for e in range(4)] + [fs[:, 424:520:5]]
-        ns, de, dd, ko = [], [], [], []
-        fill = [lambda e=e: ns.append(op("v", [], "scan", fs[:, 100 + 80 * e:180 + 80 * e], btb[:, 0:640:8], gt[:, 1 + e:640:8],
-                                         0.0, A.mult, A.add)) for e in range(4)]
-        fill += [lambda h=h: de.append(op("v", [], "cp", fs[:, 424 + 50 * h:470 + 50 * h:5], cur[h])) for h in range(2)]
-        fill += [lambda e=e: de.append(op("v", [ns[e]], "tt", far[e], fs[:, 101 + 80 * e:180 + 80 * e:4],
-                                          fs[:, 103 + 80 * e:180 + 80 * e:4], A.add)) for e in range(4)]
-        fill += [lambda: ko.append(op("v", [ks, s2], "ts", fs[:, 80:100], fs[:, 1:80:4], col(ODD), col(KO), A.mult, A.add))]
-        fill += [lambda e=e: dd.append(op("v", [de], "tt", fs[:, 420 + e:520:5], far[e], far[e + 1], A.subtract)) for e in range(4)]
-        qa = [("qa%d%d" % (r, h), 3 * far_engines) for h in range(2)]
-        tF = unpack_copy(T["f%d" % r], unpack(T["qx%d" % r], T["sx%d" % r], [qx, vE]))
-        if r > 0:
-            unpack_copy(T["fp%d" % r], unpack(T["qp%d" % r], T["sp%d" % r], [qa[0]], 0, H), 0, H)
-        sv, at = fs[:, 720:740], 0
-        for j in range(7):
+        w = {k: [] for k in "nkdmcfpq"}
+
+        def side(k, e):
+            if k == "n":
+                o = op("v", [], "scan", fs[:, 100 + 80 * e:180 + 80 * e], btb[:, 0:640:8], gt[:, 1 + e:640:8], 0.0, A.mult, A.add)
+            if k == "d":
+                o = op("v", [w["n"]], "tt", fs[:, 520:600], fs[:, 101:420:4], fs[:, 103:420:4], A.add)
+            if k == "c":
+                o = op("v", [w["d"], old], "tt", fs[:, 420 + e:520:5], far[e], far[e + 1], A.subtract)
+            if k == "k":
+                o = op("v", [ks, s2], "ts", ints[:, 240:260], fs[:, 1:80:4], col(ODD), col(KO), A.mult, A.add)
+            if k == "m":
+                o = op("v", [w["k"]], "ts", ints[:, 260 + 20 * e:280 + 20 * e], ints[:, 240:260], 5 - EA[e], 1285,
+                       A.arith_shift_right, A.bitwise_and)
+            if k == "f":
+                o = op("v", [w["m"]], "ts", sg[:, 101 + e:500:5], ints[:, 260:340], float(4 ** EA[e + 1]) if e < 3 else 0.0, None,
+                       A.not_equal)
+            if k == "p":
+                o = op("v", [w["f"], w["c"]], "scan", fs[:, 740 + 100 * e:840 + 100 * e], sg[:, 100 + 100 * e:200 + 100 * e], dv,
+                       0.0, A.mult, A.add)
+            if k == "q":
+                o = op("v", [w["p"]], "tt", fs[:, 420 + e:520:5], got[e], got[e + 1], A.subtract)
+            w[k].append(o)
+
+        def gap(j):
+            for k in WAITS[j]:
+                side(k, len(w[k]))
+            if r == 0 and j in (5, 10, 11):
+                vE.append(const_tile(len(vE)))
+        sv, at = fs[:, 80:100], 0
+        gap(0)
+        for j in range(6):
             tv = ints[:, at:at + 20]
             a = 80 * (j // 2) + 1 + 2 * (j % 2)
-            st = op("v", [st, kd[j // 2]], "tt", tv, kx[:, a:80 * (j // 2) + 80:4], sv, A.mult) if j < 6 else \
-                op("v", [st, ko], "tt", tv, fs[:, 80:100], sv, A.mult)
-            fill.pop(0)()
+            st = op("v", [st, kd[j // 2]], "tt", tv, kx[:, a:80 * (j // 2) + 80:4], sv, A.mult)
+            gap(2 * j + 1)
             sv = ints[:, at + 20:at + 40]
             st = op("v", [st], "ts", sv, tv, 15, 0x33, A.arith_shift_right, A.bitwise_and) if j % 2 else \
                 op("v", [st], "ts", sv, tv, 0xA0A0, None, A.bitwise_and)
-            fill.pop(0)()
+            gap(2 * j + 2)
             at += 40
-        fill.pop(0)()
-        hs = [op("v", [st], "ts", sg[:, e:100:5], sv, float(32 * 4 ** EA[e]) if e < 4 else 0.0, None, A.not_equal) for e in range(1, 5)]
-        st = op("v", [hs, dd], "scan", fs[:, 620:720], sg[:], dv, 0.0, A.mult, A.add)
+        qa = [("qa%d%d" % (r, h), 3 * far_engines) for h in range(2)]
+        tF = unpack_copy(T["f%d" % r], unpack(T["qx%d" % r], T["sx%d" % r], [qx]))
+        if r > 0:
+            unpack_copy(T["fp%d" % r], unpack(T["qp%d" % r], T["sp%d" % r], [qa[0]], 0, H), 0, H)
+        hs = [op("v", [st], "ts", sg[:, e:100:5], sv, float(2 ** EA[e]) if e < 4 else 0.0, None, A.not_equal) for e in range(1, 5)]
+        st = op("v", [hs, w["q"]], "scan", fs[:, 620:720], sg[:, 0:100], dv, 0.0, A.mult, A.add)
         ls = op("v", [st], "cp", us[:, 0:20], fs[:, 624:720:5])
         need("g", [ls])
         rid, pid = topo.addr(rel[0], core)
@@ -417,32 +451,40 @@ def rank_program(g, core, T, topo):
             return store_y
 
         land, la = T["ll%d" % r], ("la%d" % r, far_engines)
+        if r:
+            pP = unpack(T["qp%d" % r], T["sp%d" % r], [qa[1]], H, H)
         ps = make(0, [ls, tF], us[:, 0:10], T["f%d" % r])
+        if r:
+            tP = unpack_copy(T["fp%d" % r], pP, H, H)
         if rn < R:
             lists = [dup(T["us%d" % rn], us[:, 0:10], [ls], 0), None]
-            t0 = table_lookup(rn, 0, "s", lists[0][0])
+            t0 = table_twice(rn, 0, "s", table_lookup(rn, 0, "s", us[:, 0:10], ls))
+            keep_old(rn, 0, 10, us[:, 0:10])
         else:
             vv = op("v", [ld_v], "qz", T.vq[:], T.vp[:], T.vb[:])
             oa1 = op("s", [ls, g_iw], "act", T.orow[:, 0:H], T.iw[:].indirect(us[:, 0:10]), AF.Copy)
-        late = (H, H) if r else (0, C)
-        pP = unpack(T["qp%d" % r], T["sp%d" % r], [qa], *late)
-        o = [renew(0, b, ps, "s" if b == 3 else "v") for b in range(4)]
-        tP = unpack_copy(T["fp%d" % r], pP, *late)
+        if r == 0:
+            unpack_copy(T.fp0, unpack(T.qp0, T.sp0, [qa[0]], 0, H), 0, H)
+        o = [renew(0, b, ps, "v") for b in range(4)]
+        if r == 0:
+            tP = unpack_copy(T.fp0, unpack(T.qp0, T.sp0, [qa[1]], H, H), H, H)
         qx = [requant(0, o), None]
         if rn < R:
             s0 = scores(rn, 0, qx[0])
             send_codes(rn, 0, qx[0])
-            tab = [turn_half("gt", "tr", rn, 0, t0), None]
+            tab = [turn_tables(rn, 0, t0), None]
 
             def behind():
                 bt_[0] = bits(rn, 0, s0)
-                er[0] = edge_rows(rn, 0, bt_[0])
         else:
             behind = outputs(0, qx[0], "y", "y")
         ps = make(1, [la, tP], land[:], T["fp%d" % r], behind)
         if rn < R:
+            t1 = table_lookup(rn, 1, "v", land[:], la)
+            er[0] = edge_rows(rn, 0, bt_[0])
+            t1 = table_twice(rn, 1, "v", t1)
             lists[1] = dup(T["us%d" % rn], land[:], [la], 1)
-            tab[1] = turn_half("gt", "tr", rn, 1, table_lookup(rn, 1, "v", lists[1][0]))
+            tab[1] = turn_tables(rn, 1, t1)
             o = [renew(1, b, ps, "s") for b in range(4)]
         else:
             oa2 = op("v", [la, g_iw], "cp", T.orow[:, H:C], T.iw[:].indirect(land[:]))
@@ -452,7 +494,8 @@ def rank_program(g, core, T, topo):
         if rn < R:
             send_codes(rn, 1, qx[1])
             s1 = scores(rn, 1, qx[1])
-            e0 = turn_half("et", "er", rn, 0, er[0])
+            e0 = turn_edges(rn, 0, er[0])
+            old = keep_old(rn, 10, 10, land[:])
             bt_[1] = bits(rn, 1, s1)
         else:
             outputs(1, qx[1], "y", "s")()

@@ -3,28 +3,38 @@ from concourse.mybir import dt, AluOpType as A, ActivationFunctionType as AF
 
 N, C, H, R = 8, 320, 160, 3
 BF, F32, I32, U16, U8, MX = "bfloat16", "float32", "int32", "uint16", "uint8", "float8_e4m3fn_x4"
-EA = (0, 1, 4, 5)
-SAME = 1632.0
 INV = 0.015625
-WAITS = ["n", "nnk", "nm", "dm", "mm", "cc", "ccf", "fff", "p", "pp", "p", "qq", "qq"]
+LY, LD, LA, LN, LK = 0, 6, 11, 12, 28
+LH, LE = 14, 17
+NB = (5, 10)
+ORDER = ["TP", "MU tp MP", "MK M0 mu", "DF MP MP MP mk", "SC mp mp df", "NE PB sc", "SC mp mp ne", "NE DO DO DO sc",
+         "SC pb DO DO ne", "NE do do do sc", "PK do do ne", "CV pk", "t1", "t2", "cv"]
 
 
 def _scratch():
     s = {}
 
     def sb(name, n, t):
-        s[name] = ("sbuf", [128, n], t)
+        s[name] = ("sbuf", [128] + (n if isinstance(n, list) else [n]), t)
     for k in range(8):
         s["pk%d" % k] = ("psum", [128, 512], F32)
     sb("ub", 512, BF); sb("uq", 128, MX); sb("up", 128, U8); sb("uq2", 128, MX); sb("up2", 128, U8)
     sb("vb", 512, BF); sb("vq", 128, MX); sb("vp", 128, U8)
     sb("wq", 512, MX); sb("wp", 512, U8)
-    sb("c64", 192, BF); sb("eb", 516, BF); sb("ec", 512, MX); sb("es", 512, U8)
-    sb("ci", 64, I32); sb("cf", 64, F32); sb("uls", 8, U16); sb("sg", 500, F32); sb("rt", 24, U16)
-    sb("ali", 20, I32); sb("l0", 20, U16)
-    sb("nt", 160, I32); sb("ni", 480, I32); sb("un", 176, F32); sb("nf", 176, F32); sb("hn", 384, BF)
-    sb("ru", 384, F32); sb("rw", 672, F32); sb("gg", 384, F32); sb("tw", 384, F32); sb("tq", 320, F32)
-    sb("iw", 320, F32); sb("orow", 320, F32); sb("yb", 320, F32); sb("kx", 240, F32)
+    sb("c64", 288, BF); sb("eb", 516, BF); sb("ec", 512, MX); sb("es", 512, U8)
+    sb("ct", 96, F32); sb("cf", 96, F32); sb("ci", 8, I32); sb("rl", 22, U16); sb("uls", 8, U16); sb("th", 80, BF)
+    sb("ali", 20, I32); sb("nt", 160, I32); sb("ni", 160, I32); sb("cb", [2, 96], BF); sb("nf", [2, 96], F32)
+    sb("rc", [12, 4, 4], BF); sb("rt", [12, 4, 4], F32); sb("kw", [6, 4, 4], F32); sb("kc", [6, 4, 4], F32)
+    sb("ac", [12, 4], F32); sb("w1", [6, 4, 4], F32); sb("w2", [6, 4, 4], F32); sb("kp", [6, 4, 2], F32)
+    sb("ln", [12, 4, 16], F32); sb("tw", 768, F32); sb("bw", 640, BF); sb("cw", 640, F32)
+    for h, n in enumerate(NB):
+        sb("gg%d" % h, 32 * n, F32); sb("gt%d" % h, [n, 32], F32); sb("er%d" % h, [n, 32], BF); sb("et%d" % h, [n, 32], BF)
+        sb("tm%d" % h, [n, 4], I32); sb("y3%d" % h, [n, 9], I32); sb("dq%d" % h, 8 * n, BF); sb("me%d" % h, 8 * n, BF)
+        sb("mp%d" % h, 20 * n, BF); sb("se%d" % h, 8 * n + 8, BF); sb("ao%d" % h, 48 + 120 * h, F32)
+        sb("a4%d" % h, 112 + 112 * h, F32); sb("pb%d" % h, 20 * n, F32); sb("do%d" % h, 8 * n, F32)
+    sb("fl", 224, BF); sb("fm", 224, BF); sb("fw", [21, 32], BF); sb("ft", 672, BF)
+    sb("ae", 40, F32); sb("pm", 80, F32); sb("pa", 512, F32); sb("xt", [2, 32], F32); sb("lt", 64, F32)
+    sb("iw", 320, F32); sb("orow", 320, F32); sb("yb", 320, F32)
     for r in range(R + 1):
         sb("x%d" % r, 1280, BF); sb("qx%d" % r, 320, MX); sb("sx%d" % r, 320, U8)
     for r in range(R):
@@ -32,12 +42,7 @@ def _scratch():
         sb("qz%d" % r, 320, MX); sb("sz%d" % r, 320, U8)
         sb("qp%d" % r, 320, MX); sb("sp%d" % r, 320, U8)
         sb("rq%d" % r, 320, MX); sb("rs%d" % r, 320, U8)
-        sb("ll%d" % r, 10, U16); sb("rl%d" % r, 10, U16)
-        sb("bw%d" % r, 320, BF); sb("br%d" % r, 640, BF); sb("bt%d" % r, 640, BF)
-        s["er%d" % r] = ("sbuf", [128, 20, 32], BF); sb("et%d" % r, 640, BF)
-        s["tr%d" % r] = ("sbuf", [128, 20, 32], F32); sb("gt%d" % r, 640, F32)
-        sb("fs%d" % r, 1140, F32); sb("is%d" % r, 340, I32)
-        sb("us%d" % r, 60, U16)
+    sb("ll", 16 * R, U16); sb("lr", 16 * R, U16); sb("um", 16 * R, U16); sb("ul", 40, U16)
     return s
 
 
@@ -92,7 +97,7 @@ def _hand_on(g, core, T, topo):
             n += ne
         if k == 0:
             g.wait_ge(T.sem["rl%d" % r], near)
-            g.remote_dma(T["ll%d" % r][:], T["rl%d" % r][:], T.sem["la%d" % r], T.sem.loc, pid, rid, m)
+            g.remote_dma(T.ll[:, 16 * r:16 * r + 10], T.lr[:, 16 * r:16 * r + 10], T.sem["la%d" % r], T.sem.loc, pid, rid, m)
             n += ne
     g.wait_ge(T.sem.loc, n)
 
@@ -124,11 +129,16 @@ def rank_program(g, core, T, topo):
         q = Q[e]
         f = {"cp": lambda: q.tensor_copy(*a), "tt": lambda: q.tensor_tensor(*a), "ts": lambda: q.tensor_scalar(*a),
              "ms": lambda: q.memset(*a), "tp": lambda: q.transpose(*a), "qz": lambda: q.quantize_mx(*a),
-             "scan": lambda: q.tensor_tensor_scan(*a), "act": lambda: q.activation(*a, **k), "mm": lambda: q.matmul_mx(*a),
-             "iota": lambda: q.iota(*a, **k), "sel": lambda: q.affine_select(*a)}[name]
+             "scan": lambda: q.tensor_tensor_scan(*a, 0.0, A.mult, A.add), "act": lambda: q.activation(*a, **k),
+             "mm": lambda: q.matmul_mx(*a), "iota": lambda: q.iota(*a, **k), "sel": lambda: q.affine_select(*a)}[name]
         f().then_inc(T.sem[e + "q"], 1)
         cnt[e] += 1
         return (e + "q", cnt[e])
+
+    def copy(e, toks, out, in_, scale=None):
+        if e == "s":
+            return op("s", toks, "act", out, in_, AF.Copy, **({} if scale is None else {"scale": scale}))
+        return op("v", toks, "cp", out, in_) if scale is None else op("v", toks, "ts", out, in_, scale, None, A.mult)
 
     def dma(e, toks, out, in_, sem):
         need(e, toks)
@@ -139,11 +149,20 @@ def rank_program(g, core, T, topo):
     banks = [T["pk%d" % k] for k in range(8)]
     readers = [[] for k in range(8)]
     turn = [0]
+    held = set()
 
     def bank():
+        while turn[0] % 8 in held:
+            turn[0] += 1
         k = turn[0] % 8
         turn[0] += 1
+        held.add(k)
         return k
+
+    def read(k, o):
+        readers[k].append(o)
+        held.discard(k)
+        return o
 
     def mm(toks, k, n, lc, ls, b, rc, rs, a, start=True, stop=True):
         w = [toks, readers[k]] if start else [toks]
@@ -152,97 +171,87 @@ def rank_program(g, core, T, topo):
         return op("t", w, "mm", banks[k][:, 0:n], lc[:, 128 * b:128 * b + 128], ls[:, 128 * b:128 * b + 128],
                   rc[:, a:a + n], rs[:, a:a + n], start, stop)
 
-    ci, cf = T.ci, T.cf
-
-    def icol(k):
-        return ci[:, k:k + 1]
-
-    def col(k):
-        return cf[:, k:k + 1]
-
-    ld_nx = dma("y", [], T.nt[:], T.nx[:], "ld_nx")
-    ld_al = dma("s", [], T.ali[:], T.al[:], "ld_al")
-    ld_x = [dma("y", [], T.x0[:, 0:640], T.x[:, 0:640], "ld_x0")]
+    ld_nx = dma("s", [], T.nt[:], T.nx[:], "ld_nx")
     ld_u = dma("y", [], T.ub[:], T.u[:], "ld_u")
-    ld_x.append(dma("y", [], T.x0[:, 640:1280], T.x[:, 640:1280], "ld_x1"))
+    ld_x = [dma("y", [], T.x0[:, 640 * h:640 * h + 640], T.x[:, 640 * h:640 * h + 640], "ld_x%d" % h) for h in range(2)]
+    ld_al = dma("y", [], T.ali[:], T.al[:], "ld_al")
 
     fl = {"allow_small_or_imprecise_dtypes": True}
+    ct, ci, ln, rc, rt = T.ct, T.ci, T.ln, T.rc, T.rt
     v_c64 = op("v", [], "ms", T.c64[:], 64.0)
     v_eb = op("v", [], "ms", T.eb[:], 0.0)
-    g_p = op("g", [], "iota", icol(0), [[0, 1]], 0, 1)
-    g_eb = op("g", [v_eb], "sel", T.eb[:, 3:515:4], T.c64[:, 0:128], [[-1, 128]], A.is_equal, 0.0, 0, 1)
-    g_ul = op("g", [], "iota", ci[:, 8:16], [[16, 8]], 0, 0)
-    g_rt = op("g", [], "iota", ci[:, 16:28], [[4, 4], [32, 3]], 0, 0)
-    LANE, ODD, R8, T8 = 1, 2, 3, 4
-    for k, (sh, m) in enumerate([(0, 15), (4, 1), (0, 7), (3, 1)]):
-        o = op("v", [g_p], "ts", icol(1 + k), icol(0), sh, m, A.arith_shift_right, A.bitwise_and)
-    cols = op("v", [o], "cp", cf[:, 1:5], ci[:, 1:5])
-    KL, UP0, UP1, ES, KO, TH = 6, 7, 8, 9, 10, 11
+    g_ul = op("g", [], "iota", ci[:], [[16, 8]], 0, 0)
+    g_ac = g_eb = op("g", [v_eb], "sel", T.eb[:, 3:515:4], T.c64[:, 0:128], [[-1, 128]], A.is_equal, 0.0, 0, 1)
+    for q in range(4):
+        g_ac = op("g", [g_ac], "iota", T.ac[32 * q:32 * q + 32, 0:6, :], [[128, 3], [0, 2], [1, 4]], 0, 4, **fl)
+    g_th = op("g", [g_ac], "iota", T.th[:], [[0, 10], [1, 8]], 0, 0, **fl)
 
-    def fill_s(out, n, c, toks=()):
+    def fill(out, n, c, toks=()):
         return op("s", [v_c64, list(toks)], "act", out, T.c64[:, 0:n], AF.Copy, scale=c / 64.0)
-
-    def line(k, src, a, b):
-        return op("s", [cols], "act", col(k), col(src), AF.Identity, scale=a, bias=b)
-    fill_s(T.hn[:, 0:192], 192, 4.0)
-    o = fill_s(T.hn[:, 192:384], 192, 2.0)
-    fill_s(T.un[:, 160:176], 16, 32.0)
-    line(12, T8, -192.0, 575.0)
-    line(13, T8, 193.0, -381.0)
-    line(19, T8, 193.0, -575.0)
-    line(21, T8, -192.0, 591.0)
-    s1 = line(14, LANE, 16.0, -223.0)
-    line(22, ODD, -1.0, 1.0)
-    line(ES, LANE, -14.0, 211.0)
-    s2 = line(KO, ODD, -SAME, SAME)
-    fill_s(T.nf[:, 160:176], 16, 0.0)
-    fill_s(T.hn[:, 2:192:4], 48, 64.0, [o])
-    fill_s(T.hn[:, 194:384:4], 48, 8.0)
-    v_hn = fill_s(T.hn[:, 0:384:4], 96, 0.0)
-    fill_s(T.kx[:, 1:240:2], 120, SAME)
-    seg = fill_s(T.sg[:, 0:500:5], 100, 0.0)
-    op("v", [cols], "ts", col(KL), col(R8), 0.0, None, A.is_equal)
-    op("v", [], "ts", col(15), col(LANE), 14.0, None, A.is_lt)
-    op("v", [], "ts", col(TH), col(LANE), 0.0, 1e29, A.is_equal, A.mult)
 
     def const_tile(b):
         return op("v", [g_eb], "qz", T.ec[:, 128 * b:128 * b + 128], T.es[:, 128 * b:128 * b + 128], T.eb[:, 3 - b:515 - b])
-    vE = [const_tile(0)]
+    ES, EB, UL = T.cf[0:32, 0:1], T.cf[0:32, 32:33], T.cf[:, 64:65]
+    op("v", [], "ms", ct[:, 0:64], 0.0)
+    o = op("v", [], "ms", ct[:, 64:96], 16.0)
+    for e in range(4):
+        op("v", [], "ms", T.kw[:, :, :, e], 16.0 ** (3 - e))
+    op("v", [], "ms", T.y30[:], 0)
+    op("v", [], "ms", T.y31[:], 0)
+    fill(T.cb[:, :, 80:96], 32, 0.0)
+    s1 = fill(T.nf[:, :, 80:96], 32, 0.0)
+    for a, b, c in [(64, 67, 1.0), (67, 70, 17.0), (80, 83, 1.0), (83, 86, 17.0), (16, 19, 2.0), (19, 22, -1.0), (46, 48, 9.0),
+                    (48, 49, -1.0), (49, 50, -2.0), (50, 51, -3.0), (54, 57, 9.0)]:
+        s0 = fill(ct[:, a:b], b - a, c, [o])
+    fill(T.ac[:, 6:12, :], 24, 0.0)
+    fill(T.fl[:, 210:224], 14, 160.0)
+    fill(T.fm[:], 224, 160.0)
+    s2 = fill(ln[:, :, :, 0:6], 288, 0.0)
+    vE = [const_tile(b) for b in range(4)]
+    op("g", [s2], "iota", T.fl[:, 0:200], [[8, 10], [0, 4], [1, 5]], 0, 0, **fl)
+    op("g", [], "iota", T.fl[:, 200:210], [[8, 10]], LA - LD, 0, **fl)
+    op("g", [], "iota", T.fm[:, 4:200:5], [[8, 10], [1, 4]], 80 + LN - 8, 0, **fl)
+    g_fl = op("g", [], "iota", T.fm[:, 200:210], [[8, 10]], 80 + LA - 8, 0, **fl)
 
-    def dup(dst, src, toks, h, n=20):
-        op("v", [toks], "cp", dst[:, 20 + 20 * h:20 + 20 * h + n:2], src)
-        return op("v", [], "cp", dst[:, 21 + 20 * h:20 + 20 * h + n:2], src)
-
-    nt, ni, un, nf, ru, rw, tw = T.nt, T.ni, T.un, T.nf, T.ru, T.rw, T.tw
-    op("v", [ld_nx], "ts", ni[:, 0:160], nt[:], 1.0 / 512, 32.0 - 159.5 / 512, A.mult, A.add)
-    o = op("v", [], "ts", ni[:, 160:320], nt[:], 5, 112, A.arith_shift_right, A.bitwise_and)
-    n1 = op("v", [], "ts", ni[:, 320:480], nt[:], 511, None, A.bitwise_and)
-    op("v", [s1], "ts", col(20), col(R8), 4.0, col(21), A.min, A.add)
-    o = op("v", [o], "tt", un[:, 0:160], ni[:, 0:160], ni[:, 160:320], A.max)
-    n2 = op("v", [n1], "cp", nf[:, 0:160], ni[:, 320:480])
-    c16 = op("v", [], "ts", col(16), col(R8), 4.0, col(12), A.min, A.add)
-    op("v", [o, v_hn], "tp", ru[:, 0:96], un[:, 0:96])
-    t1 = op("v", [], "tp", ru[:, 96:192], un[:, 80:176])
-    u4 = op("s", [t1], "act", ru[:, 192:384], ru[:, 0:192], AF.Square, bias=-32.0)
-    qx = [op("v", [ld_x[0]], "qz", T.qx0[:, 0:H], T.sx0[:, 0:H], T.x0[:, 0:640])]
-    op("v", [n2], "tp", rw[:, 384:480], nf[:, 0:96])
-    n3 = op("v", [], "tp", rw[:, 480:576], nf[:, 80:176])
-    op("v", [c16], "ts", col(17), col(13), col(KL), col(16), A.mult, A.add)
-    v_ul = op("v", [g_ul], "ts", T.uls[:], ci[:, 8:16], col(15), col(14), A.mult, A.max)
+    nt, ni, nf, tw = T.nt, T.ni, T.nf, T.tw
+    c1 = op("v", [ld_nx], "ts", T.cb[:, :, 0:80], nt[:], 1.0 / 512, 127.8125, A.mult, A.add)
+    n1 = op("v", [], "ts", ni[:], nt[:], 511, None, A.bitwise_and)
+    cols = op("v", [s0, g_ul], "tp", T.cf[:], ct[:])
+    c3 = op("v", [c1, s1], "tp", rc[:], T.cb[:])
+    n2 = op("v", [n1], "cp", nf[:, :, 0:80], ni[:])
+    y1 = op("s", [c3], "act", T.w1[:], rc[:, 0:12:2], AF.Identity, scale=4.0, bias=-392.0)
+    o = op("v", [], "cp", T.uls[:], ci[:, 0:8])
     qu = op("v", [ld_u], "qz", T.uq[:], T.up[:], T.ub[:])
+    c4 = op("v", [c3], "tt", T.kc[:], rc[:, 1:12:2], T.kw[:], A.mult)
+    n3 = op("v", [n2], "tp", rt[:], nf[:])
+    v_ul = op("v", [o, cols], "cp", T.uls[:, 1:2], UL)
+    y2 = op("v", [y1], "tt", T.w2[:], T.w1[:], rc[:, 0:12:2], A.max)
+    y3 = op("s", [y2], "act", T.w1[:], T.w2[:], AF.Square, bias=-128.0)
     v_u = [op("s", [qu, v_ul], "act", T.up2[:], T.up[:].indirect(T.uls[:]), AF.Copy)]
-    k1 = op("v", [t1, v_hn], "scan", rw[:, 0:192], T.hn[:, 0:192], ru[:, 0:192], 0.0, A.mult, A.add)
-    op("v", [n3], "tt", rw[:, 576:672], rw[:, 480:576], rw[:, 384:480], A.subtract)
-    c18 = op("v", [], "ts", col(18), col(19), col(KL), col(20), A.mult, A.add)
-    k2 = op("v", [u4], "scan", rw[:, 192:384], T.hn[:, 192:384], ru[:, 192:384], 0.0, A.mult, A.add)
-    op("v", [k1], "tt", rw[:, 0:96:4], rw[:, 99:192:4], rw[:, 3:96:4], A.subtract)
-    op("v", [], "ts", rw[:, 1:96:4], rw[:, 3:96:4], -32.0 * 1285, None, A.add)
-    op("v", [g_rt, c18], "ts", T.rt[:, 0:24:2], ci[:, 16:28], col(17), None, A.add)
-    v_rt = op("v", [], "ts", T.rt[:, 1:24:2], ci[:, 16:28], col(18), None, A.add)
-    k3 = op("v", [k2], "tt", rw[:, 194:288:4], rw[:, 291:384:4], rw[:, 195:288:4], A.subtract)
-    k4 = op("s", [k3, v_rt], "act", T.gg[:], rw[:].indirect(T.rt[:]), AF.Copy)
-    v_u.append(op("v", [qu, v_ul], "cp", T.uq2[:].bitcast(dt.uint32), T.uq[:].bitcast(dt.uint32).indirect(T.uls[:])))
+    y4 = op("s", [y3, s2], "act", ln[:, 0:12:2, :, LY:LY + 4], T.w1[:], AF.Square, scale=0.25)
+    c5 = op("v", [c4], "tt", T.kc[:, 3:6], T.kc[:, 3:6], T.kc[:, 0:3], A.subtract)
+    n4 = op("v", [n3], "tt", rt[:, 6:12], rt[:, 6:12], rt[:, 0:6], A.subtract)
+    v_u.append(op("v", [v_ul], "cp", T.uq2[:].bitcast(dt.uint32), T.uq[:].bitcast(dt.uint32).indirect(T.uls[:])))
+    qx = [op("v", [ld_x[0]], "qz", T.qx0[:, 0:H], T.sx0[:, 0:H], T.x0[:, 0:640])]
+    k1 = op("v", [c5], "tt", T.kp[:], T.kc[:, :, :, 0:4:2], T.kc[:, :, :, 1:4:2], A.add)
+    op("s", [n4], "act", ln[:, :, :, LD + 4], rt[:, :, :, 3], AF.Copy)
+    op("s", [], "act", ln[:, 0:12:2, :, LN:LN + 4], rt[:, 0:12:2], AF.Copy)
+    k3 = op("s", [g_ac], "act", ln[:, :, :, LA], T.ac[:], AF.Copy)
+    op("v", [n4, s2], "tt", ln[:, :, :, LD + 1:LD + 4], rt[:, :, :, 0:3], rt[:, :, :, 1:4], A.subtract)
     qx.append(op("v", [ld_x[1]], "qz", T.qx0[:, H:C], T.sx0[:, H:C], T.x0[:, 640:1280]))
+    op("v", [g_ac], "tt", ln[:, :, :, LD], T.ac[:], rt[:, :, :, 0], A.subtract)
+    for e in range(4):
+        op("v", [k1], "tt", ln[:, 1:12:2, :, LK - 16 + e], T.kp[:, :, :, 0], T.kp[:, :, :, 1], A.add)
+    y5 = op("v", [y4], "tt", ln[:, 6:12:2, :, LY:LY + 4], ln[:, 6:12:2, :, LY:LY + 4], ln[:, 0:6:2, :, LY:LY + 4], A.subtract)
+    for a in range(0, 640, 256):
+        v_bw = fill(T.bw[:, a:min(a + 256, 640):2], min(128, (640 - a) // 2), 0.0)
+    for h, n in enumerate(NB):
+        fill(T["se%d" % h][:, 8 * n:8 * n + 8], 8, 0.0)
+        fill(T["ao%d" % h][:, 40 + 120 * h:48 + 120 * h], 8, 0.0)
+        fill(T["do%d" % h][:], 8 * n, 0.0)
+        fill(T["mp%d" % h][:, 0:20 * n:5], 4 * n, 0.0)
+    fill(T.pa[:, 4:512:8], 64, 0.0)
+    s3 = fill(T.th[:, 0:80:8], 10, -9.0, [g_th])
 
     def send_codes(r, h, tok):
         need("g", [tok])
@@ -265,176 +274,159 @@ def rank_program(g, core, T, topo):
         k = bank()
         return k, mm([tok, v_u], k, H, T.uq2, T.up2, 0, T["qx%d" % r], T["sx%d" % r], H * h)
 
-    def bits(r, h, kt):
+    def signs(h, kt):
         k, t = kt
-        o = op("v", [t], "ts", T["bw%d" % r][:, H * h:H * h + H], banks[k][:, 0:H], col(TH), None, A.is_gt)
-        readers[k].append(o)
+        return read(k, op("v", [t], "ts", T.bw[:, C * h + 1:C * h + C:2], banks[k][:, 0:H], 0.0, None, A.is_gt))
+
+    def choose(h, toks):
+        return op("v", toks, "scan", T.cw[:, C * h:C * h + C], T.bw[:, C * h:C * h + C], tw[:, C * h:C * h + C])
+
+    def edges(h, tok):
+        er, src = T["er%d" % h], T.bw[0:32, C * h + 1:C * h + C:2]
+        for out in ([er[0:32, :, 0:16], er[0:32, :, 16:32]] if h else [er[0:32]]):
+            o = op("s", [tok, cols], "act", out, src, AF.Identity, scale=ES, bias=EB)
         return o
 
-    def unpack(qc, qs, toks, a=0, n=C):
-        ks = [bank() for b in range(4)]
-        return [(ks[b], mm([toks, vE[b]], ks[b], n, T.ec, T.es, b, qc, qs, a)) for b in range(4)]
+    def turn_edges(h, tok):
+        return op("v", [tok], "tp", T["et%d" % h][0:32], T["er%d" % h][0:32])
 
-    def unpack_copy(d, ps, a=0, n=C):
-        for b in range(4):
-            k, t = ps[b]
-            o = op("s", [t], "act", d[:, C * b + a:C * b + a + n], banks[k][:, 0:n], AF.Copy, scale=INV)
-            readers[k].append(o)
+    def first_marks(h, tok):
+        et = T["et%d" % h]
+        return op("v", [tok], "tt", T["me%d" % h][0:32], et[0:32, :, LH:LH + 8], et[0:32, :, LE:LE + 8], A.is_lt)
+
+    def odd_list(r, h, src, tok):
+        for out in ([T.ul[:, 10:30:2], T.ul[:, 11:30:2]] if h else [T.ul[:, 0:10]]):
+            o = op("v", [tok], "ts", out, src, 2.0, 1.0, A.mult, A.add)
         return o
 
-    def edge_rows(r, h, tok):
-        for a in (0, 16):
-            o = op("v", [tok, s2], "ts", T["er%d" % r][:, 10 * h:10 * h + 10, a:a + 16], T["bw%d" % r][:, H * h:H * h + H],
-                   col(ES), 1.0, A.mult, A.add)
-        return o
+    def unpack(qc, qs, toks, bs=range(4)):
+        ks = {b: bank() for b in bs}
+        return {b: (ks[b], mm([toks, vE[b]], ks[b], C, T.ec, T.es, b, qc, qs, 0)) for b in bs}
 
-    def turn_edges(r, h, tok):
-        return op("v", [tok], "tp", T["et%d" % r][:, C * h:C * h + C], T["er%d" % r][:, 10 * h:10 * h + 10, :])
-
-    def turn_tables(r, h, tok):
-        return op("v", [tok], "tp", T["gt%d" % r][:, C * h:C * h + C], T["tr%d" % r][:, 10 * h:10 * h + 10, :])
-
-    def table_lookup(r, h, e, off, tok):
-        out, win = T.tq[:, H * h:H * h + H], tw[:].indirect(off)
-        return op("v", [tok, k5], "cp", out, win) if e == "v" else op("s", [tok, k5], "act", out, win, AF.Copy)
-
-    def table_twice(r, h, e, tok):
-        for s in range(2):
-            out, src = T["tr%d" % r][:, 10 * h:10 * h + 10, 16 * s:16 * s + 16], T.tq[:, H * h:H * h + H]
-            o = op("v", [tok], "ts", out, src, col(UP0 + s), None, A.mult) if e == "v" else \
-                op("s", [tok], "act", out, src, AF.Copy, scale=col(UP0 + s))
-        return o
-
-    def signs_by_list(r, h, e=None):
-        a, b = (18, 40) if h else (0, 18)
-        out, win = T["br%d" % r][:, 16 * a:16 * b], T["bw%d" % r][:].indirect(T["us%d" % r][:, 20 + a:20 + b])
-        return op("s", [bt_, lists[1]], "act", out, win, AF.Copy) if h or e else op("v", [bt_, lists[0]], "cp", out, win)
-
-    def keep_old(r, a, n, src):
-        return op("v", [], "cp", T["fs%d" % r][:, 424 + 5 * a:420 + 5 * (a + n):5], src)
+    def unpack_copy(d, ps, es):
+        return [read(ps[b][0], copy(e, [ps[b][1]], d[:, C * b:C * b + C], banks[ps[b][0]][:, 0:C], INV)) for b, e in zip(ps, es)]
 
     sc = [scores(0, 0, qx[0]), scores(0, 1, qx[1])]
     send_codes(0, 0, qx[0])
     send_codes(0, 1, qx[1])
     g_iw = op("g", [], "iota", T.iw[:], [[1, 320]], 0, 0, **fl)
-    lists = [dup(T.us0, T.ali[:], [ld_al], 0, 40)] * 2
-    op("v", [s2], "ts", col(UP0), col(22), col(KL), None, A.max)
-    op("v", [], "ts", col(UP1), col(ODD), col(KL), None, A.max)
-    l0 = op("v", [], "cp", T.l0[:], T.ali[:])
-    old = keep_old(0, 0, 20, T.ali[:])
-    bt_ = [bits(0, 0, sc[0]), bits(0, 1, sc[1])]
-    p1 = signs_by_list(0, 0, "s")
-    p2 = signs_by_list(0, 1)
-    for m in range(4):
-        k5 = op("v", [k4], "tp", tw[:, m:384:4], T.gg[:, 96 * m:96 * m + 96])
+    copy("s", [g_fl], T.fw[:, 0:14, 0:16], T.fm[:])
+    copy("s", [], T.fw[:, 0:14, 16:32], T.fl[:])
+    copy("s", [], T.fw[:, 14:21, 0:16], T.fl[:, 0:112])
+    j = copy("s", [], T.fw[:, 14:21, 16:32], T.fl[:, 0:112])
+    lk = [odd_list(0, h, T.ali[:, 10 * h:10 * h + 10], ld_al) for h in range(2)]
+    for m in range(8):
+        k5 = op("v", [y5, k3], "tp", tw[:, (m ^ 1):768:8], ln[:, 6 * (m % 2):6 * (m % 2) + 6, m // 2, :])
+    sg = [signs(0, sc[0]), signs(1, sc[1])]
+    er = [edges(0, sg[0]), None]
+    ch = [choose(0, [k5, sg[0], v_bw]), None]
 
     for r in range(R):
         rn = r + 1
-        us, fs, ints = T["us%d" % r], T["fs%d" % r], T["is%d" % r]
-        br, btb, gt, et = T["br%d" % r], T["bt%d" % r], T["gt%d" % r], T["et%d" % r]
+        us, ul = [T.ul[:, 30:40], T.um[:, 16 * r:16 * r + 10]], T.ul
+        qa = [("qa%d%d" % (r, h), 3 * far_engines) for h in range(2)]
+        qp, sp, fp = T["qp%d" % r], T["sp%d" % r], T["fp%d" % r]
+        er[1] = edges(1, sg[1])
+        ch[1] = choose(1, [sg[1]])
         if r == 0:
-            er = [edge_rows(0, h, bt_[h]) for h in range(2)]
-            trow = {h: table_twice(0, h, "s", table_lookup(0, h, "v", T.l0[:, 10 * h:10 * h + 10], l0)) for h in (1, 0)}
-            e0 = turn_edges(0, 0, er[0])
-            e1 = turn_edges(0, 1, er[1])
-            v_bt = op("v", [p1, p2], "tp", btb[:], br[:])
-            tab = [turn_tables(0, h, trow[h]) for h in (1, 0)]
+            j = op("v", [j], "tp", T.ft[:], T.fw[:])
+            e0 = turn_edges(0, er[0])
+        gm = [copy("v", [ch, lk], T.gg1[:, 0:H], T.cw[:].indirect(ul[:, 10:20])),
+              copy("s", [ch, lk], T.gg1[:, H:C], T.cw[:].indirect(ul[:, 20:30]))]
+        gs = copy("s", [], T.gg0[:], T.cw[:].indirect(ul[:, 0:10]))
+        e1 = turn_edges(1, er[1])
+        if r == 0:
+            j = op("v", [j], "cp", T.rl[:, 0:21], T.ft[:, 0:672:32])
+            first_marks(0, e0)
             dma("y", [ld_x], T.wq[:].bitcast(dt.uint8), T.wc[:], "ld_w")
             ld_w = dma("y", [], T.wp[:], T.ws[:], "ld_w")
             ld_v = dma("y", [ld_w], T.vb[:], T.v[:], "ld_v")
-        else:
-            er[1] = edge_rows(r, 1, bt_[1])
-            p1 = signs_by_list(r, 0)
-            p2 = signs_by_list(r, 1)
-            e1 = turn_edges(r, 1, er[1])
-            v_bt = op("v", [p1, p2], "tp", btb[:], br[:])
-        kx, sg, dv = T.kx, T.sg, fs[:, 420:520]
-        far = [fs[:, 520 + 20 * e:540 + 20 * e] for e in range(4)] + [fs[:, 424:520:5]]
-        got = [fs[:, 744 + 100 * e:840 + 100 * e:5] for e in range(4)] + [fs[:, 424:520:5]]
-        st = op("v", [e0, e1], "tt", fs[:, 80:100], et[:, 14:640:32], et[:, 15:640:32], A.mult)
-        k3 = op("v", [v_bt, tab, seg], "scan", kx[96:128, 0:80], btb[0:32, 0:640:8], gt[0:32, 0:640:8], 0.0, A.mult, A.add)
-        ks = op("v", [], "scan", fs[:, 0:80], btb[:, 0:640:8], gt[:, 0:640:8], 0.0, A.mult, A.add)
-        k2 = op("s", [ks], "act", kx[64:128, 81:160:2], fs[0:64, 1:80:2], AF.Copy)
-        k1 = [op("s", [], "act", kx[32 * q + 32:32 * q + 64, 161:240:2], fs[32 * q:32 * q + 32, 1:80:2], AF.Copy) for q in range(3)]
-        kd = [k3, k2, k1]
-        w = {k: [] for k in "nkdmcfpq"}
+        tok = [{"tp": gs}, {"tp": gm}]
+        count = [{}, {}]
 
-        def side(k, e):
-            if k == "n":
-                o = op("v", [], "scan", fs[:, 100 + 80 * e:180 + 80 * e], btb[:, 0:640:8], gt[:, 1 + e:640:8], 0.0, A.mult, A.add)
-            if k == "d":
-                o = op("v", [w["n"]], "tt", fs[:, 520:600], fs[:, 101:420:4], fs[:, 103:420:4], A.add)
-            if k == "c":
-                o = op("v", [w["d"], old], "tt", fs[:, 420 + e:520:5], far[e], far[e + 1], A.subtract)
-            if k == "k":
-                o = op("v", [ks, s2], "ts", ints[:, 240:260], fs[:, 1:80:4], col(ODD), col(KO), A.mult, A.add)
-            if k == "m":
-                o = op("v", [w["k"]], "ts", ints[:, 260 + 20 * e:280 + 20 * e], ints[:, 240:260], 5 - EA[e], 1285,
-                       A.arith_shift_right, A.bitwise_and)
-            if k == "f":
-                o = op("v", [w["m"]], "ts", sg[:, 101 + e:500:5], ints[:, 260:340], float(4 ** EA[e + 1]) if e < 3 else 0.0, None,
-                       A.not_equal)
-            if k == "p":
-                o = op("v", [w["f"], w["c"]], "scan", fs[:, 740 + 100 * e:840 + 100 * e], sg[:, 100 + 100 * e:200 + 100 * e], dv,
-                       0.0, A.mult, A.add)
-            if k == "q":
-                o = op("v", [w["p"]], "tt", fs[:, 420 + e:520:5], got[e], got[e + 1], A.subtract)
-            w[k].append(o)
+        def step(h, k):
+            n, w, i = NB[h], tok[h], count[h].get(k, 0)
+            count[h][k] = i + 1
+            gt, me, se, pb, do = [T["%s%d" % (s, h)] for s in ("gt", "me", "se", "pb", "do")]
+            y3, a4, ao, mp = [T["%s%d" % (s, h)] for s in ("y3", "a4", "ao", "mp")]
+            a, b = 32 * i, 32 * i + 32
+            if k == "tp":
+                o = w["go"] = op("v", [w["tp"]], "tp", gt[:], T["gg%d" % h][:])
+                p = copy("s", [o], ao[:, 0:8 * n], gt[:, :, 16 + LD:24 + LD])
+                if h:
+                    p = copy("s", [], ao[:, 80:160], gt[:, :, 8:16])
+                else:
+                    copy("s", [], T.ae[:], gt[:, :, LD:LD + 8])
+                w["a4"] = copy("s", [p, j], a4[:], ao[:].indirect(T.rl[:, 0:14] if h else T.rl[:, 14:21]))
+            if k == "mu":
+                w["go"] = op("v", [w["go"]], "tt", T["tm%d" % h][:], gt[:, :, LY:LY + 4], gt[:, :, LK:LK + 4], A.mult)
+            if k == "mk":
+                w["go"] = op("v", [w["go"]], "ts", y3[:, :, 1:5], T["tm%d" % h][:], 8, 7, A.arith_shift_right, A.bitwise_and)
+            if k == "m0":
+                first_marks(h, e1)
+            if k == "df":
+                w["go"] = op("v", [w["go"]], "tt", T["dq%d" % h][:], y3[:, :, 0:8], y3[:, :, 1:9], A.subtract)
+            if k == "sc":
+                w["go"] = op("v", [w["go"]], "scan", se[b:b + 32, 0:8 * n], me[a:b], T["dq%d" % h][a:b])
+            if k == "ne":
+                w["go"] = op("v", [w["go"], s3], "tt", me[b:b + 32], se[b:b + 32, 3:8 * n + 3], T.th[b:b + 32, 0:8 * n], A.is_lt)
+            if k == "mp":
+                w["mp"] = op("v", [s3], "ts", mp[:, 1 + i:20 * n:5], gt[:, :, LY:LY + 4], 16.0 ** (i - 1), None, A.is_lt)
+            if k == "pb":
+                w["pb"] = op("v", [w["mp"], w["a4"]], "scan", pb[:], mp[:], a4[:, 0:20 * n])
+            if k == "do" and i < 4:
+                old = pb[:, 5 * i - 1:20 * n:20] if i else a4[:, 200:210] if h else gt[:, :, 16 + LA]
+                w["do"] = op("v", [w["pb"]], "tt", do[:, i:8 * n:8], old, pb[:, 5 * i + 4:20 * n:20], A.subtract)
+            if k == "do" and i == 4:
+                w["do"] = op("v", [w["pb"]], "cp", do[:, 4:8 * n:8], pb[:, 19:20 * n:20])
+            if k == "pk" and h:
+                w["go"] = op("v", [w["go"], w["do"]], "scan", T.pm[:], me[:], do[:])
+            if k == "pk" and not h:
+                op("v", [w["go"]], "scan", T.pa[:, 0:40], me[:], T.ae[:])
+                w["go"] = op("v", [w["do"]], "scan", T.pa[:, 256:296], me[:], do[:])
+            if k == "t1":
+                w["go"] = op("v", [w["go"]], "tp", T.xt[:], T.pa[:, 4:512:8])
+            if k == "t2":
+                op("v", [w["go"]], "tp", T.lt[:, 0:64:2], T.xt[:, :, 0:16])
+                w["go"] = op("v", [], "tp", T.lt[:, 1:64:2], T.xt[:, :, 16:32])
+            if k == "cv":
+                w["go"] = op("v", [w["go"]], "cp", us[h], T.pm[:, 4:80:8] if h else T.lt[:, 0:10])
 
-        def gap(j):
-            for k in WAITS[j]:
-                side(k, len(w[k]))
-            if r == 0 and j in (5, 10, 11):
-                vE.append(const_tile(len(vE)))
-        sv, at = fs[:, 80:100], 0
-        gap(0)
-        for j in range(6):
-            tv = ints[:, at:at + 20]
-            a = 80 * (j // 2) + 1 + 2 * (j % 2)
-            st = op("v", [st, kd[j // 2]], "tt", tv, kx[:, a:80 * (j // 2) + 80:4], sv, A.mult)
-            gap(2 * j + 1)
-            sv = ints[:, at + 20:at + 40]
-            st = op("v", [st], "ts", sv, tv, 15, 0x33, A.arith_shift_right, A.bitwise_and) if j % 2 else \
-                op("v", [st], "ts", sv, tv, 0xA0A0, None, A.bitwise_and)
-            gap(2 * j + 2)
-            at += 40
-        qa = [("qa%d%d" % (r, h), 3 * far_engines) for h in range(2)]
-        tF = unpack_copy(T["f%d" % r], unpack(T["qx%d" % r], T["sx%d" % r], [qx]))
-        if r > 0:
-            unpack_copy(T["fp%d" % r], unpack(T["qp%d" % r], T["sp%d" % r], [qa[0]], 0, H), 0, H)
-        hs = [op("v", [st], "ts", sg[:, e:100:5], sv, float(2 ** EA[e]) if e < 4 else 0.0, None, A.not_equal) for e in range(1, 5)]
-        st = op("v", [hs, w["q"]], "scan", fs[:, 620:720], sg[:, 0:100], dv, 0.0, A.mult, A.add)
-        ls = op("v", [st], "cp", us[:, 0:20], fs[:, 624:720:5])
-        need("g", [ls])
-        rid, pid = topo.addr(rel[0], core)
-        g.remote_dma(T["rl%d" % r][:], us[:, 10:20], T.sem["rl%d" % r], T.sem.loc, pid, rid, topo.mask(core, rel[0]))
-        loc[0] += len(topo.engines(core, rel[0]))
+        for n, line in enumerate(ORDER):
+            for k in line.split():
+                step(int(k.isupper()), k.lower())
+                if k == "tp":
+                    tF = unpack_copy(T["f%d" % r], unpack(T["qx%d" % r], T["sx%d" % r], [qx]), "ssss")
+                    tP = unpack_copy(fp, unpack(qp, sp, [qa]), "ssss")
+                if k == "CV":
+                    need("g", [tok[1]["go"]])
+                    rid, pid = topo.addr(rel[0], core)
+                    g.remote_dma(T.lr[:, 16 * r:16 * r + 10], us[1], T.sem["rl%d" % r], T.sem.loc, pid, rid, topo.mask(core, rel[0]))
+                    loc[0] += len(topo.engines(core, rel[0]))
+        ls = tok[0]["go"]
 
-        def make(h, toks, off, F, between=None):
+        def make(h, toks, off, F, between):
             z, q, s, o = T["z%d" % r], T["qz%d" % r], T["sz%d" % r], []
             for b in range(4):
-                win, out = F[:, 320 * b:320 * b + 320].indirect(off), z[:, 640 * h + b:640 * h + 640:4]
-                o.append(op("v", [toks], "cp", out, win) if b < 2 else op("s", [toks], "act", out, win, AF.Copy))
-            if between:
-                between()
+                o.append(copy("vsvs"[b], [toks], z[:, 640 * h + b:640 * h + 640:4], F[:, 320 * b:320 * b + 320].indirect(off)))
+            more = between()
             zq = op("v", [o], "qz", q[:, H * h:H * h + H], s[:, H * h:H * h + H], z[:, 640 * h:640 * h + 640])
             ps = []
             for b in range(4):
                 k = bank()
                 mm([zq, ld_w], k, H, T.wq, T.wp, b, q, s, H * h, True, False)
                 ps.append((k, mm([zq], k, H, T.ec, T.es, b, q, s, H * h, False, True)))
-            return ps
+            return ps, more
 
-        def renew(h, b, ps, e):
-            k, t = ps[b]
-            out = T["x%d" % rn][:, 640 * h + b:640 * h + 640:4]
-            o = op("v", [t], "ts", out, banks[k][:, 0:H], INV, None, A.mult) if e == "v" else \
-                op("s", [t], "act", out, banks[k][:, 0:H], AF.Copy, scale=INV)
-            readers[k].append(o)
+        def renew(h, ps, es):
+            o = []
+            for b in range(4):
+                k, t = ps[b]
+                o.append(read(k, copy(es[b], [t], T["x%d" % rn][:, 640 * h + b:640 * h + 640:4], banks[k][:, 0:H], INV)))
             return o
 
-        def requant(h, toks):
-            return op("v", [toks], "qz", T["qx%d" % rn][:, H * h:H * h + H], T["sx%d" % rn][:, H * h:H * h + H],
+        def requant(h, o):
+            return op("v", [o], "qz", T["qx%d" % rn][:, H * h:H * h + H], T["sx%d" % rn][:, H * h:H * h + H],
                       T["x%d" % rn][:, 640 * h:640 * h + 640])
 
         def outputs(h, tok, ea, eb):
@@ -445,59 +437,42 @@ def rank_program(g, core, T, topo):
                 dma(eb if i % 2 else ea, [tok], T.osc[4 * i:4 * i + 4, H * h:H * h + H], T["sx%d" % rn][32 * i:32 * i + 4, H * h:H * h + H], "outs")
 
             def store_y():
-                o = op("v", [t], "cp", T.yb[:, H * h:H * h + H], banks[k][:, 0:H])
-                readers[k].append(o)
+                o = read(k, op("v", [t], "cp", T.yb[:, H * h:H * h + H], banks[k][:, 0:H]))
                 dma(ea, [o], T.y[:, H * h:H * h + H], T.yb[:, H * h:H * h + H], "outs")
             return store_y
 
-        land, la = T["ll%d" % r], ("la%d" % r, far_engines)
-        if r:
-            pP = unpack(T["qp%d" % r], T["sp%d" % r], [qa[1]], H, H)
-        ps = make(0, [ls, tF], us[:, 0:10], T["f%d" % r])
-        if r:
-            tP = unpack_copy(T["fp%d" % r], pP, H, H)
+        land, la = T.ll[:, 16 * r:16 * r + 10], ("la%d" % r, far_engines)
+        ps, more = make(0, [ls, tF], us[0], T["f%d" % r], lambda: None)
         if rn < R:
-            lists = [dup(T["us%d" % rn], us[:, 0:10], [ls], 0), None]
-            t0 = table_twice(rn, 0, "s", table_lookup(rn, 0, "s", us[:, 0:10], ls))
-            keep_old(rn, 0, 10, us[:, 0:10])
+            lk = [odd_list(rn, 0, T.lt[:, 0:10], ls), None]
         else:
             vv = op("v", [ld_v], "qz", T.vq[:], T.vp[:], T.vb[:])
-            oa1 = op("s", [ls, g_iw], "act", T.orow[:, 0:H], T.iw[:].indirect(us[:, 0:10]), AF.Copy)
-        if r == 0:
-            unpack_copy(T.fp0, unpack(T.qp0, T.sp0, [qa[0]], 0, H), 0, H)
-        o = [renew(0, b, ps, "v") for b in range(4)]
-        if r == 0:
-            tP = unpack_copy(T.fp0, unpack(T.qp0, T.sp0, [qa[1]], H, H), H, H)
-        qx = [requant(0, o), None]
+        p0 = ps
+        ps, x0 = make(1, [la, tP], land, fp, lambda: renew(0, p0, "svsv"))
+        qx = [requant(0, x0), None]
         if rn < R:
-            s0 = scores(rn, 0, qx[0])
             send_codes(rn, 0, qx[0])
-            tab = [turn_tables(rn, 0, t0), None]
-
-            def behind():
-                bt_[0] = bits(rn, 0, s0)
+            s0 = scores(rn, 0, qx[0])
+            lk[1] = odd_list(rn, 1, land, la)
         else:
             behind = outputs(0, qx[0], "y", "y")
-        ps = make(1, [la, tP], land[:], T["fp%d" % r], behind)
-        if rn < R:
-            t1 = table_lookup(rn, 1, "v", land[:], la)
-            er[0] = edge_rows(rn, 0, bt_[0])
-            t1 = table_twice(rn, 1, "v", t1)
-            lists[1] = dup(T["us%d" % rn], land[:], [la], 1)
-            tab[1] = turn_tables(rn, 1, t1)
-            o = [renew(1, b, ps, "s") for b in range(4)]
-        else:
-            oa2 = op("v", [la, g_iw], "cp", T.orow[:, H:C], T.iw[:].indirect(land[:]))
+            oa1 = copy("s", [ls, g_iw], T.orow[:, 0:H], T.iw[:].indirect(us[0]))
+            oa2 = copy("v", [la, g_iw], T.orow[:, H:C], T.iw[:].indirect(land))
             dma("y", [oa1, oa2], T.oa[:], T.orow[0:128:16, :], "outs")
-            o = [renew(1, b, ps, "v" if b % 2 else "s") for b in range(4)]
-        qx[1] = requant(1, o)
+        x1 = renew(1, ps, "svsv")
         if rn < R:
+            sg[0] = signs(0, s0)
+            er[0] = edges(0, sg[0])
+            qx[1] = requant(1, x1)
             send_codes(rn, 1, qx[1])
             s1 = scores(rn, 1, qx[1])
-            e0 = turn_edges(rn, 0, er[0])
-            old = keep_old(rn, 10, 10, land[:])
-            bt_[1] = bits(rn, 1, s1)
+            ch[0] = choose(0, [sg[0]])
+            e0 = turn_edges(0, er[0])
+            sg[1] = signs(1, s1)
+            first_marks(0, e0)
         else:
+            behind()
+            qx[1] = requant(1, x1)
             outputs(1, qx[1], "y", "s")()
     need("g", [("loc", loc[0]), ("outs", dma_n["outs"])])
     for e in ("v", "s", "t", "g"):

from concourse.bass import DstId, RemoteDMATransfer
from concourse.mybir import dt, AluOpType as A, ActivationFunctionType as AF

N, C, H, R = 8, 320, 160, 3
BF, F32, I32, U16, U8, MX = "bfloat16", "float32", "int32", "uint16", "uint8", "float8_e4m3fn_x4"
INV = 0.015625
LY, LD, LA, LN, LK = 0, 6, 11, 12, 28
LH, LE = 14, 17
NB = (5, 10)
ORDER = ["TP", "MU tp MP", "MK M0 mu", "DF MP MP MP mk", "SC mp mp df", "NE PB sc", "SC mp mp ne", "NE DO DO DO sc",
         "SC pb DO DO ne", "NE do do do sc", "PK do do ne", "CV pk", "t1", "t2", "cv"]


def _scratch():
    s = {}

    def sb(name, n, t):
        s[name] = ("sbuf", [128] + (n if isinstance(n, list) else [n]), t)
    for k in range(8):
        s["pk%d" % k] = ("psum", [128, 512], F32)
    sb("ub", 512, BF); sb("uq", 128, MX); sb("up", 128, U8); sb("uq2", 128, MX); sb("up2", 128, U8)
    sb("vb", 512, BF); sb("vq", 128, MX); sb("vp", 128, U8)
    sb("wq", 512, MX); sb("wp", 512, U8)
    sb("c64", 288, BF); sb("eb", 516, BF); sb("ec", 512, MX); sb("es", 512, U8)
    sb("ct", 96, F32); sb("cf", 96, F32); sb("ci", 8, I32); sb("rl", 22, U16); sb("uls", 8, U16); sb("th", 80, BF)
    sb("ali", 20, I32); sb("nt", 160, I32); sb("ni", 160, I32); sb("cb", [2, 96], BF); sb("nf", [2, 96], F32)
    sb("rc", [12, 4, 4], BF); sb("rt", [12, 4, 4], F32); sb("kw", [6, 4, 4], F32); sb("kc", [6, 4, 4], F32)
    sb("ac", [12, 4], F32); sb("w1", [6, 4, 4], F32); sb("w2", [6, 4, 4], F32); sb("kp", [6, 4, 2], F32)
    sb("ln", [12, 4, 16], F32); sb("tw", 768, F32); sb("bw", 640, BF); sb("cw", 640, F32)
    for h, n in enumerate(NB):
        sb("gg%d" % h, 32 * n, F32); sb("gt%d" % h, [n, 32], F32); sb("er%d" % h, [n, 32], BF); sb("et%d" % h, [n, 32], BF)
        sb("tm%d" % h, [n, 4], I32); sb("y3%d" % h, [n, 9], I32); sb("dq%d" % h, 8 * n, BF); sb("me%d" % h, 8 * n, BF)
        sb("mp%d" % h, 20 * n, BF); sb("se%d" % h, 8 * n + 8, BF); sb("ao%d" % h, 48 + 120 * h, F32)
        sb("a4%d" % h, 112 + 112 * h, F32); sb("pb%d" % h, 20 * n, F32); sb("do%d" % h, 8 * n, F32)
    sb("fl", 224, BF); sb("fm", 224, BF); sb("fw", [21, 32], BF); sb("ft", 672, BF)
    sb("ae", 40, F32); sb("pm", 80, F32); sb("pa", 512, F32); sb("xt", [2, 32], F32); sb("lt", 64, F32)
    sb("iw", 320, F32); sb("orow", 320, F32); sb("yb", 320, F32)
    for r in range(R + 1):
        sb("x%d" % r, 1280, BF); sb("qx%d" % r, 320, MX); sb("sx%d" % r, 320, U8)
    for r in range(R):
        sb("f%d" % r, 1280, BF); sb("fp%d" % r, 1280, BF); sb("z%d" % r, 1280, BF)
        sb("qz%d" % r, 320, MX); sb("sz%d" % r, 320, U8)
        sb("qp%d" % r, 320, MX); sb("sp%d" % r, 320, U8)
        sb("rq%d" % r, 320, MX); sb("rs%d" % r, 320, U8)
    sb("ll", 16 * R, U16); sb("lr", 16 * R, U16); sb("um", 16 * R, U16); sb("ul", 40, U16)
    return s


SCRATCH = _scratch()
SEMAPHORES = (["vq", "sq", "tq", "gq", "loc"]
              + ["ld_x0", "ld_x1", "ld_u", "ld_v", "ld_w", "ld_al", "ld_nx", "outs"]
              + ["%s%d%d" % (k, r, h) for k in ("rc", "rp", "qa") for r in range(R) for h in range(2)]
              + ["%s%d" % (k, r) for k in ("rl", "la") for r in range(R)])


def _relays(core, nxt, topo):
    w = [c for c in topo.cores_of(core) if c != core and topo.may_write(c, nxt)]
    near = [c for c in w if topo.die(c) == topo.die(core)]
    far = [c for c in w if topo.die(c) != topo.die(core)]
    return near[0], near[1], far[0], far[1]


def _mask(es):
    m = 0
    for e in es:
        m |= 1 << e
    return m


def _hand_on(g, core, T, topo):
    mine = [c for c in topo.cores_of(core) if T.rank_of(c) is not None]
    if not mine:
        return
    nxt = T.cores[(T.rank_of(mine[0]) + 1) % N]
    rel = _relays(mine[0], nxt, topo)
    if core not in rel:
        return
    k = rel.index(core)
    rid, pid = topo.addr(nxt, core)
    m = topo.mask(core, nxt)
    ne = len(topo.engines(core, nxt))
    near = len(topo.engines(mine[0], core))
    n = 0
    for r in range(R):
        for h in range(2):
            if k % 3 == 0 and k != 3 * h:
                continue
            if k % 3 == 0:
                g.wait_ge(T.sem["rp%d%d" % (r, h)], near)
                g.remote_dma(T["sp%d" % r][:, H * h:H * h + H], T["rs%d" % r][:, H * h:H * h + H],
                             T.sem["qa%d%d" % (r, h)], T.sem.loc, pid, rid, m)
            else:
                a = H * h + 80 * (k - 1)
                g.wait_ge(T.sem["rc%d%d" % (r, h)], near // 2)
                g.remote_dma(T["qp%d" % r][:, a:a + 80].bitcast(dt.uint8), T["rq%d" % r][:, a:a + 80].bitcast(dt.uint8),
                             T.sem["qa%d%d" % (r, h)], T.sem.loc, pid, rid, m)
            n += ne
        if k == 0:
            g.wait_ge(T.sem["rl%d" % r], near)
            g.remote_dma(T.ll[:, 16 * r:16 * r + 10], T.lr[:, 16 * r:16 * r + 10], T.sem["la%d" % r], T.sem.loc, pid, rid, m)
            n += ne
    g.wait_ge(T.sem.loc, n)


def rank_program(g, core, T, topo):
    rank = T.rank_of(core)
    if rank is None:
        return _hand_on(g, core, T, topo)
    nxt = T.cores[(rank + 1) % N]
    rel = _relays(core, nxt, topo)
    before = T.cores[(rank - 1) % N]
    far_engines = len(topo.engines(_relays(before, core, topo)[0], core))
    Q = {"v": g.vector, "s": g.scalar, "t": g.tensor, "g": g, "y": g.sync}
    cnt = {"v": 0, "s": 0, "t": 0, "g": 0}
    seen = {k: {} for k in Q}
    dma_n = {}
    loc = [0]

    def need(e, toks):
        for t in toks:
            if isinstance(t, list):
                need(e, t)
            elif seen[e].get(t[0], 0) < t[1]:
                Q[e].wait_ge(T.sem[t[0]], t[1])
                seen[e][t[0]] = t[1]

    def op(e, toks, name, *a, **k):
        need(e, toks)
        q = Q[e]
        f = {"cp": lambda: q.tensor_copy(*a), "tt": lambda: q.tensor_tensor(*a), "ts": lambda: q.tensor_scalar(*a),
             "ms": lambda: q.memset(*a), "tp": lambda: q.transpose(*a), "qz": lambda: q.quantize_mx(*a),
             "scan": lambda: q.tensor_tensor_scan(*a, 0.0, A.mult, A.add), "act": lambda: q.activation(*a, **k),
             "mm": lambda: q.matmul_mx(*a), "iota": lambda: q.iota(*a, **k), "sel": lambda: q.affine_select(*a)}[name]
        f().then_inc(T.sem[e + "q"], 1)
        cnt[e] += 1
        return (e + "q", cnt[e])

    def copy(e, toks, out, in_, scale=None):
        if e == "s":
            return op("s", toks, "act", out, in_, AF.Copy, **({} if scale is None else {"scale": scale}))
        return op("v", toks, "cp", out, in_) if scale is None else op("v", toks, "ts", out, in_, scale, None, A.mult)

    def dma(e, toks, out, in_, sem):
        need(e, toks)
        Q[e].dma_start(out, in_).then_inc(T.sem[sem], 16)
        dma_n[sem] = dma_n.get(sem, 0) + 16
        return (sem, dma_n[sem])

    banks = [T["pk%d" % k] for k in range(8)]
    readers = [[] for k in range(8)]
    turn = [0]
    held = set()

    def bank():
        while turn[0] % 8 in held:
            turn[0] += 1
        k = turn[0] % 8
        turn[0] += 1
        held.add(k)
        return k

    def read(k, o):
        readers[k].append(o)
        held.discard(k)
        return o

    def mm(toks, k, n, lc, ls, b, rc, rs, a, start=True, stop=True):
        w = [toks, readers[k]] if start else [toks]
        if start:
            readers[k] = []
        return op("t", w, "mm", banks[k][:, 0:n], lc[:, 128 * b:128 * b + 128], ls[:, 128 * b:128 * b + 128],
                  rc[:, a:a + n], rs[:, a:a + n], start, stop)

    ld_nx = dma("s", [], T.nt[:], T.nx[:], "ld_nx")
    ld_u = dma("y", [], T.ub[:], T.u[:], "ld_u")
    ld_x = [dma("y", [], T.x0[:, 640 * h:640 * h + 640], T.x[:, 640 * h:640 * h + 640], "ld_x%d" % h) for h in range(2)]
    ld_al = dma("y", [], T.ali[:], T.al[:], "ld_al")

    fl = {"allow_small_or_imprecise_dtypes": True}
    ct, ci, ln, rc, rt = T.ct, T.ci, T.ln, T.rc, T.rt
    v_c64 = op("v", [], "ms", T.c64[:], 64.0)
    v_eb = op("v", [], "ms", T.eb[:], 0.0)
    g_ul = op("g", [], "iota", ci[:], [[16, 8]], 0, 0)
    g_ac = g_eb = op("g", [v_eb], "sel", T.eb[:, 3:515:4], T.c64[:, 0:128], [[-1, 128]], A.is_equal, 0.0, 0, 1)
    for q in range(4):
        g_ac = op("g", [g_ac], "iota", T.ac[32 * q:32 * q + 32, 0:6, :], [[128, 3], [0, 2], [1, 4]], 0, 4, **fl)
    g_th = op("g", [g_ac], "iota", T.th[:], [[0, 10], [1, 8]], 0, 0, **fl)

    def fill(out, n, c, toks=()):
        return op("s", [v_c64, list(toks)], "act", out, T.c64[:, 0:n], AF.Copy, scale=c / 64.0)

    def const_tile(b):
        return op("v", [g_eb], "qz", T.ec[:, 128 * b:128 * b + 128], T.es[:, 128 * b:128 * b + 128], T.eb[:, 3 - b:515 - b])
    ES, EB, UL = T.cf[0:32, 0:1], T.cf[0:32, 32:33], T.cf[:, 64:65]
    op("v", [], "ms", ct[:, 0:64], 0.0)
    o = op("v", [], "ms", ct[:, 64:96], 16.0)
    for e in range(4):
        op("v", [], "ms", T.kw[:, :, :, e], 16.0 ** (3 - e))
    op("v", [], "ms", T.y30[:], 0)
    op("v", [], "ms", T.y31[:], 0)
    fill(T.cb[:, :, 80:96], 32, 0.0)
    s1 = fill(T.nf[:, :, 80:96], 32, 0.0)
    for a, b, c in [(64, 67, 1.0), (67, 70, 17.0), (80, 83, 1.0), (83, 86, 17.0), (16, 19, 2.0), (19, 22, -1.0), (46, 48, 9.0),
                    (48, 49, -1.0), (49, 50, -2.0), (50, 51, -3.0), (54, 57, 9.0)]:
        s0 = fill(ct[:, a:b], b - a, c, [o])
    fill(T.ac[:, 6:12, :], 24, 0.0)
    fill(T.fl[:, 210:224], 14, 160.0)
    fill(T.fm[:], 224, 160.0)
    s2 = fill(ln[:, :, :, 0:6], 288, 0.0)
    vE = [const_tile(b) for b in range(4)]
    op("g", [s2], "iota", T.fl[:, 0:200], [[8, 10], [0, 4], [1, 5]], 0, 0, **fl)
    op("g", [], "iota", T.fl[:, 200:210], [[8, 10]], LA - LD, 0, **fl)
    op("g", [], "iota", T.fm[:, 4:200:5], [[8, 10], [1, 4]], 80 + LN - 8, 0, **fl)
    g_fl = op("g", [], "iota", T.fm[:, 200:210], [[8, 10]], 80 + LA - 8, 0, **fl)

    nt, ni, nf, tw = T.nt, T.ni, T.nf, T.tw
    c1 = op("v", [ld_nx], "ts", T.cb[:, :, 0:80], nt[:], 1.0 / 512, 127.8125, A.mult, A.add)
    n1 = op("v", [], "ts", ni[:], nt[:], 511, None, A.bitwise_and)
    cols = op("v", [s0, g_ul], "tp", T.cf[:], ct[:])
    c3 = op("v", [c1, s1], "tp", rc[:], T.cb[:])
    n2 = op("v", [n1], "cp", nf[:, :, 0:80], ni[:])
    y1 = op("s", [c3], "act", T.w1[:], rc[:, 0:12:2], AF.Identity, scale=4.0, bias=-392.0)
    o = op("v", [], "cp", T.uls[:], ci[:, 0:8])
    qu = op("v", [ld_u], "qz", T.uq[:], T.up[:], T.ub[:])
    c4 = op("v", [c3], "tt", T.kc[:], rc[:, 1:12:2], T.kw[:], A.mult)
    n3 = op("v", [n2], "tp", rt[:], nf[:])
    v_ul = op("v", [o, cols], "cp", T.uls[:, 1:2], UL)
    y2 = op("v", [y1], "tt", T.w2[:], T.w1[:], rc[:, 0:12:2], A.max)
    y3 = op("s", [y2], "act", T.w1[:], T.w2[:], AF.Square, bias=-128.0)
    v_u = [op("s", [qu, v_ul], "act", T.up2[:], T.up[:].indirect(T.uls[:]), AF.Copy)]
    y4 = op("s", [y3, s2], "act", ln[:, 0:12:2, :, LY:LY + 4], T.w1[:], AF.Square, scale=0.25)
    c5 = op("v", [c4], "tt", T.kc[:, 3:6], T.kc[:, 3:6], T.kc[:, 0:3], A.subtract)
    n4 = op("v", [n3], "tt", rt[:, 6:12], rt[:, 6:12], rt[:, 0:6], A.subtract)
    v_u.append(op("v", [v_ul], "cp", T.uq2[:].bitcast(dt.uint32), T.uq[:].bitcast(dt.uint32).indirect(T.uls[:])))
    qx = [op("v", [ld_x[0]], "qz", T.qx0[:, 0:H], T.sx0[:, 0:H], T.x0[:, 0:640])]
    k1 = op("v", [c5], "tt", T.kp[:], T.kc[:, :, :, 0:4:2], T.kc[:, :, :, 1:4:2], A.add)
    op("s", [n4], "act", ln[:, :, :, LD + 4], rt[:, :, :, 3], AF.Copy)
    op("s", [], "act", ln[:, 0:12:2, :, LN:LN + 4], rt[:, 0:12:2], AF.Copy)
    k3 = op("s", [g_ac], "act", ln[:, :, :, LA], T.ac[:], AF.Copy)
    op("v", [n4, s2], "tt", ln[:, :, :, LD + 1:LD + 4], rt[:, :, :, 0:3], rt[:, :, :, 1:4], A.subtract)
    qx.append(op("v", [ld_x[1]], "qz", T.qx0[:, H:C], T.sx0[:, H:C], T.x0[:, 640:1280]))
    op("v", [g_ac], "tt", ln[:, :, :, LD], T.ac[:], rt[:, :, :, 0], A.subtract)
    for e in range(4):
        op("v", [k1], "tt", ln[:, 1:12:2, :, LK - 16 + e], T.kp[:, :, :, 0], T.kp[:, :, :, 1], A.add)
    y5 = op("v", [y4], "tt", ln[:, 6:12:2, :, LY:LY + 4], ln[:, 6:12:2, :, LY:LY + 4], ln[:, 0:6:2, :, LY:LY + 4], A.subtract)
    for a in range(0, 640, 256):
        v_bw = fill(T.bw[:, a:min(a + 256, 640):2], min(128, (640 - a) // 2), 0.0)
    for h, n in enumerate(NB):
        fill(T["se%d" % h][:, 8 * n:8 * n + 8], 8, 0.0)
        fill(T["ao%d" % h][:, 40 + 120 * h:48 + 120 * h], 8, 0.0)
        fill(T["do%d" % h][:], 8 * n, 0.0)
        fill(T["mp%d" % h][:, 0:20 * n:5], 4 * n, 0.0)
    fill(T.pa[:, 4:512:8], 64, 0.0)
    s3 = fill(T.th[:, 0:80:8], 10, -9.0, [g_th])

    def send_codes(r, h, tok):
        need("g", [tok])
        es = topo.engines(core, rel[1])
        n = len(es) // 2
        tr = []
        for k in (1, 2):
            a = H * h + 80 * (k - 1)
            rid, pid = topo.addr(rel[k], core)
            tr.append(RemoteDMATransfer(dst_ids=[DstId(rid=rid, pnc=pid)], dma_engine_mask=_mask(es[n * k - n:n * k]),
                                        remote_sem=T.sem["rc%d%d" % (r, h)], src=T["qx%d" % r][:, a:a + 80].bitcast(dt.uint8),
                                        dst=T["rq%d" % r][:, a:a + 80].bitcast(dt.uint8)))
        g.remote_dma_fused(tr, local_sem=T.sem.loc)
        rid, pid = topo.addr(rel[3 * h], core)
        g.remote_dma(T["rs%d" % r][:, H * h:H * h + H], T["sx%d" % r][:, H * h:H * h + H], T.sem["rp%d%d" % (r, h)],
                     T.sem.loc, pid, rid, topo.mask(core, rel[3 * h]))
        loc[0] += 4 * n

    def scores(r, h, tok):
        k = bank()
        return k, mm([tok, v_u], k, H, T.uq2, T.up2, 0, T["qx%d" % r], T["sx%d" % r], H * h)

    def signs(h, kt):
        k, t = kt
        return read(k, op("v", [t], "ts", T.bw[:, C * h + 1:C * h + C:2], banks[k][:, 0:H], 0.0, None, A.is_gt))

    def choose(h, toks):
        return op("v", toks, "scan", T.cw[:, C * h:C * h + C], T.bw[:, C * h:C * h + C], tw[:, C * h:C * h + C])

    def edges(h, tok):
        er, src = T["er%d" % h], T.bw[0:32, C * h + 1:C * h + C:2]
        for out in ([er[0:32, :, 0:16], er[0:32, :, 16:32]] if h else [er[0:32]]):
            o = op("s", [tok, cols], "act", out, src, AF.Identity, scale=ES, bias=EB)
        return o

    def turn_edges(h, tok):
        return op("v", [tok], "tp", T["et%d" % h][0:32], T["er%d" % h][0:32])

    def first_marks(h, tok):
        et = T["et%d" % h]
        return op("v", [tok], "tt", T["me%d" % h][0:32], et[0:32, :, LH:LH + 8], et[0:32, :, LE:LE + 8], A.is_lt)

    def odd_list(r, h, src, tok):
        for out in ([T.ul[:, 10:30:2], T.ul[:, 11:30:2]] if h else [T.ul[:, 0:10]]):
            o = op("v", [tok], "ts", out, src, 2.0, 1.0, A.mult, A.add)
        return o

    def unpack(qc, qs, toks, bs=range(4)):
        ks = {b: bank() for b in bs}
        return {b: (ks[b], mm([toks, vE[b]], ks[b], C, T.ec, T.es, b, qc, qs, 0)) for b in bs}

    def unpack_copy(d, ps, es):
        return [read(ps[b][0], copy(e, [ps[b][1]], d[:, C * b:C * b + C], banks[ps[b][0]][:, 0:C], INV)) for b, e in zip(ps, es)]

    sc = [scores(0, 0, qx[0]), scores(0, 1, qx[1])]
    send_codes(0, 0, qx[0])
    send_codes(0, 1, qx[1])
    g_iw = op("g", [], "iota", T.iw[:], [[1, 320]], 0, 0, **fl)
    copy("s", [g_fl], T.fw[:, 0:14, 0:16], T.fm[:])
    copy("s", [], T.fw[:, 0:14, 16:32], T.fl[:])
    copy("s", [], T.fw[:, 14:21, 0:16], T.fl[:, 0:112])
    j = copy("s", [], T.fw[:, 14:21, 16:32], T.fl[:, 0:112])
    lk = [odd_list(0, h, T.ali[:, 10 * h:10 * h + 10], ld_al) for h in range(2)]
    for m in range(8):
        k5 = op("v", [y5, k3], "tp", tw[:, (m ^ 1):768:8], ln[:, 6 * (m % 2):6 * (m % 2) + 6, m // 2, :])
    sg = [signs(0, sc[0]), signs(1, sc[1])]
    er = [edges(0, sg[0]), None]
    ch = [choose(0, [k5, sg[0], v_bw]), None]

    for r in range(R):
        rn = r + 1
        us, ul = [T.ul[:, 30:40], T.um[:, 16 * r:16 * r + 10]], T.ul
        qa = [("qa%d%d" % (r, h), 3 * far_engines) for h in range(2)]
        qp, sp, fp = T["qp%d" % r], T["sp%d" % r], T["fp%d" % r]
        er[1] = edges(1, sg[1])
        ch[1] = choose(1, [sg[1]])
        if r == 0:
            j = op("v", [j], "tp", T.ft[:], T.fw[:])
            e0 = turn_edges(0, er[0])
        gm = [copy("v", [ch, lk], T.gg1[:, 0:H], T.cw[:].indirect(ul[:, 10:20])),
              copy("s", [ch, lk], T.gg1[:, H:C], T.cw[:].indirect(ul[:, 20:30]))]
        gs = copy("s", [], T.gg0[:], T.cw[:].indirect(ul[:, 0:10]))
        e1 = turn_edges(1, er[1])
        if r == 0:
            j = op("v", [j], "cp", T.rl[:, 0:21], T.ft[:, 0:672:32])
            first_marks(0, e0)
            dma("y", [ld_x], T.wq[:].bitcast(dt.uint8), T.wc[:], "ld_w")
            ld_w = dma("y", [], T.wp[:], T.ws[:], "ld_w")
            ld_v = dma("y", [ld_w], T.vb[:], T.v[:], "ld_v")
        tok = [{"tp": gs}, {"tp": gm}]
        count = [{}, {}]

        def step(h, k):
            n, w, i = NB[h], tok[h], count[h].get(k, 0)
            count[h][k] = i + 1
            gt, me, se, pb, do = [T["%s%d" % (s, h)] for s in ("gt", "me", "se", "pb", "do")]
            y3, a4, ao, mp = [T["%s%d" % (s, h)] for s in ("y3", "a4", "ao", "mp")]
            a, b = 32 * i, 32 * i + 32
            if k == "tp":
                o = w["go"] = op("v", [w["tp"]], "tp", gt[:], T["gg%d" % h][:])
                p = copy("s", [o], ao[:, 0:8 * n], gt[:, :, 16 + LD:24 + LD])
                if h:
                    p = copy("s", [], ao[:, 80:160], gt[:, :, 8:16])
                else:
                    copy("s", [], T.ae[:], gt[:, :, LD:LD + 8])
                w["a4"] = copy("s", [p, j], a4[:], ao[:].indirect(T.rl[:, 0:14] if h else T.rl[:, 14:21]))
            if k == "mu":
                w["go"] = op("v", [w["go"]], "tt", T["tm%d" % h][:], gt[:, :, LY:LY + 4], gt[:, :, LK:LK + 4], A.mult)
            if k == "mk":
                w["go"] = op("v", [w["go"]], "ts", y3[:, :, 1:5], T["tm%d" % h][:], 8, 7, A.arith_shift_right, A.bitwise_and)
            if k == "m0":
                first_marks(h, e1)
            if k == "df":
                w["go"] = op("v", [w["go"]], "tt", T["dq%d" % h][:], y3[:, :, 0:8], y3[:, :, 1:9], A.subtract)
            if k == "sc":
                w["go"] = op("v", [w["go"]], "scan", se[b:b + 32, 0:8 * n], me[a:b], T["dq%d" % h][a:b])
            if k == "ne":
                w["go"] = op("v", [w["go"], s3], "tt", me[b:b + 32], se[b:b + 32, 3:8 * n + 3], T.th[b:b + 32, 0:8 * n], A.is_lt)
            if k == "mp":
                w["mp"] = op("v", [s3], "ts", mp[:, 1 + i:20 * n:5], gt[:, :, LY:LY + 4], 16.0 ** (i - 1), None, A.is_lt)
            if k == "pb":
                w["pb"] = op("v", [w["mp"], w["a4"]], "scan", pb[:], mp[:], a4[:, 0:20 * n])
            if k == "do" and i < 4:
                old = pb[:, 5 * i - 1:20 * n:20] if i else a4[:, 200:210] if h else gt[:, :, 16 + LA]
                w["do"] = op("v", [w["pb"]], "tt", do[:, i:8 * n:8], old, pb[:, 5 * i + 4:20 * n:20], A.subtract)
            if k == "do" and i == 4:
                w["do"] = op("v", [w["pb"]], "cp", do[:, 4:8 * n:8], pb[:, 19:20 * n:20])
            if k == "pk" and h:
                w["go"] = op("v", [w["go"], w["do"]], "scan", T.pm[:], me[:], do[:])
            if k == "pk" and not h:
                op("v", [w["go"]], "scan", T.pa[:, 0:40], me[:], T.ae[:])
                w["go"] = op("v", [w["do"]], "scan", T.pa[:, 256:296], me[:], do[:])
            if k == "t1":
                w["go"] = op("v", [w["go"]], "tp", T.xt[:], T.pa[:, 4:512:8])
            if k == "t2":
                op("v", [w["go"]], "tp", T.lt[:, 0:64:2], T.xt[:, :, 0:16])
                w["go"] = op("v", [], "tp", T.lt[:, 1:64:2], T.xt[:, :, 16:32])
            if k == "cv":
                w["go"] = op("v", [w["go"]], "cp", us[h], T.pm[:, 4:80:8] if h else T.lt[:, 0:10])

        for n, line in enumerate(ORDER):
            for k in line.split():
                step(int(k.isupper()), k.lower())
                if k == "tp":
                    tF = unpack_copy(T["f%d" % r], unpack(T["qx%d" % r], T["sx%d" % r], [qx]), "ssss")
                    tP = unpack_copy(fp, unpack(qp, sp, [qa]), "ssss")
                if k == "CV":
                    need("g", [tok[1]["go"]])
                    rid, pid = topo.addr(rel[0], core)
                    g.remote_dma(T.lr[:, 16 * r:16 * r + 10], us[1], T.sem["rl%d" % r], T.sem.loc, pid, rid, topo.mask(core, rel[0]))
                    loc[0] += len(topo.engines(core, rel[0]))
        ls = tok[0]["go"]

        def make(h, toks, off, F, between):
            z, q, s, o = T["z%d" % r], T["qz%d" % r], T["sz%d" % r], []
            for b in range(4):
                o.append(copy("vsvs"[b], [toks], z[:, 640 * h + b:640 * h + 640:4], F[:, 320 * b:320 * b + 320].indirect(off)))
            more = between()
            zq = op("v", [o], "qz", q[:, H * h:H * h + H], s[:, H * h:H * h + H], z[:, 640 * h:640 * h + 640])
            ps = []
            for b in range(4):
                k = bank()
                mm([zq, ld_w], k, H, T.wq, T.wp, b, q, s, H * h, True, False)
                ps.append((k, mm([zq], k, H, T.ec, T.es, b, q, s, H * h, False, True)))
            return ps, more

        def renew(h, ps, es):
            o = []
            for b in range(4):
                k, t = ps[b]
                o.append(read(k, copy(es[b], [t], T["x%d" % rn][:, 640 * h + b:640 * h + 640:4], banks[k][:, 0:H], INV)))
            return o

        def requant(h, o):
            return op("v", [o], "qz", T["qx%d" % rn][:, H * h:H * h + H], T["sx%d" % rn][:, H * h:H * h + H],
                      T["x%d" % rn][:, 640 * h:640 * h + 640])

        def outputs(h, tok, ea, eb):
            k = bank()
            t = mm([tok, vv], k, H, T.vq, T.vp, 0, T["qx%d" % rn], T["sx%d" % rn], H * h)
            dma(ea, [tok], T.oc[:, 640 * h:640 * h + 640], T["qx%d" % rn][:, H * h:H * h + H].bitcast(dt.uint8), "outs")
            for i in range(4):
                dma(eb if i % 2 else ea, [tok], T.osc[4 * i:4 * i + 4, H * h:H * h + H], T["sx%d" % rn][32 * i:32 * i + 4, H * h:H * h + H], "outs")

            def store_y():
                o = read(k, op("v", [t], "cp", T.yb[:, H * h:H * h + H], banks[k][:, 0:H]))
                dma(ea, [o], T.y[:, H * h:H * h + H], T.yb[:, H * h:H * h + H], "outs")
            return store_y

        land, la = T.ll[:, 16 * r:16 * r + 10], ("la%d" % r, far_engines)
        ps, more = make(0, [ls, tF], us[0], T["f%d" % r], lambda: None)
        if rn < R:
            lk = [odd_list(rn, 0, T.lt[:, 0:10], ls), None]
        else:
            vv = op("v", [ld_v], "qz", T.vq[:], T.vp[:], T.vb[:])
        p0 = ps
        ps, x0 = make(1, [la, tP], land, fp, lambda: renew(0, p0, "svsv"))
        qx = [requant(0, x0), None]
        if rn < R:
            send_codes(rn, 0, qx[0])
            s0 = scores(rn, 0, qx[0])
            lk[1] = odd_list(rn, 1, land, la)
        else:
            behind = outputs(0, qx[0], "y", "y")
            oa1 = copy("s", [ls, g_iw], T.orow[:, 0:H], T.iw[:].indirect(us[0]))
            oa2 = copy("v", [la, g_iw], T.orow[:, H:C], T.iw[:].indirect(land))
            dma("y", [oa1, oa2], T.oa[:], T.orow[0:128:16, :], "outs")
        x1 = renew(1, ps, "svsv")
        if rn < R:
            sg[0] = signs(0, s0)
            er[0] = edges(0, sg[0])
            qx[1] = requant(1, x1)
            send_codes(rn, 1, qx[1])
            s1 = scores(rn, 1, qx[1])
            ch[0] = choose(0, [sg[0]])
            e0 = turn_edges(0, er[0])
            sg[1] = signs(1, s1)
            first_marks(0, e0)
        else:
            behind()
            qx[1] = requant(1, x1)
            outputs(1, qx[1], "y", "s")()
    need("g", [("loc", loc[0]), ("outs", dma_n["outs"])])
    for e in ("v", "s", "t", "g"):
        need("g", [(e + "q", cnt[e])])
